import numpy as np
import ml_dtypes


def mxq(x, axis, fmt="e4m3"):
    dtype, down = {"e4m3": (ml_dtypes.float8_e4m3fn, 7), "e5m2": (ml_dtypes.float8_e5m2, 14)}[fmt]
    v = np.moveaxis(np.asarray(x, np.float32).astype(ml_dtypes.bfloat16).astype(np.float64), axis, -1)
    blocks = v.reshape(v.shape[:-1] + (-1, 32))
    amax = np.abs(blocks).max(-1, keepdims=True)
    byte = np.maximum(np.where(amax > 0, np.frexp(amax)[1] - 1 + 127, 0) - down, 1)
    scale = np.exp2(byte - 127.0)
    codes = (blocks / scale).astype(np.float32).astype(dtype).astype(np.float64)
    return np.moveaxis((codes * scale).reshape(v.shape), -1, axis)


WIDE = False


def mx_kscale(k):
    if not WIDE:
        return np.ones(k)
    levels = np.array([10, -10, 5, -5, 0])
    if k % 512:
        return np.exp2(np.random.permutation(np.resize(levels, k // 32))).repeat(32)
    a = np.empty((k // 512, 16))
    for p in range(k // 512):
        a[p, :8] = np.random.permutation(np.resize(levels, 8))
        for g in range(8):
            far = levels[np.abs(levels - a[p, g]) >= 10]
            a[p, g + 8] = far[np.random.randint(len(far))]
    return np.exp2(a.ravel()).repeat(32)


BF16 = ml_dtypes.bfloat16


def bf(x):
    return np.asarray(x, np.float32).astype(BF16)


def f64(x):
    return np.asarray(x).astype(np.float64)


E2M1 = np.array([0.0, 0.5, 1.0, 1.5, 2.0, 3.0, 4.0, 6.0, -0.0, -0.5, -1.0, -1.5, -2.0, -3.0, -4.0, -6.0])


def pack_weight(w, fmt):
    k, n = w.shape
    w = f64(bf(w)).reshape(k // 32, 32, n)
    amax = np.abs(w).max(1)
    if fmt == "e4m3":
        byte = np.frexp(amax)[1] - 1 + 127 - 7
    else:
        mant, ex = np.frexp(amax / 6.0)
        byte = np.where(mant > 0.5, ex, ex - 1) + 127
    byte = np.clip(np.where(amax > 0, byte, 1), 1, 254)
    scaled = (w * np.exp2(127.0 - byte)[:, None, :]).reshape(k, n).astype(np.float32)
    by_word = np.ascontiguousarray(scaled.reshape(k // 512, 128, 4, n).transpose(0, 1, 3, 2))
    if fmt == "e4m3":
        words = by_word.astype(ml_dtypes.float8_e4m3fn).view(np.uint8)
    else:
        c = by_word.astype(ml_dtypes.float4_e2m1fn).view(np.uint8) & 0xF
        words = c[..., 0::2] | (c[..., 1::2] << 4)
    return np.ascontiguousarray(words), np.ascontiguousarray(byte.astype(np.uint8).reshape(k // 512, 16, n))


def unpack_weight(words, scales, fmt):
    g, p, n, _ = words.shape
    if fmt == "e4m3":
        vals = np.ascontiguousarray(words).view(ml_dtypes.float8_e4m3fn).astype(np.float64)
    else:
        nib = np.empty((g, p, n, 4), np.uint8)
        nib[..., 0::2] = words & 0xF
        nib[..., 1::2] = words >> 4
        vals = E2M1[nib]
    vals = vals * np.repeat(np.exp2(scales.astype(np.float64) - 127.0), 8, axis=1)[..., None]
    return vals.transpose(0, 1, 3, 2).reshape(g * 512, n)
def pack4(w):
    words, scales = pack_weight(w, "e2m1")
    return words.reshape(words.shape[0], 128, -1), scales


def unpack4(words, scales):
    return unpack_weight(words.reshape(words.shape[0], 128, -1, 2), scales, "e2m1")


T, K, R, C = 2048, 1024, 512, 1024


def draw0():
    s = mx_kscale(K)
    v = mx_kscale(T)
    a = T ** -0.25
    far = np.random.standard_normal((T, K)) * s * v[:, None]
    mic = np.random.standard_normal((T, C)) * v[:, None]
    path = np.random.standard_normal((K, C)) / np.sqrt(K) / s[:, None]
    basis = np.random.standard_normal((K, R)) / np.sqrt(K) * a / s[:, None]
    basis_words, basis_scales = pack4(basis)
    step = (0.5 + np.random.random(T)) * a / v ** 2
    gain = 0.5 + np.random.random(R)
    return {"far": bf(far),
            "mic": bf(mic),
            "path": bf(path),
            "basis_words": basis_words,
            "basis_scales": basis_scales,
            "step": bf(step),
            "gain": bf(gain)}


def core(far, mic, path, basis_words, basis_scales, step, gain):
    x = mxq(f64(far), 1, "e4m3")
    echo = x @ mxq(f64(path), 0, "e4m3")
    u = x @ unpack4(basis_words, basis_scales)
    e = (f64(mic) - echo) * f64(step)[:, None]
    grad = mxq(u, 0, "e4m3").T @ mxq(e, 0, "e4m3")
    return grad * f64(gain)[:, None]


def e4m3fn_bytes(y):
    return np.clip(np.asarray(y, np.float64), -448.0, 448.0).astype(np.float32).astype(ml_dtypes.float8_e4m3fn).view(np.uint8)


def e4m3fn_values(b):
    return np.asarray(b, np.uint8).view(ml_dtypes.float8_e4m3fn).astype(np.float64)


def setup_inputs():
    d = draw0()
    x0 = np.asarray(d['path']).astype(np.float64)
    s = (np.max(np.abs(x0), axis=(1,), keepdims=True) / 448.0).astype(np.float32)
    out = {}
    for k, v in d.items():
        if k == 'path':
            out['path_bytes'] = e4m3fn_bytes(x0 / s.astype(np.float64))
            out['path_scale'] = s
        else:
            out[k] = v
    return out


def reference(far, mic, path_bytes, path_scale, basis_words, basis_scales, step, gain):
    return core(far, mic, e4m3fn_values(path_bytes) * path_scale.astype(np.float64), basis_words, basis_scales, step, gain)

@@ -1,0 +1,598 @@
+from contextlib import ExitStack
+
+import concourse.mybir as mybir
+from concourse.masks import make_identity
+
+T, K, R, C = 2048, 1024, 512, 1024
+FLOPS = 2 * T * K * C + 2 * T * K * R + 2 * T * R * C
+
+F32 = mybir.dt.float32
+BF16 = mybir.dt.bfloat16
+I32 = mybir.dt.int32
+U32 = mybir.dt.uint32
+U8 = mybir.dt.uint8
+FP8 = mybir.dt.float8_e4m3fn
+FP8X4 = mybir.dt.float8_e4m3fn_x4
+FP4X4 = mybir.dt.float4_e2m1fn_x4
+ALU = mybir.AluOpType
+COPY = mybir.ActivationFunctionType.Copy
+
+P = 128
+PACK = 4
+PASS = P * PACK
+NG = T // PASS
+NK = K // PASS
+NH = 2
+W = C // NH
+
+
+def tile_echo_nlms_gradient_s11_kernel(
+    tc, far, mic, path_bytes, path_scale, basis_words, basis_scales, step, gain, out
+):
+    nc = tc.nc
+    with ExitStack() as ctx:
+        keep = ctx.enter_context(tc.tile_pool(name="keep", bufs=1))
+        work = ctx.enter_context(tc.tile_pool(name="work", bufs=2))
+        turn = ctx.enter_context(tc.psum_pool(name="turn", bufs=3))
+        comp = ctx.enter_context(tc.psum_pool(name="comp", bufs=2))
+        echo = ctx.enter_context(tc.psum_pool(name="echo", bufs=3))
+
+        ident = keep.tile([P, P], F32, name="ident")
+        make_identity(nc, ident[:])
+        pscale = keep.tile([P, NK, PACK], F32, name="pscale")
+        nc.scalar.dma_start(out=pscale[:], in_=path_scale.rearrange("(g p t) o -> p g (t o)", p=P, t=PACK))
+        step_bf = keep.tile([P, NG, PACK], BF16, name="step_bf")
+        nc.scalar.dma_start(out=step_bf[:], in_=step.rearrange("(g p j) -> p g j", p=P, j=PACK))
+        gain_bf = keep.tile([P, PACK], BF16, name="gain_bf")
+        nc.scalar.dma_start(out=gain_bf[:], in_=gain.rearrange("(q m) -> q m", m=PACK))
+        bscale = keep.tile([P, NK, R], U8, name="bscale", align_bytes=64)
+        nc.vector.memset(bscale[:].rearrange("p g n -> p (g n)").bitcast(I32), 0)
+
+        far_t = [keep.tile([P, PACK, K], BF16, name=f"far{g}") for g in range(NG)]
+        mic_t = [[keep.tile([P, PACK, W], BF16, name=f"mic{g}_{h}") for h in range(NH)] for g in range(NG)]
+        pbytes = [keep.tile([P, PACK, C], U8, name=f"pbytes{g}", align_bytes=64) for g in range(NK)]
+        bwords = keep.tile([P, NK, 2 * R], U8, name="bwords", align_bytes=64)
+        far_v = far.rearrange("(g p j) k -> g p j k", p=P, j=PACK)
+        mic_v = mic.rearrange("(g p j) c -> g p j c", p=P, j=PACK)
+        path_v = path_bytes.rearrange("(g p t) c -> g p t c", p=P, t=PACK)
+
+        def load_far(g, lo, hi):
+            nc.sync.dma_start(out=far_t[g][:, lo:hi, :], in_=far_v[g][:, lo:hi, :])
+
+        def load_mic(g, h):
+            nc.sync.dma_start(out=mic_t[g][h][:], in_=mic_v[g][:, :, h * W : (h + 1) * W])
+
+        def load_path(g, half):
+            ts = slice(2 * half, 2 * half + 2)
+            nc.sync.dma_start(out=pbytes[g][:, ts, :], in_=path_v[g][:, ts, :])
+
+        def load_basis():
+            nc.sync.dma_start(out=bwords[:], in_=basis_words.rearrange("g p n -> p g n"))
+
+        def load_scales():
+            for q in range(4):
+                nc.sync.dma_start(
+                    out=bscale[32 * q : 32 * q + 4, :, :].bitcast(I32),
+                    in_=basis_scales[:, 4 * q : 4 * q + 4, :].bitcast(I32).rearrange("g q n -> q g n"),
+                )
+
+
+        steps = keep.tile([P, NG, PACK], F32, name="steps")
+        negstep = keep.tile([P, NG, PACK], F32, name="negstep")
+        gains = keep.tile([P, PACK], F32, name="gains")
+
+        def prep_steps():
+            nc.gpsimd.tensor_copy(out=steps[:], in_=step_bf[:])
+            nc.gpsimd.tensor_scalar(out=negstep[:], in0=step_bf[:], scalar1=-1.0, scalar2=0.0, op0=ALU.mult, op1=ALU.add)
+
+        def prep_gains():
+            nc.gpsimd.tensor_copy(out=gains[:], in_=gain_bf[:])
+
+
+        x_codes = [keep.tile([P, NK, PASS], U32, name=f"x_codes{g}", align_bytes=64) for g in range(NG)]
+        x_scales = [keep.tile([P, NK, PASS], U8, name=f"x_scales{g}", align_bytes=64) for g in range(NG)]
+        p_codes = [[keep.tile([P, W], U32, name=f"p_codes{g}_{h}", align_bytes=64) for h in range(NH)] for g in range(NK)]
+        p_scales = [[keep.tile([P, W], U8, name=f"p_scales{g}_{h}", align_bytes=64) for h in range(NH)] for g in range(NK)]
+        u_codes = [keep.tile([P, R], U32, name=f"u_codes{g}", align_bytes=64) for g in range(NG)]
+        u_scales = [keep.tile([P, R], U8, name=f"u_scales{g}", align_bytes=64) for g in range(NG)]
+        e_codes = [[keep.tile([P, W], U32, name=f"e_codes{g}_{h}", align_bytes=64) for h in range(NH)] for g in range(NG)]
+        e_scales = [[keep.tile([P, W], U8, name=f"e_scales{g}_{h}", align_bytes=64) for h in range(NH)] for g in range(NG)]
+
+        pwide = [[keep.tile([P, PACK, W], BF16, name=f"pwide{g}_{h}") for h in range(NH)] for g in range(NK)]
+        pil = {}
+
+        def widen_v(g, h, t):
+            nc.vector.tensor_scalar(
+                out=pwide[g][h][:, t, :],
+                in0=pbytes[g][:, t, h * W : (h + 1) * W].bitcast(FP8),
+                scalar1=pscale[:, g, t : t + 1],
+                scalar2=None,
+                op0=ALU.mult,
+            )
+
+        def widen(g, h, t):
+            nc.scalar.activation(
+                out=pwide[g][h][:, t, :],
+                in_=pbytes[g][:, t, h * W : (h + 1) * W].bitcast(FP8),
+                func=COPY,
+                scale=pscale[:, g, t : t + 1],
+            )
+
+        def path_il(g, h):
+            pil[g, h] = work.tile([P, W, PACK], BF16, name="p_grouped", align_bytes=64)
+            nc.vector.tensor_copy(
+                out=pil[g, h][:].rearrange("p (c i) t -> p c t i", i=4),
+                in_=pwide[g][h][:].rearrange("p t (c i) -> p c t i", i=4),
+            )
+
+        def path_il_s(g, h):
+            pil[g, h] = work.tile([P, W, PACK], BF16, name="p_grouped", align_bytes=64)
+            nc.scalar.copy(
+                out=pil[g, h][:].rearrange("p (c i) t -> p c t i", i=4),
+                in_=pwide[g][h][:].rearrange("p t (c i) -> p c t i", i=4),
+            )
+
+        def path_q(g, h):
+            nc.vector.quantize_mx(
+                out=p_codes[g][h][:].bitcast(FP8X4),
+                scales=p_scales[g][h][:],
+                in_=pil[g, h][:].rearrange("p c t -> p (c t)"),
+            )
+
+        xg = {}
+
+        xbank = {}
+
+        def far_turn(g, half, k):
+            words = far_t[g][:].bitcast(F32)
+            bank = turn.tile([P, 2, 2, P], F32, name="turn_bank")
+            for jj in range(2):
+                for u in range(2):
+                    nc.tensor.transpose(
+                        bank[:, jj, u, :], words[:, 2 * half + jj, 256 * k + u : 256 * (k + 1) : 2], ident[:]
+                    )
+            xbank[g, half, k] = bank
+
+        def far_copy(g, half, k):
+            if g not in xg:
+                xg[g] = work.tile([P, NK, PACK, P, 2], F32, name="x_grouped", align_bytes=64)
+            nc.scalar.copy(
+                out=xg[g][:, k, 2 * half : 2 * half + 2, :, :],
+                in_=xbank[g, half, k][:].rearrange("p j u n -> p j n u"),
+            )
+
+        def far_q(g, k):
+            flat = xg[g][:].rearrange("p k j n u -> p k (j n u)").bitcast(BF16)
+            nc.vector.quantize_mx(
+                out=x_codes[g][:, k, :].bitcast(FP8X4), scales=x_scales[g][:, k, :], in_=flat[:, k, :]
+            )
+
+        def far_q2(g):
+            nc.vector.quantize_mx(
+                out=x_codes[g][:].rearrange("p k n -> p (k n)").bitcast(FP8X4),
+                scales=x_scales[g][:].rearrange("p k n -> p (k n)"),
+                in_=xg[g][:].rearrange("p k j n u -> p (k j n u)").bitcast(BF16),
+            )
+
+        ug = {}
+
+        ubank = {}
+
+        def comp_mm(g, chunk):
+            bank = comp.tile([P, PACK, P], F32, name="comp_bank")
+            cols = slice(chunk * P, (chunk + 1) * P)
+            for j in range(PACK):
+                for k in range(NK):
+                    nc.tensor.matmul_mx(
+                        out=bank[:, j, :],
+                        lhsT=x_codes[g][:, k, j * P : (j + 1) * P].bitcast(FP8X4),
+                        lhsT_scale=x_scales[g][:, k, j * P : (j + 1) * P],
+                        rhs=bwords[:, k, 2 * chunk * P : 2 * (chunk + 1) * P].bitcast(FP4X4),
+                        rhs_scale=bscale[:, k, cols],
+                        start=(k == 0),
+                        stop=(k == NK - 1),
+                    )
+            ubank[g, chunk] = bank
+
+        def comp_copy(g, chunk):
+            if g not in ug:
+                ug[g] = work.tile([P, 4, P, PACK], BF16, name="u_grouped", align_bytes=64)
+            nc.scalar.copy(
+                out=ug[g][:, :, 32 * chunk : 32 * (chunk + 1), :],
+                in_=ubank[g, chunk][:].rearrange("p j (q m) -> p m q j", m=4),
+            )
+
+        def comp_q(g):
+            nc.vector.quantize_mx(
+                out=u_codes[g][:].bitcast(FP8X4),
+                scales=u_scales[g][:],
+                in_=ug[g][:].rearrange("p m q j -> p (m q j)"),
+            )
+
+        ms = {}
+        ep = {}
+        eg = {}
+        ebank = {}
+
+        def mic_scale_v(g, h, j):
+            if (g, h) not in ms:
+                ms[g, h] = work.tile([P, PACK, W], F32, name="mic_scaled", bufs=3)
+            nc.vector.tensor_scalar(
+                out=ms[g, h][:, j, :], in0=mic_t[g][h][:, j, :], scalar1=steps[:, g, j : j + 1], scalar2=None, op0=ALU.mult
+            )
+
+        def mic_scale_g(g, h, j):
+            if (g, h) not in ms:
+                ms[g, h] = work.tile([P, PACK, W], F32, name="mic_scaled", bufs=3)
+            nc.gpsimd.tensor_scalar(
+                out=ms[g, h][:, j, :],
+                in0=mic_t[g][h][:, j, :],
+                scalar1=steps[:, g, j : j + 1],
+                scalar2=0.0,
+                op0=ALU.mult,
+                op1=ALU.add,
+            )
+
+        def mic_scale(g, h, j):
+            if (g, h) not in ms:
+                ms[g, h] = work.tile([P, PACK, W], F32, name="mic_scaled", bufs=3)
+            nc.scalar.activation(
+                out=ms[g, h][:, j, :], in_=mic_t[g][h][:, j, :], func=COPY, scale=steps[:, g, j : j + 1]
+            )
+
+        def echo_mm(g, h, j):
+            bank = echo.tile([P, W], F32, name="echo_bank")
+            for k in range(NK):
+                nc.tensor.matmul_mx(
+                    out=bank[:],
+                    lhsT=x_codes[g][:, k, j * P : (j + 1) * P].bitcast(FP8X4),
+                    lhsT_scale=x_scales[g][:, k, j * P : (j + 1) * P],
+                    rhs=p_codes[k][h][:].bitcast(FP8X4),
+                    rhs_scale=p_scales[k][h][:],
+                    start=(k == 0),
+                    stop=(k == NK - 1),
+                )
+            ebank[g, h, j] = bank
+
+        def err(g, h, j):
+            if (g, h) not in ep:
+                ep[g, h] = work.tile([P, PACK, W], BF16, name="e_rows", bufs=3)
+            nc.vector.scalar_tensor_tensor(
+                out=ep[g, h][:, j, :],
+                in0=ebank[g, h, j][:],
+                scalar=negstep[:, g, j : j + 1],
+                in1=ms[g, h][:, j, :],
+                op0=ALU.mult,
+                op1=ALU.add,
+            )
+
+        def err_il(g, h, lo, hi):
+            if (g, h) not in eg:
+                eg[g, h] = work.tile([P, W, PACK], BF16, name="e_grouped", align_bytes=64)
+            nc.vector.tensor_copy(
+                out=eg[g, h][:, lo:hi, :].rearrange("p (c i) j -> p c j i", i=4),
+                in_=ep[g, h][:, :, lo:hi].rearrange("p j (c i) -> p c j i", i=4),
+            )
+
+        def err_il_s(g, h, lo, hi):
+            if (g, h) not in eg:
+                eg[g, h] = work.tile([P, W, PACK], BF16, name="e_grouped", align_bytes=64)
+            nc.scalar.copy(
+                out=eg[g, h][:, lo:hi, :].rearrange("p (c i) j -> p c j i", i=4),
+                in_=ep[g, h][:, :, lo:hi].rearrange("p j (c i) -> p c j i", i=4),
+            )
+
+        def err_q(g, h, lo=0, hi=W):
+            nc.vector.quantize_mx(
+                out=e_codes[g][h][:, lo:hi].bitcast(FP8X4),
+                scales=e_scales[g][h][:, lo:hi],
+                in_=eg[g, h][:, lo:hi, :].rearrange("p c j -> p (c j)"),
+            )
+
+        out_v = out.rearrange("(q m) c -> m q c", m=4)
+
+        def grad_mm(bank, g, h, m):
+            nc.tensor.matmul_mx(
+                out=bank[:],
+                lhsT=u_codes[g][:, m * P : (m + 1) * P].bitcast(FP8X4),
+                lhsT_scale=u_scales[g][:, m * P : (m + 1) * P],
+                rhs=e_codes[g][h][:].bitcast(FP8X4),
+                rhs_scale=e_scales[g][h][:],
+                start=(g == 0),
+                stop=(g == NG - 1),
+            )
+
+        gbank = {}
+
+        def grad0(m):
+            bank = comp.tile([P, W], F32, name="comp_bank")
+            for g in range(NG):
+                grad_mm(bank, g, 0, m)
+            gbank[0, m] = bank
+
+        def grad1(m):
+            if m < 2:
+                bank = turn.tile([P, W], F32, name="turn_bank")
+            else:
+                bank = comp.tile([P, W], F32, name="comp_bank")
+            for g in range(NG - 1):
+                grad_mm(bank, g, 1, m)
+            gbank[1, m] = bank
+
+        def grad2(m):
+            grad_mm(gbank[1, m], NG - 1, 1, m)
+
+        def out_s(h, m):
+            res = work.tile([P, W], F32, name="res", bufs=4)
+            nc.scalar.activation(out=res[:], in_=gbank[h, m][:], func=COPY, scale=gains[:, m : m + 1])
+            nc.sync.dma_start(out=out_v[m][:, h * W : (h + 1) * W], in_=res[:])
+
+        def out_v_(h, m):
+            res = work.tile([P, W], F32, name="res", bufs=4)
+            nc.vector.tensor_scalar(
+                out=res[:], in0=gbank[h, m][:], scalar1=gains[:, m : m + 1], scalar2=None, op0=ALU.mult
+            )
+            nc.sync.dma_start(out=out_v[m][:, h * W : (h + 1) * W], in_=res[:])
+
+        ctx.enter_context(tc.manual_schedule())
+        load_path(1, 1)
+        load_path(0, 0)
+        load_path(0, 1)
+        load_path(1, 0)
+        load_far(0, 0, 2)
+        load_far(0, 2, 4)
+        load_far(1, 2, 4)
+        load_far(1, 0, 2)
+        load_far(3, 0, 2)
+        load_mic(0, 0)
+        load_far(2, 2, 4)
+        load_mic(1, 0)
+        load_basis()
+        load_far(3, 2, 4)
+        load_far(2, 0, 2)
+        load_mic(1, 1)
+        load_mic(0, 1)
+        load_mic(3, 0)
+        load_mic(3, 1)
+        load_mic(2, 1)
+        load_scales()
+        load_mic(2, 0)
+        widen_v(1, 0, 3)
+        prep_steps()
+        far_turn(0, 0, 1)
+        widen_v(1, 0, 2)
+        widen_v(1, 1, 3)
+        widen(1, 1, 2)
+        far_turn(0, 0, 0)
+        widen_v(0, 0, 0)
+        far_turn(0, 1, 1)
+        widen(0, 0, 1)
+        widen_v(0, 1, 0)
+        widen(0, 0, 2)
+        far_turn(0, 1, 0)
+        widen_v(0, 0, 3)
+        widen_v(0, 1, 2)
+        widen_v(1, 0, 0)
+        path_il(0, 0)
+        widen(1, 0, 1)
+        widen(1, 1, 0)
+        path_il(1, 0)
+        widen(1, 1, 1)
+        far_copy(0, 0, 1)
+        path_q(0, 0)
+        far_copy(0, 0, 0)
+        far_turn(1, 1, 0)
+        far_turn(1, 1, 1)
+        far_copy(0, 1, 1)
+        far_turn(1, 0, 1)
+        far_copy(0, 1, 0)
+        path_q(1, 0)
+        far_copy(1, 1, 0)
+        far_q(0, 1)
+        far_turn(1, 0, 0)
+        far_copy(1, 1, 1)
+        far_q(0, 0)
+        echo_mm(0, 0, 0)
+        echo_mm(0, 0, 2)
+        far_copy(1, 0, 1)
+        far_copy(1, 0, 0)
+        mic_scale(0, 0, 0)
+        widen(0, 1, 3)
+        far_turn(3, 0, 1)
+        path_il(1, 1)
+        far_q2(1)
+        widen(0, 1, 1)
+        path_q(1, 1)
+        far_turn(3, 0, 0)
+        far_turn(2, 1, 1)
+        err(0, 0, 0)
+        echo_mm(1, 0, 1)
+        mic_scale(0, 0, 2)
+        err(0, 0, 2)
+        mic_scale_g(1, 0, 1)
+        mic_scale_g(0, 0, 1)
+        err(1, 0, 1)
+        far_copy(3, 0, 1)
+        echo_mm(0, 0, 1)
+        err(0, 0, 1)
+        mic_scale_g(0, 0, 3)
+        echo_mm(0, 0, 3)
+        err(0, 0, 3)
+        prep_gains()
+        echo_mm(1, 0, 0)
+        far_copy(3, 0, 0)
+        path_il_s(0, 1)
+        far_turn(3, 1, 1)
+        err_il(0, 0, 0, 256)
+        far_copy(2, 1, 1)
+        far_turn(3, 1, 0)
+        mic_scale_g(1, 0, 2)
+        mic_scale_g(1, 0, 0)
+        mic_scale_g(1, 1, 2)
+        echo_mm(1, 0, 2)
+        err(1, 0, 0)
+        echo_mm(1, 0, 3)
+        far_turn(2, 1, 0)
+        far_copy(3, 1, 1)
+        far_copy(3, 1, 0)
+        mic_scale_g(1, 0, 3)
+        path_q(0, 1)
+        far_turn(2, 0, 1)
+        err(1, 0, 2)
+        far_q2(3)
+        mic_scale_g(3, 0, 0)
+        err_il_s(0, 0, 256, 512)
+        far_turn(2, 0, 0)
+        echo_mm(1, 1, 2)
+        mic_scale(3, 0, 1)
+        err(1, 0, 3)
+        far_copy(2, 0, 0)
+        far_copy(2, 0, 1)
+        far_copy(2, 1, 0)
+        err_q(0, 0, 0, 512)
+        comp_mm(0, 0)
+        comp_copy(0, 0)
+        echo_mm(1, 1, 1)
+        err(1, 1, 2)
+        mic_scale(3, 0, 3)
+        err_il(1, 0, 0, 256)
+        mic_scale_g(1, 1, 1)
+        mic_scale_g(3, 0, 2)
+        mic_scale_g(1, 1, 3)
+        echo_mm(3, 0, 0)
+        err(1, 1, 1)
+        comp_mm(1, 0)
+        comp_copy(1, 0)
+        echo_mm(1, 1, 0)
+        comp_mm(1, 1)
+        err(3, 0, 0)
+        mic_scale(1, 1, 0)
+        echo_mm(3, 0, 3)
+        comp_copy(1, 1)
+        err_il_s(1, 0, 256, 512)
+        echo_mm(1, 1, 3)
+        mic_scale_g(2, 0, 2)
+        far_q2(2)
+        comp_mm(0, 1)
+        comp_copy(0, 1)
+        mic_scale_g(2, 0, 0)
+        err(1, 1, 0)
+        comp_mm(0, 2)
+        comp_copy(0, 2)
+        mic_scale_g(0, 1, 1)
+        echo_mm(2, 0, 2)
+        err(3, 0, 3)
+        err(1, 1, 3)
+        err_q(1, 0, 0, 512)
+        echo_mm(3, 0, 2)
+        mic_scale(2, 0, 1)
+        mic_scale(0, 1, 3)
+        comp_mm(0, 3)
+        comp_copy(0, 3)
+        mic_scale_g(2, 0, 3)
+        echo_mm(3, 0, 1)
+        err(2, 0, 2)
+        comp_mm(1, 2)
+        comp_copy(1, 2)
+        echo_mm(2, 0, 1)
+        err_il_s(1, 1, 256, 512)
+        err_il(1, 1, 0, 256)
+        echo_mm(2, 0, 0)
+        comp_mm(2, 0)
+        err(3, 0, 2)
+        err(3, 0, 1)
+        mic_scale_g(3, 1, 2)
+        comp_mm(1, 3)
+        comp_q(0)
+        err(2, 0, 1)
+        comp_copy(2, 0)
+        echo_mm(2, 0, 3)
+        echo_mm(0, 1, 1)
+        mic_scale_g(0, 1, 2)
+        comp_copy(1, 3)
+        comp_mm(2, 1)
+        err_il(3, 0, 0, 256)
+        err(2, 0, 0)
+        err_il_s(3, 0, 256, 512)
+        echo_mm(0, 1, 2)
+        mic_scale_g(2, 1, 2)
+        err(2, 0, 3)
+        comp_copy(2, 1)
+        comp_mm(3, 0)
+        err_q(1, 1, 0, 512)
+        mic_scale_g(2, 1, 0)
+        err_il_s(2, 0, 256, 512)
+        echo_mm(3, 1, 2)
+        comp_copy(3, 0)
+        echo_mm(0, 1, 3)
+        err(0, 1, 1)
+        comp_q(1)
+        comp_mm(3, 1)
+        err(0, 1, 2)
+        err_il(2, 0, 0, 256)
+        mic_scale_g(3, 1, 0)
+        echo_mm(0, 1, 0)
+        mic_scale(0, 1, 0)
+        comp_copy(3, 1)
+        mic_scale(2, 1, 1)
+        comp_mm(3, 2)
+        comp_copy(3, 2)
+        err(3, 1, 2)
+        echo_mm(2, 1, 0)
+        err(0, 1, 3)
+        err(0, 1, 0)
+        comp_mm(3, 3)
+        comp_copy(3, 3)
+        echo_mm(2, 1, 3)
+        comp_mm(2, 2)
+        err_q(2, 0, 0, 512)
+        err(2, 1, 0)
+        mic_scale(2, 1, 3)
+        echo_mm(2, 1, 2)
+        comp_mm(2, 3)
+        comp_copy(2, 2)
+        err_q(3, 0, 0, 512)
+        comp_q(3)
+        echo_mm(2, 1, 1)
+        err(2, 1, 3)
+        comp_copy(2, 3)
+        err(2, 1, 2)
+        err_il_s(0, 1, 384, 512)
+        echo_mm(3, 1, 0)
+        echo_mm(3, 1, 1)
+        err(2, 1, 1)
+        echo_mm(3, 1, 3)
+        comp_q(2)
+        grad0(2)
+        err_il_s(2, 1, 256, 512)
+        mic_scale(3, 1, 1)
+        err_il(0, 1, 0, 384)
+        err(3, 1, 0)
+        err_il(2, 1, 0, 256)
+        err_q(0, 1, 0, 512)
+        out_s(0, 2)
+        err(3, 1, 1)
+        grad0(0)
+        out_s(0, 0)
+        grad0(1)
+        grad0(3)
+        err_q(2, 1, 0, 512)
+        grad1(1)
+        grad1(3)
+        out_s(0, 1)
+        grad1(0)
+        mic_scale_g(3, 1, 3)
+        err(3, 1, 3)
+        err_il_s(3, 1, 352, 512)
+        err_il(3, 1, 0, 352)
+        err_q(3, 1, 0, 512)
+        out_s(0, 3)
+        grad2(0)
+        out_s(1, 0)
+        grad2(1)
+        out_v_(1, 1)
+        grad2(3)
+        out_v_(1, 3)
+        grad1(2)
+        grad2(2)
+        out_s(1, 2)

@@ -22,8 +22,12 @@ PACK = 4
 PASS = P * PACK
 NG = T // PASS
 NK = K // PASS
-NH = 2
-W = C // NH
+WIDTH = [512, 512]
+MS_BUFS = 1
+POOL_ROWS = 2
+TAIL = 256
+NH = len(WIDTH)
+COLS = [slice(sum(WIDTH[:h]), sum(WIDTH[: h + 1])) for h in range(NH)]
 
 
 def tile_echo_nlms_gradient_s11_kernel(
@@ -33,566 +37,379 @@ def tile_echo_nlms_gradient_s11_kernel(
     with ExitStack() as ctx:
         keep = ctx.enter_context(tc.tile_pool(name="keep", bufs=1))
         work = ctx.enter_context(tc.tile_pool(name="work", bufs=2))
-        turn = ctx.enter_context(tc.psum_pool(name="turn", bufs=3))
-        comp = ctx.enter_context(tc.psum_pool(name="comp", bufs=2))
-        echo = ctx.enter_context(tc.psum_pool(name="echo", bufs=3))
+        side = ctx.enter_context(tc.psum_pool(name="side", bufs=4))
+        echo = ctx.enter_context(tc.psum_pool(name="echo", bufs=4))
+        ctx.enter_context(tc.manual_schedule())
 
         ident = keep.tile([P, P], F32, name="ident")
-        make_identity(nc, ident[:])
         pscale = keep.tile([P, NK, PACK], F32, name="pscale")
-        nc.scalar.dma_start(out=pscale[:], in_=path_scale.rearrange("(g p t) o -> p g (t o)", p=P, t=PACK))
         step_bf = keep.tile([P, NG, PACK], BF16, name="step_bf")
-        nc.scalar.dma_start(out=step_bf[:], in_=step.rearrange("(g p j) -> p g j", p=P, j=PACK))
         gain_bf = keep.tile([P, PACK], BF16, name="gain_bf")
-        nc.scalar.dma_start(out=gain_bf[:], in_=gain.rearrange("(q m) -> q m", m=PACK))
+        negstep = keep.tile([P, NG, PACK], F32, name="negstep")
+        gains = keep.tile([P, PACK], F32, name="gains")
         bscale = keep.tile([P, NK, R], U8, name="bscale", align_bytes=64)
-        nc.vector.memset(bscale[:].rearrange("p g n -> p (g n)").bitcast(I32), 0)
-
-        far_t = [keep.tile([P, PACK, K], BF16, name=f"far{g}") for g in range(NG)]
-        mic_t = [[keep.tile([P, PACK, W], BF16, name=f"mic{g}_{h}") for h in range(NH)] for g in range(NG)]
-        pbytes = [keep.tile([P, PACK, C], U8, name=f"pbytes{g}", align_bytes=64) for g in range(NK)]
         bwords = keep.tile([P, NK, 2 * R], U8, name="bwords", align_bytes=64)
         far_v = far.rearrange("(g p j) k -> g p j k", p=P, j=PACK)
         mic_v = mic.rearrange("(g p j) c -> g p j c", p=P, j=PACK)
         path_v = path_bytes.rearrange("(g p t) c -> g p t c", p=P, t=PACK)
+        out_v = out.rearrange("(q m) c -> m q c", m=PACK)
+        out_q = out.rearrange("(q m) c -> q m c", m=PACK)
+
+        far_t, mic_t, pbytes = {}, {}, {}
 
         def load_far(g, lo, hi):
-            nc.sync.dma_start(out=far_t[g][:, lo:hi, :], in_=far_v[g][:, lo:hi, :])
+            rows = keep.tile([P, hi - lo, K], BF16, name=f"far{g}_{lo}")
+            nc.sync.dma_start(out=rows[:], in_=far_v[g][:, lo:hi, :])
+            for j in range(lo, hi):
+                far_t[g, j] = rows[:, j - lo, :]
 
         def load_mic(g, h):
-            nc.sync.dma_start(out=mic_t[g][h][:], in_=mic_v[g][:, :, h * W : (h + 1) * W])
+            mic_t[g, h] = keep.tile([P, PACK, WIDTH[h]], BF16, name=f"mic{g}_{h}")
+            nc.sync.dma_start(out=mic_t[g, h][:], in_=mic_v[g][:, :, COLS[h]])
 
-        def load_path(g, half):
-            ts = slice(2 * half, 2 * half + 2)
-            nc.sync.dma_start(out=pbytes[g][:, ts, :], in_=path_v[g][:, ts, :])
+        def load_path(k, h):
+            pbytes[k, h] = keep.tile([P, 2, C], U8, name=f"pbytes{k}_{h}", align_bytes=64)
+            nc.sync.dma_start(out=pbytes[k, h][:], in_=path_v[k][:, 2 * h : 2 * h + 2, :])
 
-        def load_basis():
+        def load_basis_words():
             nc.sync.dma_start(out=bwords[:], in_=basis_words.rearrange("g p n -> p g n"))
 
-        def load_scales():
-            for q in range(4):
-                nc.sync.dma_start(
-                    out=bscale[32 * q : 32 * q + 4, :, :].bitcast(I32),
-                    in_=basis_scales[:, 4 * q : 4 * q + 4, :].bitcast(I32).rearrange("g q n -> q g n"),
-                )
+        def load_basis_scales(q):
+            nc.scalar.dma_start(
+                out=bscale[32 * q : 32 * q + 4, :, :].bitcast(I32),
+                in_=basis_scales[:, 4 * q : 4 * q + 4, :].bitcast(I32).rearrange("g q n -> q g n"),
+            )
 
-
-        steps = keep.tile([P, NG, PACK], F32, name="steps")
-        negstep = keep.tile([P, NG, PACK], F32, name="negstep")
-        gains = keep.tile([P, PACK], F32, name="gains")
-
-        def prep_steps():
-            nc.gpsimd.tensor_copy(out=steps[:], in_=step_bf[:])
-            nc.gpsimd.tensor_scalar(out=negstep[:], in0=step_bf[:], scalar1=-1.0, scalar2=0.0, op0=ALU.mult, op1=ALU.add)
-
-        def prep_gains():
-            nc.gpsimd.tensor_copy(out=gains[:], in_=gain_bf[:])
-
-
-        x_codes = [keep.tile([P, NK, PASS], U32, name=f"x_codes{g}", align_bytes=64) for g in range(NG)]
-        x_scales = [keep.tile([P, NK, PASS], U8, name=f"x_scales{g}", align_bytes=64) for g in range(NG)]
-        p_codes = [[keep.tile([P, W], U32, name=f"p_codes{g}_{h}", align_bytes=64) for h in range(NH)] for g in range(NK)]
-        p_scales = [[keep.tile([P, W], U8, name=f"p_scales{g}_{h}", align_bytes=64) for h in range(NH)] for g in range(NK)]
+        x_codes = [keep.tile([P, PACK, NK, P], U32, name=f"x_codes{g}", align_bytes=64) for g in range(NG)]
+        x_scales = [keep.tile([P, PACK, NK, P], U8, name=f"x_scales{g}", align_bytes=64) for g in range(NG)]
+        p_codes = [[keep.tile([P, WIDTH[h]], U32, name=f"p_codes{k}_{h}", align_bytes=64) for h in range(NH)] for k in range(NK)]
+        p_scales = [[keep.tile([P, WIDTH[h]], U8, name=f"p_scales{k}_{h}", align_bytes=64) for h in range(NH)] for k in range(NK)]
         u_codes = [keep.tile([P, R], U32, name=f"u_codes{g}", align_bytes=64) for g in range(NG)]
         u_scales = [keep.tile([P, R], U8, name=f"u_scales{g}", align_bytes=64) for g in range(NG)]
-        e_codes = [[keep.tile([P, W], U32, name=f"e_codes{g}_{h}", align_bytes=64) for h in range(NH)] for g in range(NG)]
-        e_scales = [[keep.tile([P, W], U8, name=f"e_scales{g}_{h}", align_bytes=64) for h in range(NH)] for g in range(NG)]
+        e_codes = [[keep.tile([P, WIDTH[h]], U32, name=f"e_codes{g}_{h}", align_bytes=64) for h in range(NH)] for g in range(NG)]
+        e_scales = [[keep.tile([P, WIDTH[h]], U8, name=f"e_scales{g}_{h}", align_bytes=64) for h in range(NH)] for g in range(NG)]
 
-        pwide = [[keep.tile([P, PACK, W], BF16, name=f"pwide{g}_{h}") for h in range(NH)] for g in range(NK)]
-        pil = {}
+        def interleave(engine, grouped, rows, lo, hi):
+            dst = grouped[:, lo:hi, :].rearrange("p (c i) t -> p c t i", i=4)
+            src = rows[:, :, lo:hi].rearrange("p t (c i) -> p c t i", i=4)
+            if engine == "vector":
+                nc.vector.tensor_copy(out=dst, in_=src)
+            else:
+                nc.scalar.copy(out=dst, in_=src)
 
-        def widen_v(g, h, t):
-            nc.vector.tensor_scalar(
-                out=pwide[g][h][:, t, :],
-                in0=pbytes[g][:, t, h * W : (h + 1) * W].bitcast(FP8),
-                scalar1=pscale[:, g, t : t + 1],
-                scalar2=None,
-                op0=ALU.mult,
-            )
+        def quantise(codes, scales, values):
+            nc.vector.quantize_mx(out=codes.bitcast(FP8X4), scales=scales, in_=values)
 
-        def widen(g, h, t):
-            nc.scalar.activation(
-                out=pwide[g][h][:, t, :],
-                in_=pbytes[g][:, t, h * W : (h + 1) * W].bitcast(FP8),
-                func=COPY,
-                scale=pscale[:, g, t : t + 1],
-            )
+        p_rows, p_grouped = {}, {}
 
-        def path_il(g, h):
-            pil[g, h] = work.tile([P, W, PACK], BF16, name="p_grouped", align_bytes=64)
-            nc.vector.tensor_copy(
-                out=pil[g, h][:].rearrange("p (c i) t -> p c t i", i=4),
-                in_=pwide[g][h][:].rearrange("p t (c i) -> p c t i", i=4),
-            )
+        def path_widen(engine, k, h, t):
+            if (k, h) not in p_rows:
+                p_rows[k, h] = work.tile([P, PACK, WIDTH[h]], BF16, name="p_rows", bufs=3)
+            dst, src, scale = p_rows[k, h][:, t, :], pbytes[k, t // 2][:, t % 2, COLS[h]].bitcast(FP8), pscale[:, k, t : t + 1]
+            if engine == "vector":
+                nc.vector.tensor_scalar(out=dst, in0=src, scalar1=scale, scalar2=None, op0=ALU.mult)
+            else:
+                nc.scalar.activation(out=dst, in_=src, func=COPY, scale=scale)
 
-        def path_il_s(g, h):
-            pil[g, h] = work.tile([P, W, PACK], BF16, name="p_grouped", align_bytes=64)
-            nc.scalar.copy(
-                out=pil[g, h][:].rearrange("p (c i) t -> p c t i", i=4),
-                in_=pwide[g][h][:].rearrange("p t (c i) -> p c t i", i=4),
-            )
+        def path_interleave(engine, k, h, lo=0, hi=None):
+            if (k, h) not in p_grouped:
+                p_grouped[k, h] = work.tile([P, WIDTH[h], PACK], BF16, name="p_grouped", align_bytes=64)
+            interleave(engine, p_grouped[k, h], p_rows[k, h], lo, hi)
 
-        def path_q(g, h):
-            nc.vector.quantize_mx(
-                out=p_codes[g][h][:].bitcast(FP8X4),
-                scales=p_scales[g][h][:],
-                in_=pil[g, h][:].rearrange("p c t -> p (c t)"),
-            )
+        def path_quantise(k, h):
+            quantise(p_codes[k][h][:], p_scales[k][h][:], p_grouped[k, h][:].rearrange("p c t -> p (c t)"))
 
-        xg = {}
+        x_grouped, side_bank = {}, {}
 
-        xbank = {}
-
-        def far_turn(g, half, k):
-            words = far_t[g][:].bitcast(F32)
-            bank = turn.tile([P, 2, 2, P], F32, name="turn_bank")
-            for jj in range(2):
+        def far_turn(g, j):
+            words = far_t[g, j].bitcast(F32)
+            bank = side.tile([P, NK, 2, P], F32, name="side_bank")
+            for k in range(NK):
                 for u in range(2):
-                    nc.tensor.transpose(
-                        bank[:, jj, u, :], words[:, 2 * half + jj, 256 * k + u : 256 * (k + 1) : 2], ident[:]
-                    )
-            xbank[g, half, k] = bank
+                    nc.tensor.transpose(bank[:, k, u, :], words[:, 256 * k + u : 256 * (k + 1) : 2], ident[:])
+            side_bank["far", g, j] = bank
 
-        def far_copy(g, half, k):
-            if g not in xg:
-                xg[g] = work.tile([P, NK, PACK, P, 2], F32, name="x_grouped", align_bytes=64)
-            nc.scalar.copy(
-                out=xg[g][:, k, 2 * half : 2 * half + 2, :, :],
-                in_=xbank[g, half, k][:].rearrange("p j u n -> p j n u"),
+        def far_copy(g, j):
+            if g not in x_grouped:
+                x_grouped[g] = work.tile([P, PACK, NK, P, 2], F32, name="x_grouped", align_bytes=64)
+            nc.scalar.copy(out=x_grouped[g][:, j, :, :, :], in_=side_bank["far", g, j][:].rearrange("p k u n -> p k n u"))
+
+        def far_quantise(g, lo, hi):
+            quantise(
+                x_codes[g][:, lo:hi, :, :].rearrange("p j k n -> p (j k n)"),
+                x_scales[g][:, lo:hi, :, :].rearrange("p j k n -> p (j k n)"),
+                x_grouped[g][:, lo:hi, :, :, :].rearrange("p j k n u -> p (j k n u)").bitcast(BF16),
             )
 
-        def far_q(g, k):
-            flat = xg[g][:].rearrange("p k j n u -> p k (j n u)").bitcast(BF16)
-            nc.vector.quantize_mx(
-                out=x_codes[g][:, k, :].bitcast(FP8X4), scales=x_scales[g][:, k, :], in_=flat[:, k, :]
-            )
+        u_grouped = {}
 
-        def far_q2(g):
-            nc.vector.quantize_mx(
-                out=x_codes[g][:].rearrange("p k n -> p (k n)").bitcast(FP8X4),
-                scales=x_scales[g][:].rearrange("p k n -> p (k n)"),
-                in_=xg[g][:].rearrange("p k j n u -> p (k j n u)").bitcast(BF16),
-            )
-
-        ug = {}
-
-        ubank = {}
-
-        def comp_mm(g, chunk):
-            bank = comp.tile([P, PACK, P], F32, name="comp_bank")
-            cols = slice(chunk * P, (chunk + 1) * P)
-            for j in range(PACK):
-                for k in range(NK):
-                    nc.tensor.matmul_mx(
-                        out=bank[:, j, :],
-                        lhsT=x_codes[g][:, k, j * P : (j + 1) * P].bitcast(FP8X4),
-                        lhsT_scale=x_scales[g][:, k, j * P : (j + 1) * P],
-                        rhs=bwords[:, k, 2 * chunk * P : 2 * (chunk + 1) * P].bitcast(FP4X4),
-                        rhs_scale=bscale[:, k, cols],
-                        start=(k == 0),
-                        stop=(k == NK - 1),
-                    )
-            ubank[g, chunk] = bank
+        def comp_mm(g, chunk, j, pool, name):
+            if ("u", g, chunk) not in side_bank:
+                side_bank["u", g, chunk] = pool.tile([P, PACK, P], F32, name=name)
+            for k in range(NK):
+                nc.tensor.matmul_mx(
+                    out=side_bank["u", g, chunk][:, j, :],
+                    lhsT=x_codes[g][:, j, k, :].bitcast(FP8X4),
+                    lhsT_scale=x_scales[g][:, j, k, :],
+                    rhs=bwords[:, k, 2 * chunk * P : 2 * (chunk + 1) * P].bitcast(FP4X4),
+                    rhs_scale=bscale[:, k, chunk * P : (chunk + 1) * P],
+                    start=(k == 0),
+                    stop=(k == NK - 1),
+                )
 
         def comp_copy(g, chunk):
-            if g not in ug:
-                ug[g] = work.tile([P, 4, P, PACK], BF16, name="u_grouped", align_bytes=64)
+            if g not in u_grouped:
+                u_grouped[g] = work.tile([P, PACK, P, PACK], BF16, name="u_grouped", align_bytes=64, bufs=3)
             nc.scalar.copy(
-                out=ug[g][:, :, 32 * chunk : 32 * (chunk + 1), :],
-                in_=ubank[g, chunk][:].rearrange("p j (q m) -> p m q j", m=4),
+                out=u_grouped[g][:, :, 32 * chunk : 32 * (chunk + 1), :],
+                in_=side_bank["u", g, chunk][:].rearrange("p j (q m) -> p m q j", m=PACK),
             )
 
-        def comp_q(g):
-            nc.vector.quantize_mx(
-                out=u_codes[g][:].bitcast(FP8X4),
-                scales=u_scales[g][:],
-                in_=ug[g][:].rearrange("p m q j -> p (m q j)"),
-            )
+        def comp_quantise(g):
+            quantise(u_codes[g][:], u_scales[g][:], u_grouped[g][:].rearrange("p m q j -> p (m q j)"))
 
-        ms = {}
-        ep = {}
-        eg = {}
-        ebank = {}
+        mic_scaled, e_rows, e_grouped, echo_bank = {}, {}, {}, {}
 
-        def mic_scale_v(g, h, j):
-            if (g, h) not in ms:
-                ms[g, h] = work.tile([P, PACK, W], F32, name="mic_scaled", bufs=3)
-            nc.vector.tensor_scalar(
-                out=ms[g, h][:, j, :], in0=mic_t[g][h][:, j, :], scalar1=steps[:, g, j : j + 1], scalar2=None, op0=ALU.mult
-            )
-
-        def mic_scale_g(g, h, j):
-            if (g, h) not in ms:
-                ms[g, h] = work.tile([P, PACK, W], F32, name="mic_scaled", bufs=3)
-            nc.gpsimd.tensor_scalar(
-                out=ms[g, h][:, j, :],
-                in0=mic_t[g][h][:, j, :],
-                scalar1=steps[:, g, j : j + 1],
-                scalar2=0.0,
-                op0=ALU.mult,
-                op1=ALU.add,
-            )
-
-        def mic_scale(g, h, j):
-            if (g, h) not in ms:
-                ms[g, h] = work.tile([P, PACK, W], F32, name="mic_scaled", bufs=3)
-            nc.scalar.activation(
-                out=ms[g, h][:, j, :], in_=mic_t[g][h][:, j, :], func=COPY, scale=steps[:, g, j : j + 1]
-            )
+        def mic_scale(engine, g, h, j):
+            mic_scaled[g, h, j] = work.tile([P, WIDTH[h]], F32, name=f"mic_scaled{j}", bufs=MS_BUFS)
+            dst, src, scale = mic_scaled[g, h, j][:], mic_t[g, h][:, j, :], negstep[:, g, j : j + 1]
+            if engine == "vector":
+                nc.vector.tensor_scalar(out=dst, in0=src, scalar1=scale, scalar2=None, op0=ALU.mult)
+            elif engine == "gpsimd":
+                nc.gpsimd.tensor_scalar(out=dst, in0=src, scalar1=scale, scalar2=0.0, op0=ALU.mult, op1=ALU.add)
+            else:
+                nc.scalar.activation(out=dst, in_=src, func=COPY, scale=scale)
 
         def echo_mm(g, h, j):
-            bank = echo.tile([P, W], F32, name="echo_bank")
+            bank = echo.tile([P, WIDTH[h]], F32, name="echo_bank")
             for k in range(NK):
                 nc.tensor.matmul_mx(
                     out=bank[:],
-                    lhsT=x_codes[g][:, k, j * P : (j + 1) * P].bitcast(FP8X4),
-                    lhsT_scale=x_scales[g][:, k, j * P : (j + 1) * P],
+                    lhsT=x_codes[g][:, j, k, :].bitcast(FP8X4),
+                    lhsT_scale=x_scales[g][:, j, k, :],
                     rhs=p_codes[k][h][:].bitcast(FP8X4),
                     rhs_scale=p_scales[k][h][:],
                     start=(k == 0),
                     stop=(k == NK - 1),
                 )
-            ebank[g, h, j] = bank
+            echo_bank[g, h, j] = bank
 
         def err(g, h, j):
-            if (g, h) not in ep:
-                ep[g, h] = work.tile([P, PACK, W], BF16, name="e_rows", bufs=3)
+            if (g, h) not in e_rows:
+                e_rows[g, h] = work.tile([P, PACK, WIDTH[h]], BF16, name="e_rows", bufs=4)
             nc.vector.scalar_tensor_tensor(
-                out=ep[g, h][:, j, :],
-                in0=ebank[g, h, j][:],
+                out=e_rows[g, h][:, j, :],
+                in0=echo_bank[g, h, j][:],
                 scalar=negstep[:, g, j : j + 1],
-                in1=ms[g, h][:, j, :],
+                in1=mic_scaled[g, h, j][:],
                 op0=ALU.mult,
-                op1=ALU.add,
+                op1=ALU.subtract,
             )
 
-        def err_il(g, h, lo, hi):
-            if (g, h) not in eg:
-                eg[g, h] = work.tile([P, W, PACK], BF16, name="e_grouped", align_bytes=64)
-            nc.vector.tensor_copy(
-                out=eg[g, h][:, lo:hi, :].rearrange("p (c i) j -> p c j i", i=4),
-                in_=ep[g, h][:, :, lo:hi].rearrange("p j (c i) -> p c j i", i=4),
+        def err_interleave(engine, g, h, lo=0, hi=None):
+            if (g, h) not in e_grouped:
+                e_grouped[g, h] = work.tile([P, WIDTH[h], PACK], BF16, name="e_grouped", align_bytes=64, bufs=3)
+            interleave(engine, e_grouped[g, h], e_rows[g, h], lo, hi)
+
+        def err_quantise(g, h, lo=0, hi=None):
+            quantise(
+                e_codes[g][h][:, lo:hi],
+                e_scales[g][h][:, lo:hi],
+                e_grouped[g, h][:, lo:hi, :].rearrange("p c j -> p (c j)"),
             )
 
-        def err_il_s(g, h, lo, hi):
-            if (g, h) not in eg:
-                eg[g, h] = work.tile([P, W, PACK], BF16, name="e_grouped", align_bytes=64)
-            nc.scalar.copy(
-                out=eg[g, h][:, lo:hi, :].rearrange("p (c i) j -> p c j i", i=4),
-                in_=ep[g, h][:, :, lo:hi].rearrange("p j (c i) -> p c j i", i=4),
-            )
+        def grad_mm(h, m, groups):
+            if ("grad", h, m) not in side_bank:
+                side_bank["grad", h, m] = side.tile([P, WIDTH[h]], F32, name="side_bank")
+            for g in groups:
+                nc.tensor.matmul_mx(
+                    out=side_bank["grad", h, m][:],
+                    lhsT=u_codes[g][:, m * P : (m + 1) * P].bitcast(FP8X4),
+                    lhsT_scale=u_scales[g][:, m * P : (m + 1) * P],
+                    rhs=e_codes[g][h][:].bitcast(FP8X4),
+                    rhs_scale=e_scales[g][h][:],
+                    start=(g == 0),
+                    stop=(g == NG - 1),
+                )
 
-        def err_q(g, h, lo=0, hi=W):
-            nc.vector.quantize_mx(
-                out=e_codes[g][h][:, lo:hi].bitcast(FP8X4),
-                scales=e_scales[g][h][:, lo:hi],
-                in_=eg[g, h][:, lo:hi, :].rearrange("p c j -> p (c j)"),
-            )
+        def tail_mm(c, pair, g):
+            if ("tail", c, pair) not in side_bank:
+                side_bank["tail", c, pair] = side.tile([P, 2, TAIL], F32, name="side_bank")
+            for i in range(2):
+                m = 2 * pair + i
+                nc.tensor.matmul_mx(
+                    out=side_bank["tail", c, pair][:, i, :],
+                    lhsT=u_codes[g][:, m * P : (m + 1) * P].bitcast(FP8X4),
+                    lhsT_scale=u_scales[g][:, m * P : (m + 1) * P],
+                    rhs=e_codes[g][1][:, c * TAIL : (c + 1) * TAIL].bitcast(FP8X4),
+                    rhs_scale=e_scales[g][1][:, c * TAIL : (c + 1) * TAIL],
+                    start=(g == 0 and i == 0),
+                    stop=(g == NG - 1 and i == 1),
+                )
 
-        out_v = out.rearrange("(q m) c -> m q c", m=4)
+        def tail_out(engine, c, pair):
+            res = work.tile([P, 2, TAIL], F32, name="res", bufs=4)
+            for i in range(2):
+                src, scale = side_bank["tail", c, pair][:, i, :], gains[:, 2 * pair + i : 2 * pair + i + 1]
+                if engine == "vector":
+                    nc.vector.tensor_scalar(out=res[:, i, :], in0=src, scalar1=scale, scalar2=None, op0=ALU.mult)
+                else:
+                    nc.scalar.activation(out=res[:, i, :], in_=src, func=COPY, scale=scale)
+            first = WIDTH[0] + c * TAIL
+            nc.sync.dma_start(out=out_q[:, 2 * pair : 2 * pair + 2, first : first + TAIL], in_=res[:])
 
-        def grad_mm(bank, g, h, m):
-            nc.tensor.matmul_mx(
-                out=bank[:],
-                lhsT=u_codes[g][:, m * P : (m + 1) * P].bitcast(FP8X4),
-                lhsT_scale=u_scales[g][:, m * P : (m + 1) * P],
-                rhs=e_codes[g][h][:].bitcast(FP8X4),
-                rhs_scale=e_scales[g][h][:],
-                start=(g == 0),
-                stop=(g == NG - 1),
-            )
-
-        gbank = {}
-
-        def grad0(m):
-            bank = comp.tile([P, W], F32, name="comp_bank")
-            for g in range(NG):
-                grad_mm(bank, g, 0, m)
-            gbank[0, m] = bank
-
-        def grad1(m):
-            if m < 2:
-                bank = turn.tile([P, W], F32, name="turn_bank")
+        def grad_out(engine, h, m):
+            res = work.tile([P, WIDTH[h]], F32, name="res", bufs=4)
+            bank, scale = side_bank["grad", h, m], gains[:, m : m + 1]
+            if engine == "vector":
+                nc.vector.tensor_scalar(out=res[:], in0=bank[:], scalar1=scale, scalar2=None, op0=ALU.mult)
             else:
-                bank = comp.tile([P, W], F32, name="comp_bank")
-            for g in range(NG - 1):
-                grad_mm(bank, g, 1, m)
-            gbank[1, m] = bank
+                nc.scalar.activation(out=res[:], in_=bank[:], func=COPY, scale=scale)
+            nc.sync.dma_start(out=out_v[m][:, COLS[h]], in_=res[:])
 
-        def grad2(m):
-            grad_mm(gbank[1, m], NG - 1, 1, m)
-
-        def out_s(h, m):
-            res = work.tile([P, W], F32, name="res", bufs=4)
-            nc.scalar.activation(out=res[:], in_=gbank[h, m][:], func=COPY, scale=gains[:, m : m + 1])
-            nc.sync.dma_start(out=out_v[m][:, h * W : (h + 1) * W], in_=res[:])
-
-        def out_v_(h, m):
-            res = work.tile([P, W], F32, name="res", bufs=4)
-            nc.vector.tensor_scalar(
-                out=res[:], in0=gbank[h, m][:], scalar1=gains[:, m : m + 1], scalar2=None, op0=ALU.mult
-            )
-            nc.sync.dma_start(out=out_v[m][:, h * W : (h + 1) * W], in_=res[:])
-
-        ctx.enter_context(tc.manual_schedule())
-        load_path(1, 1)
+        nc.vector.memset(bscale[:].rearrange("p g n -> p (g n)").bitcast(I32), 0)
+        make_identity(nc, ident[:])
+        nc.scalar.dma_start(out=pscale[:], in_=path_scale.rearrange("(g p t) o -> p g (t o)", p=P, t=PACK))
         load_path(0, 0)
+        load_far(0, 0, 1)
         load_path(0, 1)
-        load_path(1, 0)
-        load_far(0, 0, 2)
+        load_far(0, 1, 2)
         load_far(0, 2, 4)
-        load_far(1, 2, 4)
-        load_far(1, 0, 2)
-        load_far(3, 0, 2)
-        load_mic(0, 0)
-        load_far(2, 2, 4)
-        load_mic(1, 0)
-        load_basis()
-        load_far(3, 2, 4)
-        load_far(2, 0, 2)
-        load_mic(1, 1)
-        load_mic(0, 1)
-        load_mic(3, 0)
-        load_mic(3, 1)
-        load_mic(2, 1)
-        load_scales()
-        load_mic(2, 0)
-        widen_v(1, 0, 3)
-        prep_steps()
-        far_turn(0, 0, 1)
-        widen_v(1, 0, 2)
-        widen_v(1, 1, 3)
-        widen(1, 1, 2)
-        far_turn(0, 0, 0)
-        widen_v(0, 0, 0)
-        far_turn(0, 1, 1)
-        widen(0, 0, 1)
-        widen_v(0, 1, 0)
-        widen(0, 0, 2)
-        far_turn(0, 1, 0)
-        widen_v(0, 0, 3)
-        widen_v(0, 1, 2)
-        widen_v(1, 0, 0)
-        path_il(0, 0)
-        widen(1, 0, 1)
-        widen(1, 1, 0)
-        path_il(1, 0)
-        widen(1, 1, 1)
-        far_copy(0, 0, 1)
-        path_q(0, 0)
-        far_copy(0, 0, 0)
-        far_turn(1, 1, 0)
-        far_turn(1, 1, 1)
-        far_copy(0, 1, 1)
-        far_turn(1, 0, 1)
-        far_copy(0, 1, 0)
-        path_q(1, 0)
-        far_copy(1, 1, 0)
-        far_q(0, 1)
-        far_turn(1, 0, 0)
-        far_copy(1, 1, 1)
-        far_q(0, 0)
-        echo_mm(0, 0, 0)
-        echo_mm(0, 0, 2)
-        far_copy(1, 0, 1)
-        far_copy(1, 0, 0)
-        mic_scale(0, 0, 0)
-        widen(0, 1, 3)
-        far_turn(3, 0, 1)
-        path_il(1, 1)
-        far_q2(1)
-        widen(0, 1, 1)
-        path_q(1, 1)
-        far_turn(3, 0, 0)
-        far_turn(2, 1, 1)
-        err(0, 0, 0)
-        echo_mm(1, 0, 1)
-        mic_scale(0, 0, 2)
-        err(0, 0, 2)
-        mic_scale_g(1, 0, 1)
-        mic_scale_g(0, 0, 1)
-        err(1, 0, 1)
-        far_copy(3, 0, 1)
-        echo_mm(0, 0, 1)
-        err(0, 0, 1)
-        mic_scale_g(0, 0, 3)
-        echo_mm(0, 0, 3)
-        err(0, 0, 3)
-        prep_gains()
-        echo_mm(1, 0, 0)
-        far_copy(3, 0, 0)
-        path_il_s(0, 1)
-        far_turn(3, 1, 1)
-        err_il(0, 0, 0, 256)
-        far_copy(2, 1, 1)
-        far_turn(3, 1, 0)
-        mic_scale_g(1, 0, 2)
-        mic_scale_g(1, 0, 0)
-        mic_scale_g(1, 1, 2)
-        echo_mm(1, 0, 2)
-        err(1, 0, 0)
-        echo_mm(1, 0, 3)
-        far_turn(2, 1, 0)
-        far_copy(3, 1, 1)
-        far_copy(3, 1, 0)
-        mic_scale_g(1, 0, 3)
-        path_q(0, 1)
-        far_turn(2, 0, 1)
-        err(1, 0, 2)
-        far_q2(3)
-        mic_scale_g(3, 0, 0)
-        err_il_s(0, 0, 256, 512)
-        far_turn(2, 0, 0)
-        echo_mm(1, 1, 2)
-        mic_scale(3, 0, 1)
-        err(1, 0, 3)
-        far_copy(2, 0, 0)
-        far_copy(2, 0, 1)
-        far_copy(2, 1, 0)
-        err_q(0, 0, 0, 512)
-        comp_mm(0, 0)
-        comp_copy(0, 0)
-        echo_mm(1, 1, 1)
-        err(1, 1, 2)
-        mic_scale(3, 0, 3)
-        err_il(1, 0, 0, 256)
-        mic_scale_g(1, 1, 1)
-        mic_scale_g(3, 0, 2)
-        mic_scale_g(1, 1, 3)
-        echo_mm(3, 0, 0)
-        err(1, 1, 1)
-        comp_mm(1, 0)
-        comp_copy(1, 0)
-        echo_mm(1, 1, 0)
-        comp_mm(1, 1)
-        err(3, 0, 0)
-        mic_scale(1, 1, 0)
-        echo_mm(3, 0, 3)
-        comp_copy(1, 1)
-        err_il_s(1, 0, 256, 512)
-        echo_mm(1, 1, 3)
-        mic_scale_g(2, 0, 2)
-        far_q2(2)
-        comp_mm(0, 1)
-        comp_copy(0, 1)
-        mic_scale_g(2, 0, 0)
-        err(1, 1, 0)
-        comp_mm(0, 2)
-        comp_copy(0, 2)
-        mic_scale_g(0, 1, 1)
-        echo_mm(2, 0, 2)
-        err(3, 0, 3)
-        err(1, 1, 3)
-        err_q(1, 0, 0, 512)
-        echo_mm(3, 0, 2)
-        mic_scale(2, 0, 1)
-        mic_scale(0, 1, 3)
-        comp_mm(0, 3)
-        comp_copy(0, 3)
-        mic_scale_g(2, 0, 3)
-        echo_mm(3, 0, 1)
-        err(2, 0, 2)
-        comp_mm(1, 2)
-        comp_copy(1, 2)
-        echo_mm(2, 0, 1)
-        err_il_s(1, 1, 256, 512)
-        err_il(1, 1, 0, 256)
-        echo_mm(2, 0, 0)
-        comp_mm(2, 0)
-        err(3, 0, 2)
-        err(3, 0, 1)
-        mic_scale_g(3, 1, 2)
-        comp_mm(1, 3)
-        comp_q(0)
-        err(2, 0, 1)
-        comp_copy(2, 0)
-        echo_mm(2, 0, 3)
-        echo_mm(0, 1, 1)
-        mic_scale_g(0, 1, 2)
-        comp_copy(1, 3)
-        comp_mm(2, 1)
-        err_il(3, 0, 0, 256)
-        err(2, 0, 0)
-        err_il_s(3, 0, 256, 512)
-        echo_mm(0, 1, 2)
-        mic_scale_g(2, 1, 2)
-        err(2, 0, 3)
-        comp_copy(2, 1)
-        comp_mm(3, 0)
-        err_q(1, 1, 0, 512)
-        mic_scale_g(2, 1, 0)
-        err_il_s(2, 0, 256, 512)
-        echo_mm(3, 1, 2)
-        comp_copy(3, 0)
-        echo_mm(0, 1, 3)
-        err(0, 1, 1)
-        comp_q(1)
-        comp_mm(3, 1)
-        err(0, 1, 2)
-        err_il(2, 0, 0, 256)
-        mic_scale_g(3, 1, 0)
-        echo_mm(0, 1, 0)
-        mic_scale(0, 1, 0)
-        comp_copy(3, 1)
-        mic_scale(2, 1, 1)
-        comp_mm(3, 2)
-        comp_copy(3, 2)
-        err(3, 1, 2)
-        echo_mm(2, 1, 0)
-        err(0, 1, 3)
-        err(0, 1, 0)
-        comp_mm(3, 3)
-        comp_copy(3, 3)
-        echo_mm(2, 1, 3)
-        comp_mm(2, 2)
-        err_q(2, 0, 0, 512)
-        err(2, 1, 0)
-        mic_scale(2, 1, 3)
-        echo_mm(2, 1, 2)
-        comp_mm(2, 3)
-        comp_copy(2, 2)
-        err_q(3, 0, 0, 512)
-        comp_q(3)
-        echo_mm(2, 1, 1)
-        err(2, 1, 3)
-        comp_copy(2, 3)
-        err(2, 1, 2)
-        err_il_s(0, 1, 384, 512)
-        echo_mm(3, 1, 0)
-        echo_mm(3, 1, 1)
-        err(2, 1, 1)
-        echo_mm(3, 1, 3)
-        comp_q(2)
-        grad0(2)
-        err_il_s(2, 1, 256, 512)
-        mic_scale(3, 1, 1)
-        err_il(0, 1, 0, 384)
-        err(3, 1, 0)
-        err_il(2, 1, 0, 256)
-        err_q(0, 1, 0, 512)
-        out_s(0, 2)
-        err(3, 1, 1)
-        grad0(0)
-        out_s(0, 0)
-        grad0(1)
-        grad0(3)
-        err_q(2, 1, 0, 512)
-        grad1(1)
-        grad1(3)
-        out_s(0, 1)
-        grad1(0)
-        mic_scale_g(3, 1, 3)
-        err(3, 1, 3)
-        err_il_s(3, 1, 352, 512)
-        err_il(3, 1, 0, 352)
-        err_q(3, 1, 0, 512)
-        out_s(0, 3)
-        grad2(0)
-        out_s(1, 0)
-        grad2(1)
-        out_v_(1, 1)
-        grad2(3)
-        out_v_(1, 3)
-        grad1(2)
-        grad2(2)
-        out_s(1, 2)
+        load_basis_words()
+        load_path(1, 0)
+        for q in range(4):
+            load_basis_scales(q)
+        load_path(1, 1)
+        units = [(g, h) for h in range(NH) for g in range(NG)]
+        for g in range(1, NG):
+            load_far(g, 0, 2)
+            load_far(g, 2, 4)
+            if g == 1:
+                nc.sync.dma_start(out=step_bf[:], in_=step.rearrange("(g p j) -> p g j", p=P, j=PACK))
+            load_mic(g - 1, 0)
+        for g, h in units[NG - 1 :]:
+            load_mic(g, h)
+        nc.sync.dma_start(out=gain_bf[:], in_=gain.rearrange("(q m) -> q m", m=PACK))
+        nc.gpsimd.tensor_scalar(out=negstep[:], in0=step_bf[:], scalar1=-1.0, scalar2=0.0, op0=ALU.mult, op1=ALU.add)
+
+        def turn_group(g):
+            for j in range(PACK):
+                far_turn(g, j)
+                far_copy(g, j)
+
+        def comp_group(g):
+            for chunk in range(PACK):
+                for j in range(PACK):
+                    comp_mm(g, chunk, j, side, "side_bank")
+                comp_copy(g, chunk)
+
+        def widen_pass(engine, k, h):
+            for t in range(PACK):
+                path_widen(engine, k, h, t)
+
+        turn_group(0)
+        widen_pass("vector", 0, 0)
+        widen_pass("scalar", 0, 1)
+        path_interleave("vector", 0, 0)
+        far_quantise(0, 0, 2)
+        path_quantise(0, 0)
+        path_widen("vector", 1, 0, 0)
+        path_widen("vector", 1, 0, 1)
+        far_quantise(0, 2, 4)
+        path_widen("vector", 1, 0, 2)
+        path_widen("vector", 1, 0, 3)
+        comp_group(0)
+        turn_group(1)
+        path_interleave("vector", 1, 0)
+        path_interleave("vector", 0, 1)
+        path_quantise(1, 0)
+        for j in range(PACK):
+            mic_scale("vector", 0, 0, j)
+        path_quantise(0, 1)
+
+        def echo_round(r):
+            g, h = units[r]
+            for j in range(PACK):
+                echo_mm(g, h, j)
+                err(g, h, j)
+                if r + 1 < len(units) and j < POOL_ROWS:
+                    mic_scale("gpsimd", *units[r + 1], j)
+
+        def rest_of_mic(r, engine="vector"):
+            for j in range(POOL_ROWS, PACK):
+                mic_scale(engine, *units[r + 1], j)
+
+        echo_round(0)
+        widen_pass("scalar", 1, 1)
+        far_quantise(1, 0, 2)
+        far_quantise(1, 2, 4)
+        turn_group(2)
+        rest_of_mic(0)
+        comp_quantise(0)
+
+        echo_round(1)
+        err_interleave("scalar", *units[0])
+        far_quantise(2, 0, 2)
+        far_quantise(2, 2, 4)
+        turn_group(3)
+        rest_of_mic(1)
+        err_quantise(*units[0])
+
+        echo_round(2)
+        err_interleave("scalar", *units[1])
+        far_quantise(3, 0, 2)
+        far_quantise(3, 2, 4)
+        comp_group(1)
+        rest_of_mic(2)
+        path_interleave("vector", 1, 1)
+
+        echo_round(3)
+        err_interleave("scalar", *units[2])
+        comp_group(2)
+        path_quantise(1, 1)
+        rest_of_mic(3)
+        err_quantise(*units[1])
+        comp_quantise(1)
+        nc.gpsimd.tensor_copy(out=gains[:], in_=gain_bf[:])
+
+        echo_round(4)
+        err_interleave("scalar", *units[3])
+        comp_group(3)
+        rest_of_mic(4)
+        err_quantise(*units[2])
+        comp_quantise(2)
+
+        echo_round(5)
+        err_interleave("scalar", *units[4])
+        for m in range(PACK):
+            grad_mm(0, m, range(NG // 2))
+        rest_of_mic(5, "scalar")
+        err_quantise(*units[3])
+        comp_quantise(3)
+        err_quantise(*units[4])
+
+        echo_round(6)
+        err_interleave("scalar", *units[5])
+        rest_of_mic(6, "scalar")
+        for m in range(PACK):
+            grad_mm(0, m, range(NG // 2, NG))
+            grad_out("scalar", 0, m)
+        err_interleave("vector", *units[6], 0, TAIL)
+        err_interleave("scalar", *units[6], TAIL, WIDTH[1])
+        err_quantise(*units[5])
+
+        echo_round(7)
+        err_interleave("vector", *units[7], 0, TAIL)
+        err_interleave("scalar", *units[7], TAIL, WIDTH[1])
+        err_quantise(*units[6])
+        for c in range(2):
+            err_quantise(*units[7], c * TAIL, (c + 1) * TAIL)
+        for g in range(NG - 2):
+            for c in range(2):
+                for pair in range(2):
+                    tail_mm(c, pair, g)
+        for c in range(2):
+            for pair in range(2):
+                for g in range(NG - 2, NG):
+                    tail_mm(c, pair, g)
+                tail_out("scalar" if pair == 0 else "vector", c, pair)

@@ -23,8 +23,7 @@ PASS = P * PACK
 NG = T // PASS
 NK = K // PASS
 WIDTH = [512, 512]
-MS_BUFS = 1
-POOL_ROWS = 2
+POOL_ROWS = 3
 TAIL = 256
 NH = len(WIDTH)
 COLS = [slice(sum(WIDTH[:h]), sum(WIDTH[: h + 1])) for h in range(NH)]
@@ -45,7 +44,6 @@ def tile_echo_nlms_gradient_s11_kernel(
         pscale = keep.tile([P, NK, PACK], F32, name="pscale")
         step_bf = keep.tile([P, NG, PACK], BF16, name="step_bf")
         gain_bf = keep.tile([P, PACK], BF16, name="gain_bf")
-        negstep = keep.tile([P, NG, PACK], F32, name="negstep")
         gains = keep.tile([P, PACK], F32, name="gains")
         bscale = keep.tile([P, NK, R], U8, name="bscale", align_bytes=64)
         bwords = keep.tile([P, NK, 2 * R], U8, name="bwords", align_bytes=64)
@@ -56,6 +54,12 @@ def tile_echo_nlms_gradient_s11_kernel(
         out_q = out.rearrange("(q m) c -> q m c", m=PACK)
 
         far_t, mic_t, pbytes = {}, {}, {}
+        zeros = keep.tile([P, PASS], BF16, name="zeros")
+
+        def warm_tensor(count):
+            bank = echo.tile([P, PASS], F32, name="echo_bank")
+            for i in range(count):
+                nc.tensor.matmul(bank[:], lhsT=zeros[:, :P], rhs=zeros[:], start=(i == 0), stop=(i == count - 1))
 
         def load_far(g, lo, hi):
             rows = keep.tile([P, hi - lo, K], BF16, name=f"far{g}_{lo}")
@@ -68,8 +72,8 @@ def tile_echo_nlms_gradient_s11_kernel(
             nc.sync.dma_start(out=mic_t[g, h][:], in_=mic_v[g][:, :, COLS[h]])
 
         def load_path(k, h):
-            pbytes[k, h] = keep.tile([P, 2, C], U8, name=f"pbytes{k}_{h}", align_bytes=64)
-            nc.sync.dma_start(out=pbytes[k, h][:], in_=path_v[k][:, 2 * h : 2 * h + 2, :])
+            pbytes[k, h] = keep.tile([P, PACK, WIDTH[h]], U8, name=f"pbytes{k}_{h}", align_bytes=64)
+            nc.sync.dma_start(out=pbytes[k, h][:], in_=path_v[k][:, :, COLS[h]])
 
         def load_basis_words():
             nc.sync.dma_start(out=bwords[:], in_=basis_words.rearrange("g p n -> p g n"))
@@ -104,8 +108,8 @@ def tile_echo_nlms_gradient_s11_kernel(
 
         def path_widen(engine, k, h, t):
             if (k, h) not in p_rows:
-                p_rows[k, h] = work.tile([P, PACK, WIDTH[h]], BF16, name="p_rows", bufs=3)
-            dst, src, scale = p_rows[k, h][:, t, :], pbytes[k, t // 2][:, t % 2, COLS[h]].bitcast(FP8), pscale[:, k, t : t + 1]
+                p_rows[k, h] = work.tile([P, PACK, WIDTH[h]], BF16, name="p_rows")
+            dst, src, scale = p_rows[k, h][:, t, :], pbytes[k, h][:, t, :].bitcast(FP8), pscale[:, k, t : t + 1]
             if engine == "vector":
                 nc.vector.tensor_scalar(out=dst, in0=src, scalar1=scale, scalar2=None, op0=ALU.mult)
             else:
@@ -170,9 +174,15 @@ def tile_echo_nlms_gradient_s11_kernel(
 
         mic_scaled, e_rows, e_grouped, echo_bank = {}, {}, {}, {}
 
+        negstep = {}
+
+        def negate_step(g, h):
+            negstep[g, h] = keep.tile([P, PACK], F32, name=f"negstep{g}_{h}")
+            nc.vector.tensor_scalar(out=negstep[g, h][:], in0=step_bf[:, g, :], scalar1=-1.0, scalar2=None, op0=ALU.mult)
+
         def mic_scale(engine, g, h, j):
-            mic_scaled[g, h, j] = work.tile([P, WIDTH[h]], F32, name=f"mic_scaled{j}", bufs=MS_BUFS)
-            dst, src, scale = mic_scaled[g, h, j][:], mic_t[g, h][:, j, :], negstep[:, g, j : j + 1]
+            mic_scaled[g, h, j] = work.tile([P, WIDTH[h]], F32, name=f"mic_scaled{j}", bufs=2 if j < POOL_ROWS else 1)
+            dst, src, scale = mic_scaled[g, h, j][:], mic_t[g, h][:, j, :], negstep[g, h][:, j : j + 1]
             if engine == "vector":
                 nc.vector.tensor_scalar(out=dst, in0=src, scalar1=scale, scalar2=None, op0=ALU.mult)
             elif engine == "gpsimd":
@@ -200,7 +210,7 @@ def tile_echo_nlms_gradient_s11_kernel(
             nc.vector.scalar_tensor_tensor(
                 out=e_rows[g, h][:, j, :],
                 in0=echo_bank[g, h, j][:],
-                scalar=negstep[:, g, j : j + 1],
+                scalar=negstep[g, h][:, j : j + 1],
                 in1=mic_scaled[g, h, j][:],
                 op0=ALU.mult,
                 op1=ALU.subtract,
@@ -268,29 +278,30 @@ def tile_echo_nlms_gradient_s11_kernel(
             nc.sync.dma_start(out=out_v[m][:, COLS[h]], in_=res[:])
 
         nc.vector.memset(bscale[:].rearrange("p g n -> p (g n)").bitcast(I32), 0)
+        nc.vector.memset(zeros[:], 0.0)
         make_identity(nc, ident[:])
         nc.scalar.dma_start(out=pscale[:], in_=path_scale.rearrange("(g p t) o -> p g (t o)", p=P, t=PACK))
         load_path(0, 0)
         load_far(0, 0, 1)
-        load_path(0, 1)
         load_far(0, 1, 2)
         load_far(0, 2, 4)
         load_basis_words()
         load_path(1, 0)
+        load_far(1, 0, 2)
         for q in range(4):
             load_basis_scales(q)
-        load_path(1, 1)
+        load_far(1, 2, 4)
+        nc.sync.dma_start(out=step_bf[:], in_=step.rearrange("(g p j) -> p g j", p=P, j=PACK))
         units = [(g, h) for h in range(NH) for g in range(NG)]
-        for g in range(1, NG):
-            load_far(g, 0, 2)
-            load_far(g, 2, 4)
-            if g == 1:
-                nc.sync.dma_start(out=step_bf[:], in_=step.rearrange("(g p j) -> p g j", p=P, j=PACK))
+        load_mic(0, 0)
+        for g in range(2, NG):
             load_mic(g - 1, 0)
+            load_far(g, 0, 2)
+            load_path(g - 2, 1)
+            load_far(g, 2, 4)
         for g, h in units[NG - 1 :]:
             load_mic(g, h)
         nc.sync.dma_start(out=gain_bf[:], in_=gain.rearrange("(q m) -> q m", m=PACK))
-        nc.gpsimd.tensor_scalar(out=negstep[:], in0=step_bf[:], scalar1=-1.0, scalar2=0.0, op0=ALU.mult, op1=ALU.add)
 
         def turn_group(g):
             for j in range(PACK):
@@ -307,25 +318,36 @@ def tile_echo_nlms_gradient_s11_kernel(
             for t in range(PACK):
                 path_widen(engine, k, h, t)
 
-        turn_group(0)
+        warm_tensor(4)
+        for j in range(PACK):
+            far_turn(0, j)
+            far_copy(0, j)
+            if j == 1:
+                warm_tensor(2)
         widen_pass("vector", 0, 0)
-        widen_pass("scalar", 0, 1)
         path_interleave("vector", 0, 0)
-        far_quantise(0, 0, 2)
+        far_quantise(0, 0, 1)
         path_quantise(0, 0)
+        far_quantise(0, 1, 2)
         path_widen("vector", 1, 0, 0)
+        path_widen("scalar", 1, 0, 2)
+        path_widen("scalar", 1, 0, 3)
+        far_quantise(0, 2, 3)
         path_widen("vector", 1, 0, 1)
-        far_quantise(0, 2, 4)
-        path_widen("vector", 1, 0, 2)
-        path_widen("vector", 1, 0, 3)
-        comp_group(0)
+        far_quantise(0, 3, 4)
+        for j in range(PACK):
+            for chunk in range(PACK):
+                comp_mm(0, chunk, j, echo, "echo_bank")
+        for chunk in range(PACK):
+            comp_copy(0, chunk)
         turn_group(1)
         path_interleave("vector", 1, 0)
-        path_interleave("vector", 0, 1)
+        negate_step(0, 0)
         path_quantise(1, 0)
         for j in range(PACK):
+            if j == PACK - 1:
+                negate_step(*units[1])
             mic_scale("vector", 0, 0, j)
-        path_quantise(0, 1)
 
         def echo_round(r):
             g, h = units[r]
@@ -340,60 +362,69 @@ def tile_echo_nlms_gradient_s11_kernel(
                 mic_scale(engine, *units[r + 1], j)
 
         echo_round(0)
-        widen_pass("scalar", 1, 1)
+        widen_pass("scalar", 0, 1)
         far_quantise(1, 0, 2)
         far_quantise(1, 2, 4)
         turn_group(2)
         rest_of_mic(0)
+        negate_step(*units[2])
         comp_quantise(0)
 
         echo_round(1)
-        err_interleave("scalar", *units[0])
+        widen_pass("scalar", 1, 1)
         far_quantise(2, 0, 2)
         far_quantise(2, 2, 4)
         turn_group(3)
         rest_of_mic(1)
-        err_quantise(*units[0])
+        negate_step(*units[3])
+        path_interleave("vector", 0, 1)
 
         echo_round(2)
-        err_interleave("scalar", *units[1])
+        err_interleave("scalar", *units[0])
         far_quantise(3, 0, 2)
         far_quantise(3, 2, 4)
         comp_group(1)
+        path_quantise(0, 1)
         rest_of_mic(2)
+        negate_step(*units[4])
         path_interleave("vector", 1, 1)
 
         echo_round(3)
-        err_interleave("scalar", *units[2])
+        err_interleave("scalar", *units[1])
         comp_group(2)
         path_quantise(1, 1)
         rest_of_mic(3)
-        err_quantise(*units[1])
+        err_quantise(*units[0])
+        negate_step(*units[5])
         comp_quantise(1)
-        nc.gpsimd.tensor_copy(out=gains[:], in_=gain_bf[:])
 
         echo_round(4)
-        err_interleave("scalar", *units[3])
+        err_interleave("scalar", *units[2])
         comp_group(3)
         rest_of_mic(4)
-        err_quantise(*units[2])
+        err_quantise(*units[1])
+        negate_step(*units[6])
         comp_quantise(2)
 
+        nc.scalar.copy(out=gains[:], in_=gain_bf[:])
         echo_round(5)
-        err_interleave("scalar", *units[4])
+        err_interleave("scalar", *units[3])
         for m in range(PACK):
             grad_mm(0, m, range(NG // 2))
-        rest_of_mic(5, "scalar")
-        err_quantise(*units[3])
+        err_interleave("scalar", *units[4])
+        err_quantise(*units[2])
         comp_quantise(3)
-        err_quantise(*units[4])
+        rest_of_mic(5)
+        negate_step(*units[7])
+        err_quantise(*units[3])
 
         echo_round(6)
         err_interleave("scalar", *units[5])
-        rest_of_mic(6, "scalar")
         for m in range(PACK):
             grad_mm(0, m, range(NG // 2, NG))
             grad_out("scalar", 0, m)
+        rest_of_mic(6)
+        err_quantise(*units[4])
         err_interleave("vector", *units[6], 0, TAIL)
         err_interleave("scalar", *units[6], TAIL, WIDTH[1])
         err_quantise(*units[5])

@@ -53,7 +53,7 @@ def tile_echo_nlms_gradient_s11_kernel(
         out_v = out.rearrange("(q m) c -> m q c", m=PACK)
         out_q = out.rearrange("(q m) c -> q m c", m=PACK)
 
-        far_t, mic_t, pbytes = {}, {}, {}
+        far_t, far_pair, far_sorted, mic_t, pbytes = {}, {}, {}, {}, {}
         zeros = keep.tile([P, PASS], BF16, name="zeros")
 
         def warm_tensor(count):
@@ -63,6 +63,7 @@ def tile_echo_nlms_gradient_s11_kernel(
 
         def load_far(g, lo, hi):
             rows = keep.tile([P, hi - lo, K], BF16, name=f"far{g}_{lo}")
+            far_pair[g, lo] = rows
             nc.sync.dma_start(out=rows[:], in_=far_v[g][:, lo:hi, :])
             for j in range(lo, hi):
                 far_t[g, j] = rows[:, j - lo, :]
@@ -79,7 +80,7 @@ def tile_echo_nlms_gradient_s11_kernel(
             nc.sync.dma_start(out=bwords[:], in_=basis_words.rearrange("g p n -> p g n"))
 
         def load_basis_scales(q):
-            nc.scalar.dma_start(
+            nc.sync.dma_start(
                 out=bscale[32 * q : 32 * q + 4, :, :].bitcast(I32),
                 in_=basis_scales[:, 4 * q : 4 * q + 4, :].bitcast(I32).rearrange("g q n -> q g n"),
             )
@@ -125,12 +126,24 @@ def tile_echo_nlms_gradient_s11_kernel(
 
         x_grouped, side_bank = {}, {}
 
+        def far_sort(engine, g, lo):
+            far_sorted[g, lo] = work.tile([P, 2 * NK, 2, P], F32, name="far_sorted")
+            src = far_pair[g, lo][:].rearrange("p j k -> p (j k)").bitcast(F32).rearrange("p (a n u) -> p a u n", u=2, n=P)
+            if engine == "vector":
+                nc.vector.tensor_copy(out=far_sorted[g, lo][:], in_=src)
+            else:
+                nc.scalar.copy(out=far_sorted[g, lo][:], in_=src)
+
         def far_turn(g, j):
             words = far_t[g, j].bitcast(F32)
             bank = side.tile([P, NK, 2, P], F32, name="side_bank")
             for k in range(NK):
                 for u in range(2):
-                    nc.tensor.transpose(bank[:, k, u, :], words[:, 256 * k + u : 256 * (k + 1) : 2], ident[:])
+                    if (g, j - j % 2) in far_sorted:
+                        src = far_sorted[g, j - j % 2][:, NK * (j % 2) + k, u, :]
+                    else:
+                        src = words[:, 256 * k + u : 256 * (k + 1) : 2]
+                    nc.tensor.transpose(bank[:, k, u, :], src, ident[:])
             side_bank["far", g, j] = bank
 
         def far_copy(g, j):
@@ -258,7 +271,7 @@ def tile_echo_nlms_gradient_s11_kernel(
                 )
 
         def tail_out(engine, c, pair):
-            res = work.tile([P, 2, TAIL], F32, name="res", bufs=4)
+            res = work.tile([P, 2, TAIL], F32, name="res", bufs=3)
             for i in range(2):
                 src, scale = side_bank["tail", c, pair][:, i, :], gains[:, 2 * pair + i : 2 * pair + i + 1]
                 if engine == "vector":
@@ -269,7 +282,7 @@ def tile_echo_nlms_gradient_s11_kernel(
             nc.sync.dma_start(out=out_q[:, 2 * pair : 2 * pair + 2, first : first + TAIL], in_=res[:])
 
         def grad_out(engine, h, m):
-            res = work.tile([P, WIDTH[h]], F32, name="res", bufs=4)
+            res = work.tile([P, WIDTH[h]], F32, name="res", bufs=3)
             bank, scale = side_bank["grad", h, m], gains[:, m : m + 1]
             if engine == "vector":
                 nc.vector.tensor_scalar(out=res[:], in0=bank[:], scalar1=scale, scalar2=None, op0=ALU.mult)
@@ -281,15 +294,17 @@ def tile_echo_nlms_gradient_s11_kernel(
         nc.vector.memset(zeros[:], 0.0)
         make_identity(nc, ident[:])
         nc.scalar.dma_start(out=pscale[:], in_=path_scale.rearrange("(g p t) o -> p g (t o)", p=P, t=PACK))
+        warm_column = keep.tile([P, 1], F32, name="warm_column")
+        nc.scalar.activation(out=warm_column[:], in_=zeros[:, :1], func=COPY, scale=1.0)
         load_path(0, 0)
         load_far(0, 0, 1)
+        for q in range(4):
+            load_basis_scales(q)
         load_far(0, 1, 2)
         load_far(0, 2, 4)
         load_basis_words()
         load_path(1, 0)
         load_far(1, 0, 2)
-        for q in range(4):
-            load_basis_scales(q)
         load_far(1, 2, 4)
         nc.sync.dma_start(out=step_bf[:], in_=step.rearrange("(g p j) -> p g j", p=P, j=PACK))
         units = [(g, h) for h in range(NH) for g in range(NG)]
@@ -297,8 +312,9 @@ def tile_echo_nlms_gradient_s11_kernel(
         for g in range(2, NG):
             load_mic(g - 1, 0)
             load_far(g, 0, 2)
-            load_path(g - 2, 1)
             load_far(g, 2, 4)
+        for k in range(NK):
+            load_path(k, 1)
         for g, h in units[NG - 1 :]:
             load_mic(g, h)
         nc.sync.dma_start(out=gain_bf[:], in_=gain.rearrange("(q m) -> q m", m=PACK))
@@ -330,11 +346,13 @@ def tile_echo_nlms_gradient_s11_kernel(
         path_quantise(0, 0)
         far_quantise(0, 1, 2)
         path_widen("vector", 1, 0, 0)
-        path_widen("scalar", 1, 0, 2)
-        path_widen("scalar", 1, 0, 3)
         far_quantise(0, 2, 3)
         path_widen("vector", 1, 0, 1)
         far_quantise(0, 3, 4)
+        path_widen("vector", 1, 0, 2)
+        path_widen("vector", 1, 0, 3)
+        far_sort("scalar", 1, 0)
+        far_sort("scalar", 1, 2)
         for j in range(PACK):
             for chunk in range(PACK):
                 comp_mm(0, chunk, j, echo, "echo_bank")
@@ -362,7 +380,6 @@ def tile_echo_nlms_gradient_s11_kernel(
                 mic_scale(engine, *units[r + 1], j)
 
         echo_round(0)
-        widen_pass("scalar", 0, 1)
         far_quantise(1, 0, 2)
         far_quantise(1, 2, 4)
         turn_group(2)
@@ -371,36 +388,41 @@ def tile_echo_nlms_gradient_s11_kernel(
         comp_quantise(0)
 
         echo_round(1)
-        widen_pass("scalar", 1, 1)
+        far_sort("scalar", 3, 0)
+        far_sort("scalar", 3, 2)
         far_quantise(2, 0, 2)
         far_quantise(2, 2, 4)
         turn_group(3)
         rest_of_mic(1)
-        negate_step(*units[3])
-        path_interleave("vector", 0, 1)
+        for t in range(PACK):
+            if t == PACK - 2:
+                negate_step(*units[3])
+            path_widen("vector", 0, 1, t)
 
         echo_round(2)
-        err_interleave("scalar", *units[0])
+        widen_pass("scalar", 1, 1)
         far_quantise(3, 0, 2)
         far_quantise(3, 2, 4)
         comp_group(1)
-        path_quantise(0, 1)
-        rest_of_mic(2)
+        path_interleave("vector", 0, 1)
         negate_step(*units[4])
         path_interleave("vector", 1, 1)
+        rest_of_mic(2, "scalar")
 
         echo_round(3)
-        err_interleave("scalar", *units[1])
+        err_interleave("scalar", *units[0])
         comp_group(2)
+        path_quantise(0, 1)
         path_quantise(1, 1)
         rest_of_mic(3)
-        err_quantise(*units[0])
-        negate_step(*units[5])
         comp_quantise(1)
+        negate_step(*units[5])
+        err_quantise(*units[0])
 
         echo_round(4)
-        err_interleave("scalar", *units[2])
+        err_interleave("scalar", *units[1])
         comp_group(3)
+        err_interleave("vector", *units[2])
         rest_of_mic(4)
         err_quantise(*units[1])
         negate_step(*units[6])

@@ -51,7 +51,6 @@ def tile_echo_nlms_gradient_s11_kernel(
         mic_v = mic.rearrange("(g p j) c -> g p j c", p=P, j=PACK)
         path_v = path_bytes.rearrange("(g p t) c -> g p t c", p=P, t=PACK)
         out_v = out.rearrange("(q m) c -> m q c", m=PACK)
-        out_q = out.rearrange("(q m) c -> q m c", m=PACK)
 
         far_t, far_pair, far_sorted, mic_t, pbytes = {}, {}, {}, {}, {}
         zeros = keep.tile([P, PASS], BF16, name="zeros")
@@ -160,23 +159,24 @@ def tile_echo_nlms_gradient_s11_kernel(
 
         u_grouped = {}
 
-        def comp_mm(g, chunk, j, pool, name):
-            if ("u", g, chunk) not in side_bank:
-                side_bank["u", g, chunk] = pool.tile([P, PACK, P], F32, name=name)
+        def comp_mm(g, j, pool, name):
             for k in range(NK):
-                nc.tensor.matmul_mx(
-                    out=side_bank["u", g, chunk][:, j, :],
-                    lhsT=x_codes[g][:, j, k, :].bitcast(FP8X4),
-                    lhsT_scale=x_scales[g][:, j, k, :],
-                    rhs=bwords[:, k, 2 * chunk * P : 2 * (chunk + 1) * P].bitcast(FP4X4),
-                    rhs_scale=bscale[:, k, chunk * P : (chunk + 1) * P],
-                    start=(k == 0),
-                    stop=(k == NK - 1),
-                )
+                for chunk in range(PACK):
+                    if ("u", g, chunk) not in side_bank:
+                        side_bank["u", g, chunk] = pool.tile([P, PACK, P], F32, name=name)
+                    nc.tensor.matmul_mx(
+                        out=side_bank["u", g, chunk][:, j, :],
+                        lhsT=x_codes[g][:, j, k, :].bitcast(FP8X4),
+                        lhsT_scale=x_scales[g][:, j, k, :],
+                        rhs=bwords[:, k, 2 * chunk * P : 2 * (chunk + 1) * P].bitcast(FP4X4),
+                        rhs_scale=bscale[:, k, chunk * P : (chunk + 1) * P],
+                        start=(k == 0),
+                        stop=(k == NK - 1),
+                    )
 
         def comp_copy(g, chunk):
             if g not in u_grouped:
-                u_grouped[g] = work.tile([P, PACK, P, PACK], BF16, name="u_grouped", align_bytes=64, bufs=3)
+                u_grouped[g] = work.tile([P, PACK, P, PACK], BF16, name="u_grouped", align_bytes=64)
             nc.scalar.copy(
                 out=u_grouped[g][:, :, 32 * chunk : 32 * (chunk + 1), :],
                 in_=side_bank["u", g, chunk][:].rearrange("p j (q m) -> p m q j", m=PACK),
@@ -194,7 +194,7 @@ def tile_echo_nlms_gradient_s11_kernel(
             nc.vector.tensor_scalar(out=negstep[g, h][:], in0=step_bf[:, g, :], scalar1=-1.0, scalar2=None, op0=ALU.mult)
 
         def mic_scale(engine, g, h, j):
-            mic_scaled[g, h, j] = work.tile([P, WIDTH[h]], F32, name=f"mic_scaled{j}", bufs=2 if j < POOL_ROWS else 1)
+            mic_scaled[g, h, j] = work.tile([P, WIDTH[h]], F32, name=f"mic_scaled{j}", bufs=2)
             dst, src, scale = mic_scaled[g, h, j][:], mic_t[g, h][:, j, :], negstep[g, h][:, j : j + 1]
             if engine == "vector":
                 nc.vector.tensor_scalar(out=dst, in0=src, scalar1=scale, scalar2=None, op0=ALU.mult)
@@ -203,28 +203,28 @@ def tile_echo_nlms_gradient_s11_kernel(
             else:
                 nc.scalar.activation(out=dst, in_=src, func=COPY, scale=scale)
 
-        def echo_mm(g, h, j):
-            bank = echo.tile([P, WIDTH[h]], F32, name="echo_bank")
+        def echo_mm(g, h, j, lo=0, hi=PASS):
+            bank = echo.tile([P, hi - lo], F32, name="echo_bank")
             for k in range(NK):
                 nc.tensor.matmul_mx(
                     out=bank[:],
                     lhsT=x_codes[g][:, j, k, :].bitcast(FP8X4),
                     lhsT_scale=x_scales[g][:, j, k, :],
-                    rhs=p_codes[k][h][:].bitcast(FP8X4),
-                    rhs_scale=p_scales[k][h][:],
+                    rhs=p_codes[k][h][:, lo:hi].bitcast(FP8X4),
+                    rhs_scale=p_scales[k][h][:, lo:hi],
                     start=(k == 0),
                     stop=(k == NK - 1),
                 )
             echo_bank[g, h, j] = bank
 
-        def err(g, h, j):
+        def err(g, h, j, lo=0, hi=PASS):
             if (g, h) not in e_rows:
                 e_rows[g, h] = work.tile([P, PACK, WIDTH[h]], BF16, name="e_rows", bufs=4)
             nc.vector.scalar_tensor_tensor(
-                out=e_rows[g, h][:, j, :],
+                out=e_rows[g, h][:, j, lo:hi],
                 in0=echo_bank[g, h, j][:],
                 scalar=negstep[g, h][:, j : j + 1],
-                in1=mic_scaled[g, h, j][:],
+                in1=mic_scaled[g, h, j][:, lo:hi],
                 op0=ALU.mult,
                 op1=ALU.subtract,
             )
@@ -255,34 +255,36 @@ def tile_echo_nlms_gradient_s11_kernel(
                     stop=(g == NG - 1),
                 )
 
-        def tail_mm(c, pair, g):
-            if ("tail", c, pair) not in side_bank:
-                side_bank["tail", c, pair] = side.tile([P, 2, TAIL], F32, name="side_bank")
-            for i in range(2):
-                m = 2 * pair + i
-                nc.tensor.matmul_mx(
-                    out=side_bank["tail", c, pair][:, i, :],
-                    lhsT=u_codes[g][:, m * P : (m + 1) * P].bitcast(FP8X4),
-                    lhsT_scale=u_scales[g][:, m * P : (m + 1) * P],
-                    rhs=e_codes[g][1][:, c * TAIL : (c + 1) * TAIL].bitcast(FP8X4),
-                    rhs_scale=e_scales[g][1][:, c * TAIL : (c + 1) * TAIL],
-                    start=(g == 0 and i == 0),
-                    stop=(g == NG - 1 and i == 1),
-                )
+        def tail_mm(c, m, g):
+            if ("tail", c, m) not in side_bank:
+                pool, name = (side, "side_bank") if c == 0 else (echo, "echo_bank")
+                side_bank["tail", c, m] = pool.tile([P, TAIL], F32, name=name)
+            nc.tensor.matmul_mx(
+                out=side_bank["tail", c, m][:],
+                lhsT=u_codes[g][:, m * P : (m + 1) * P].bitcast(FP8X4),
+                lhsT_scale=u_scales[g][:, m * P : (m + 1) * P],
+                rhs=e_codes[g][1][:, c * TAIL : (c + 1) * TAIL].bitcast(FP8X4),
+                rhs_scale=e_scales[g][1][:, c * TAIL : (c + 1) * TAIL],
+                start=(g == 0),
+                stop=(g == NG - 1),
+            )
 
-        def tail_out(engine, c, pair):
-            res = work.tile([P, 2, TAIL], F32, name="res", bufs=3)
-            for i in range(2):
-                src, scale = side_bank["tail", c, pair][:, i, :], gains[:, 2 * pair + i : 2 * pair + i + 1]
-                if engine == "vector":
-                    nc.vector.tensor_scalar(out=res[:, i, :], in0=src, scalar1=scale, scalar2=None, op0=ALU.mult)
-                else:
-                    nc.scalar.activation(out=res[:, i, :], in_=src, func=COPY, scale=scale)
+        tail_res = []
+
+        def tail_out(engine, c, m):
+            if not tail_res:
+                tail_res.append(work.tile([P, 2, PACK, TAIL], F32, name="x_grouped", align_bytes=64))
+            res = tail_res[0][:, c, m, :]
+            src, scale = side_bank["tail", c, m][:], gains[:, m : m + 1]
+            if engine == "vector":
+                nc.vector.tensor_scalar(out=res, in0=src, scalar1=scale, scalar2=None, op0=ALU.mult)
+            else:
+                nc.scalar.activation(out=res, in_=src, func=COPY, scale=scale)
             first = WIDTH[0] + c * TAIL
-            nc.sync.dma_start(out=out_q[:, 2 * pair : 2 * pair + 2, first : first + TAIL], in_=res[:])
+            nc.sync.dma_start(out=out_v[m][:, first : first + TAIL], in_=res)
 
         def grad_out(engine, h, m):
-            res = work.tile([P, WIDTH[h]], F32, name="res", bufs=3)
+            res = work.tile([P, WIDTH[h]], F32, name="res", bufs=4)
             bank, scale = side_bank["grad", h, m], gains[:, m : m + 1]
             if engine == "vector":
                 nc.vector.tensor_scalar(out=res[:], in0=bank[:], scalar1=scale, scalar2=None, op0=ALU.mult)
@@ -325,9 +327,11 @@ def tile_echo_nlms_gradient_s11_kernel(
                 far_copy(g, j)
 
         def comp_group(g):
+            for j in range(PACK):
+                comp_mm(g, j, side, "side_bank")
+
+        def comp_copies(g):
             for chunk in range(PACK):
-                for j in range(PACK):
-                    comp_mm(g, chunk, j, side, "side_bank")
                 comp_copy(g, chunk)
 
         def widen_pass(engine, k, h):
@@ -354,10 +358,8 @@ def tile_echo_nlms_gradient_s11_kernel(
         far_sort("scalar", 1, 0)
         far_sort("scalar", 1, 2)
         for j in range(PACK):
-            for chunk in range(PACK):
-                comp_mm(0, chunk, j, echo, "echo_bank")
-        for chunk in range(PACK):
-            comp_copy(0, chunk)
+            comp_mm(0, j, echo, "echo_bank")
+        comp_copies(0)
         turn_group(1)
         path_interleave("vector", 1, 0)
         negate_step(0, 0)
@@ -408,61 +410,67 @@ def tile_echo_nlms_gradient_s11_kernel(
         negate_step(*units[4])
         path_interleave("vector", 1, 1)
         rest_of_mic(2, "scalar")
+        err_interleave("scalar", *units[0])
 
         echo_round(3)
-        err_interleave("scalar", *units[0])
+        comp_copies(1)
         comp_group(2)
         path_quantise(0, 1)
         path_quantise(1, 1)
         rest_of_mic(3)
-        comp_quantise(1)
-        negate_step(*units[5])
         err_quantise(*units[0])
+        negate_step(*units[5])
+        comp_quantise(1)
+        err_interleave("scalar", *units[1])
 
         echo_round(4)
-        err_interleave("scalar", *units[1])
+        comp_copies(2)
         comp_group(3)
         err_interleave("vector", *units[2])
         rest_of_mic(4)
         err_quantise(*units[1])
         negate_step(*units[6])
         comp_quantise(2)
+        err_interleave("scalar", *units[3])
 
         nc.scalar.copy(out=gains[:], in_=gain_bf[:])
         echo_round(5)
-        err_interleave("scalar", *units[3])
+        comp_copies(3)
         for m in range(PACK):
             grad_mm(0, m, range(NG // 2))
         err_interleave("scalar", *units[4])
         err_quantise(*units[2])
-        comp_quantise(3)
         rest_of_mic(5)
-        negate_step(*units[7])
         err_quantise(*units[3])
+        negate_step(*units[7])
+        comp_quantise(3)
 
         echo_round(6)
         err_interleave("scalar", *units[5])
+        err_interleave("scalar", *units[6], TAIL, WIDTH[1])
         for m in range(PACK):
             grad_mm(0, m, range(NG // 2, NG))
             grad_out("scalar", 0, m)
         rest_of_mic(6)
         err_quantise(*units[4])
         err_interleave("vector", *units[6], 0, TAIL)
-        err_interleave("scalar", *units[6], TAIL, WIDTH[1])
         err_quantise(*units[5])
 
-        echo_round(7)
-        err_interleave("vector", *units[7], 0, TAIL)
-        err_interleave("scalar", *units[7], TAIL, WIDTH[1])
-        err_quantise(*units[6])
         for c in range(2):
-            err_quantise(*units[7], c * TAIL, (c + 1) * TAIL)
-        for g in range(NG - 2):
-            for c in range(2):
-                for pair in range(2):
-                    tail_mm(c, pair, g)
+            for j in range(PACK):
+                echo_mm(*units[7], j, c * TAIL, (c + 1) * TAIL)
+                err(*units[7], j, c * TAIL, (c + 1) * TAIL)
+            if c == 0:
+                err_interleave("scalar", *units[7], 0, TAIL)
+                err_quantise(*units[6])
+        err_quantise(*units[7], 0, TAIL)
+        err_interleave("vector", *units[7], TAIL, WIDTH[1])
+        for g in range(NG - 1):
+            for m in range(PACK):
+                tail_mm(0, m, g)
+        err_quantise(*units[7], TAIL, WIDTH[1])
         for c in range(2):
-            for pair in range(2):
-                for g in range(NG - 2, NG):
-                    tail_mm(c, pair, g)
-                tail_out("scalar" if pair == 0 else "vector", c, pair)
+            for m in range(PACK):
+                for g in range(NG - 1 if c == 0 else 0, NG):
+                    tail_mm(c, m, g)
+                tail_out("scalar" if m % 2 == 0 else "vector", c, m)

@@ -25,6 +25,9 @@ NK = K // PASS
 WIDTH = [512, 512]
 POOL_ROWS = 3
 TAIL = 256
+SPLIT = 256
+U_BUFS = 2
+E_BUFS = 3
 NH = len(WIDTH)
 COLS = [slice(sum(WIDTH[:h]), sum(WIDTH[: h + 1])) for h in range(NH)]
 
@@ -52,7 +55,7 @@ def tile_echo_nlms_gradient_s11_kernel(
         path_v = path_bytes.rearrange("(g p t) c -> g p t c", p=P, t=PACK)
         out_v = out.rearrange("(q m) c -> m q c", m=PACK)
 
-        far_t, far_pair, far_sorted, mic_t, pbytes = {}, {}, {}, {}, {}
+        far_t, mic_t, pbytes = {}, {}, {}
         zeros = keep.tile([P, PASS], BF16, name="zeros")
 
         def warm_tensor(count):
@@ -62,7 +65,6 @@ def tile_echo_nlms_gradient_s11_kernel(
 
         def load_far(g, lo, hi):
             rows = keep.tile([P, hi - lo, K], BF16, name=f"far{g}_{lo}")
-            far_pair[g, lo] = rows
             nc.sync.dma_start(out=rows[:], in_=far_v[g][:, lo:hi, :])
             for j in range(lo, hi):
                 far_t[g, j] = rows[:, j - lo, :]
@@ -71,9 +73,12 @@ def tile_echo_nlms_gradient_s11_kernel(
             mic_t[g, h] = keep.tile([P, PACK, WIDTH[h]], BF16, name=f"mic{g}_{h}")
             nc.sync.dma_start(out=mic_t[g, h][:], in_=mic_v[g][:, :, COLS[h]])
 
-        def load_path(k, h):
-            pbytes[k, h] = keep.tile([P, PACK, WIDTH[h]], U8, name=f"pbytes{k}_{h}", align_bytes=64)
-            nc.sync.dma_start(out=pbytes[k, h][:], in_=path_v[k][:, :, COLS[h]])
+        def load_path(k, halves):
+            cols = slice(COLS[halves[0]].start, COLS[halves[-1]].stop)
+            rows = keep.tile([P, PACK, cols.stop - cols.start], U8, name=f"pbytes{k}_{halves[0]}", align_bytes=64)
+            nc.sync.dma_start(out=rows[:], in_=path_v[k][:, :, cols])
+            for h in halves:
+                pbytes[k, h] = rows[:, :, COLS[h].start - cols.start : COLS[h].stop - cols.start]
 
         def load_basis_words():
             nc.sync.dma_start(out=bwords[:], in_=basis_words.rearrange("g p n -> p g n"))
@@ -86,12 +91,12 @@ def tile_echo_nlms_gradient_s11_kernel(
 
         x_codes = [keep.tile([P, PACK, NK, P], U32, name=f"x_codes{g}", align_bytes=64) for g in range(NG)]
         x_scales = [keep.tile([P, PACK, NK, P], U8, name=f"x_scales{g}", align_bytes=64) for g in range(NG)]
-        p_codes = [[keep.tile([P, WIDTH[h]], U32, name=f"p_codes{k}_{h}", align_bytes=64) for h in range(NH)] for k in range(NK)]
-        p_scales = [[keep.tile([P, WIDTH[h]], U8, name=f"p_scales{k}_{h}", align_bytes=64) for h in range(NH)] for k in range(NK)]
-        u_codes = [keep.tile([P, R], U32, name=f"u_codes{g}", align_bytes=64) for g in range(NG)]
-        u_scales = [keep.tile([P, R], U8, name=f"u_scales{g}", align_bytes=64) for g in range(NG)]
-        e_codes = [[keep.tile([P, WIDTH[h]], U32, name=f"e_codes{g}_{h}", align_bytes=64) for h in range(NH)] for g in range(NG)]
-        e_scales = [[keep.tile([P, WIDTH[h]], U8, name=f"e_scales{g}_{h}", align_bytes=64) for h in range(NH)] for g in range(NG)]
+        p_codes = [keep.tile([P, NK, PASS], U32, name=f"p_codes{h}", align_bytes=64) for h in range(NH)]
+        p_scales = [keep.tile([P, NK, PASS], U8, name=f"p_scales{h}", align_bytes=64) for h in range(NH)]
+        u_codes = keep.tile([P, NG, R], U32, name="u_codes", align_bytes=64)
+        u_scales = keep.tile([P, NG, R], U8, name="u_scales", align_bytes=64)
+        e_codes = [keep.tile([P, NG, PASS], U32, name=f"e_codes{h}", align_bytes=64) for h in range(NH)]
+        e_scales = [keep.tile([P, NG, PASS], U8, name=f"e_scales{h}", align_bytes=64) for h in range(NH)]
 
         def interleave(engine, grouped, rows, lo, hi):
             dst = grouped[:, lo:hi, :].rearrange("p (c i) t -> p c t i", i=4)
@@ -104,45 +109,40 @@ def tile_echo_nlms_gradient_s11_kernel(
         def quantise(codes, scales, values):
             nc.vector.quantize_mx(out=codes.bitcast(FP8X4), scales=scales, in_=values)
 
+        def quantise_slots(codes, scales, grouped, lo, hi, first):
+            quantise(
+                codes[:, lo:hi, :].rearrange("p a c -> p (a c)"),
+                scales[:, lo:hi, :].rearrange("p a c -> p (a c)"),
+                grouped[:, lo - first : hi - first, :, :].rearrange("p a c t -> p (a c t)"),
+            )
+
         p_rows, p_grouped = {}, {}
 
         def path_widen(engine, k, h, t):
             if (k, h) not in p_rows:
-                p_rows[k, h] = work.tile([P, PACK, WIDTH[h]], BF16, name="p_rows")
+                p_rows[k, h] = work.tile([P, PACK, WIDTH[h]], BF16, name="p_rows", bufs=3)
             dst, src, scale = p_rows[k, h][:, t, :], pbytes[k, h][:, t, :].bitcast(FP8), pscale[:, k, t : t + 1]
             if engine == "vector":
                 nc.vector.tensor_scalar(out=dst, in0=src, scalar1=scale, scalar2=None, op0=ALU.mult)
             else:
                 nc.scalar.activation(out=dst, in_=src, func=COPY, scale=scale)
 
-        def path_interleave(engine, k, h, lo=0, hi=None):
-            if (k, h) not in p_grouped:
-                p_grouped[k, h] = work.tile([P, WIDTH[h], PACK], BF16, name="p_grouped", align_bytes=64)
-            interleave(engine, p_grouped[k, h], p_rows[k, h], lo, hi)
+        def path_interleave(k, h):
+            if h not in p_grouped:
+                p_grouped[h] = work.tile([P, NK, PASS, PACK], BF16, name="p_grouped", align_bytes=64, bufs=1)
+            interleave("vector", p_grouped[h][:, k, :, :], p_rows[k, h], 0, PASS)
 
-        def path_quantise(k, h):
-            quantise(p_codes[k][h][:], p_scales[k][h][:], p_grouped[k, h][:].rearrange("p c t -> p (c t)"))
+        def path_quantise(h, lo, hi):
+            quantise_slots(p_codes[h], p_scales[h], p_grouped[h], lo, hi, 0)
 
         x_grouped, side_bank = {}, {}
-
-        def far_sort(engine, g, lo):
-            far_sorted[g, lo] = work.tile([P, 2 * NK, 2, P], F32, name="far_sorted")
-            src = far_pair[g, lo][:].rearrange("p j k -> p (j k)").bitcast(F32).rearrange("p (a n u) -> p a u n", u=2, n=P)
-            if engine == "vector":
-                nc.vector.tensor_copy(out=far_sorted[g, lo][:], in_=src)
-            else:
-                nc.scalar.copy(out=far_sorted[g, lo][:], in_=src)
 
         def far_turn(g, j):
             words = far_t[g, j].bitcast(F32)
             bank = side.tile([P, NK, 2, P], F32, name="side_bank")
             for k in range(NK):
                 for u in range(2):
-                    if (g, j - j % 2) in far_sorted:
-                        src = far_sorted[g, j - j % 2][:, NK * (j % 2) + k, u, :]
-                    else:
-                        src = words[:, 256 * k + u : 256 * (k + 1) : 2]
-                    nc.tensor.transpose(bank[:, k, u, :], src, ident[:])
+                    nc.tensor.transpose(bank[:, k, u, :], words[:, 256 * k + u : 256 * (k + 1) : 2], ident[:])
             side_bank["far", g, j] = bank
 
         def far_copy(g, j):
@@ -159,31 +159,32 @@ def tile_echo_nlms_gradient_s11_kernel(
 
         u_grouped = {}
 
-        def comp_mm(g, j, pool, name):
+        def comp_mm(g, chunk, j, pool, name):
+            if ("u", g, chunk) not in side_bank:
+                side_bank["u", g, chunk] = pool.tile([P, PACK, P], F32, name=name)
             for k in range(NK):
-                for chunk in range(PACK):
-                    if ("u", g, chunk) not in side_bank:
-                        side_bank["u", g, chunk] = pool.tile([P, PACK, P], F32, name=name)
-                    nc.tensor.matmul_mx(
-                        out=side_bank["u", g, chunk][:, j, :],
-                        lhsT=x_codes[g][:, j, k, :].bitcast(FP8X4),
-                        lhsT_scale=x_scales[g][:, j, k, :],
-                        rhs=bwords[:, k, 2 * chunk * P : 2 * (chunk + 1) * P].bitcast(FP4X4),
-                        rhs_scale=bscale[:, k, chunk * P : (chunk + 1) * P],
-                        start=(k == 0),
-                        stop=(k == NK - 1),
-                    )
+                nc.tensor.matmul_mx(
+                    out=side_bank["u", g, chunk][:, j, :],
+                    lhsT=x_codes[g][:, j, k, :].bitcast(FP8X4),
+                    lhsT_scale=x_scales[g][:, j, k, :],
+                    rhs=bwords[:, k, 2 * chunk * P : 2 * (chunk + 1) * P].bitcast(FP4X4),
+                    rhs_scale=bscale[:, k, chunk * P : (chunk + 1) * P],
+                    start=(k == 0),
+                    stop=(k == NK - 1),
+                )
 
         def comp_copy(g, chunk):
-            if g not in u_grouped:
-                u_grouped[g] = work.tile([P, PACK, P, PACK], BF16, name="u_grouped", align_bytes=64)
+            if g // 2 not in u_grouped:
+                u_grouped[g // 2] = work.tile([P, 2, R, PACK], BF16, name="u_grouped", align_bytes=64, bufs=U_BUFS)
             nc.scalar.copy(
-                out=u_grouped[g][:, :, 32 * chunk : 32 * (chunk + 1), :],
+                out=u_grouped[g // 2][:, g % 2, :, :].rearrange("p (m q) j -> p m q j", m=PACK)[
+                    :, :, 32 * chunk : 32 * (chunk + 1), :
+                ],
                 in_=side_bank["u", g, chunk][:].rearrange("p j (q m) -> p m q j", m=PACK),
             )
 
-        def comp_quantise(g):
-            quantise(u_codes[g][:], u_scales[g][:], u_grouped[g][:].rearrange("p m q j -> p (m q j)"))
+        def comp_quantise(lo, hi):
+            quantise_slots(u_codes, u_scales, u_grouped[lo // 2], lo, hi, lo - lo % 2)
 
         mic_scaled, e_rows, e_grouped, echo_bank = {}, {}, {}, {}
 
@@ -210,8 +211,8 @@ def tile_echo_nlms_gradient_s11_kernel(
                     out=bank[:],
                     lhsT=x_codes[g][:, j, k, :].bitcast(FP8X4),
                     lhsT_scale=x_scales[g][:, j, k, :],
-                    rhs=p_codes[k][h][:, lo:hi].bitcast(FP8X4),
-                    rhs_scale=p_scales[k][h][:, lo:hi],
+                    rhs=p_codes[h][:, k, lo:hi].bitcast(FP8X4),
+                    rhs_scale=p_scales[h][:, k, lo:hi],
                     start=(k == 0),
                     stop=(k == NK - 1),
                 )
@@ -219,7 +220,7 @@ def tile_echo_nlms_gradient_s11_kernel(
 
         def err(g, h, j, lo=0, hi=PASS):
             if (g, h) not in e_rows:
-                e_rows[g, h] = work.tile([P, PACK, WIDTH[h]], BF16, name="e_rows", bufs=4)
+                e_rows[g, h] = work.tile([P, PACK, WIDTH[h]], BF16, name="e_rows", bufs=E_BUFS)
             nc.vector.scalar_tensor_tensor(
                 out=e_rows[g, h][:, j, lo:hi],
                 in0=echo_bank[g, h, j][:],
@@ -229,16 +230,19 @@ def tile_echo_nlms_gradient_s11_kernel(
                 op1=ALU.subtract,
             )
 
-        def err_interleave(engine, g, h, lo=0, hi=None):
-            if (g, h) not in e_grouped:
-                e_grouped[g, h] = work.tile([P, WIDTH[h], PACK], BF16, name="e_grouped", align_bytes=64, bufs=3)
-            interleave(engine, e_grouped[g, h], e_rows[g, h], lo, hi)
+        def err_interleave(engine, g, h, lo=0, hi=PASS):
+            if (g // 2, h) not in e_grouped:
+                e_grouped[g // 2, h] = work.tile([P, 2, PASS, PACK], BF16, name="e_grouped", align_bytes=64)
+            interleave(engine, e_grouped[g // 2, h][:, g % 2, :, :], e_rows[g, h], lo, hi)
 
-        def err_quantise(g, h, lo=0, hi=None):
+        def err_quantise(h, lo, hi):
+            quantise_slots(e_codes[h], e_scales[h], e_grouped[lo // 2, h], lo, hi, lo - lo % 2)
+
+        def err_quantise_columns(g, h, lo, hi):
             quantise(
-                e_codes[g][h][:, lo:hi],
-                e_scales[g][h][:, lo:hi],
-                e_grouped[g, h][:, lo:hi, :].rearrange("p c j -> p (c j)"),
+                e_codes[h][:, g, lo:hi],
+                e_scales[h][:, g, lo:hi],
+                e_grouped[g // 2, h][:, g % 2, lo:hi, :].rearrange("p c j -> p (c j)"),
             )
 
         def grad_mm(h, m, groups):
@@ -247,10 +251,10 @@ def tile_echo_nlms_gradient_s11_kernel(
             for g in groups:
                 nc.tensor.matmul_mx(
                     out=side_bank["grad", h, m][:],
-                    lhsT=u_codes[g][:, m * P : (m + 1) * P].bitcast(FP8X4),
-                    lhsT_scale=u_scales[g][:, m * P : (m + 1) * P],
-                    rhs=e_codes[g][h][:].bitcast(FP8X4),
-                    rhs_scale=e_scales[g][h][:],
+                    lhsT=u_codes[:, g, m * P : (m + 1) * P].bitcast(FP8X4),
+                    lhsT_scale=u_scales[:, g, m * P : (m + 1) * P],
+                    rhs=e_codes[h][:, g, :].bitcast(FP8X4),
+                    rhs_scale=e_scales[h][:, g, :],
                     start=(g == 0),
                     stop=(g == NG - 1),
                 )
@@ -261,15 +265,15 @@ def tile_echo_nlms_gradient_s11_kernel(
                 side_bank["tail", c, m] = pool.tile([P, TAIL], F32, name=name)
             nc.tensor.matmul_mx(
                 out=side_bank["tail", c, m][:],
-                lhsT=u_codes[g][:, m * P : (m + 1) * P].bitcast(FP8X4),
-                lhsT_scale=u_scales[g][:, m * P : (m + 1) * P],
-                rhs=e_codes[g][1][:, c * TAIL : (c + 1) * TAIL].bitcast(FP8X4),
-                rhs_scale=e_scales[g][1][:, c * TAIL : (c + 1) * TAIL],
+                lhsT=u_codes[:, g, m * P : (m + 1) * P].bitcast(FP8X4),
+                lhsT_scale=u_scales[:, g, m * P : (m + 1) * P],
+                rhs=e_codes[1][:, g, c * TAIL : (c + 1) * TAIL].bitcast(FP8X4),
+                rhs_scale=e_scales[1][:, g, c * TAIL : (c + 1) * TAIL],
                 start=(g == 0),
                 stop=(g == NG - 1),
             )
 
-        tail_res = []
+        tail_res, half_res = [], []
 
         def tail_out(engine, c, m):
             if not tail_res:
@@ -284,13 +288,15 @@ def tile_echo_nlms_gradient_s11_kernel(
             nc.sync.dma_start(out=out_v[m][:, first : first + TAIL], in_=res)
 
         def grad_out(engine, h, m):
-            res = work.tile([P, WIDTH[h]], F32, name="res", bufs=4)
+            if not half_res:
+                half_res.append(work.tile([P, PACK, PASS], F32, name="x_grouped", align_bytes=64))
+            res = half_res[0][:, m, :]
             bank, scale = side_bank["grad", h, m], gains[:, m : m + 1]
             if engine == "vector":
-                nc.vector.tensor_scalar(out=res[:], in0=bank[:], scalar1=scale, scalar2=None, op0=ALU.mult)
+                nc.vector.tensor_scalar(out=res, in0=bank[:], scalar1=scale, scalar2=None, op0=ALU.mult)
             else:
-                nc.scalar.activation(out=res[:], in_=bank[:], func=COPY, scale=scale)
-            nc.sync.dma_start(out=out_v[m][:, COLS[h]], in_=res[:])
+                nc.scalar.activation(out=res, in_=bank[:], func=COPY, scale=scale)
+            nc.sync.dma_start(out=out_v[m][:, COLS[h]], in_=res)
 
         nc.vector.memset(bscale[:].rearrange("p g n -> p (g n)").bitcast(I32), 0)
         nc.vector.memset(zeros[:], 0.0)
@@ -298,14 +304,14 @@ def tile_echo_nlms_gradient_s11_kernel(
         nc.scalar.dma_start(out=pscale[:], in_=path_scale.rearrange("(g p t) o -> p g (t o)", p=P, t=PACK))
         warm_column = keep.tile([P, 1], F32, name="warm_column")
         nc.scalar.activation(out=warm_column[:], in_=zeros[:, :1], func=COPY, scale=1.0)
-        load_path(0, 0)
+        load_path(0, [0, 1])
         load_far(0, 0, 1)
         for q in range(4):
             load_basis_scales(q)
         load_far(0, 1, 2)
         load_far(0, 2, 4)
         load_basis_words()
-        load_path(1, 0)
+        load_path(1, [0])
         load_far(1, 0, 2)
         load_far(1, 2, 4)
         nc.sync.dma_start(out=step_bf[:], in_=step.rearrange("(g p j) -> p g j", p=P, j=PACK))
@@ -314,9 +320,9 @@ def tile_echo_nlms_gradient_s11_kernel(
         for g in range(2, NG):
             load_mic(g - 1, 0)
             load_far(g, 0, 2)
+            if g == 2:
+                load_path(1, [1])
             load_far(g, 2, 4)
-        for k in range(NK):
-            load_path(k, 1)
         for g, h in units[NG - 1 :]:
             load_mic(g, h)
         nc.sync.dma_start(out=gain_bf[:], in_=gain.rearrange("(q m) -> q m", m=PACK))
@@ -327,11 +333,9 @@ def tile_echo_nlms_gradient_s11_kernel(
                 far_copy(g, j)
 
         def comp_group(g):
-            for j in range(PACK):
-                comp_mm(g, j, side, "side_bank")
-
-        def comp_copies(g):
             for chunk in range(PACK):
+                for j in range(PACK):
+                    comp_mm(g, chunk, j, side, "side_bank")
                 comp_copy(g, chunk)
 
         def widen_pass(engine, k, h):
@@ -345,25 +349,23 @@ def tile_echo_nlms_gradient_s11_kernel(
             if j == 1:
                 warm_tensor(2)
         widen_pass("vector", 0, 0)
-        path_interleave("vector", 0, 0)
-        far_quantise(0, 0, 1)
-        path_quantise(0, 0)
-        far_quantise(0, 1, 2)
+        path_interleave(0, 0)
+        far_quantise(0, 0, 2)
+        path_quantise(0, 0, 1)
         path_widen("vector", 1, 0, 0)
-        far_quantise(0, 2, 3)
-        path_widen("vector", 1, 0, 1)
-        far_quantise(0, 3, 4)
-        path_widen("vector", 1, 0, 2)
-        path_widen("vector", 1, 0, 3)
-        far_sort("scalar", 1, 0)
-        far_sort("scalar", 1, 2)
+        widen_pass("scalar", 0, 1)
+        far_quantise(0, 2, 4)
+        for t in range(1, PACK):
+            path_widen("vector", 1, 0, t)
         for j in range(PACK):
-            comp_mm(0, j, echo, "echo_bank")
-        comp_copies(0)
+            for chunk in range(PACK):
+                comp_mm(0, chunk, j, echo, "echo_bank")
+        for chunk in range(PACK):
+            comp_copy(0, chunk)
         turn_group(1)
-        path_interleave("vector", 1, 0)
+        path_interleave(1, 0)
         negate_step(0, 0)
-        path_quantise(1, 0)
+        path_quantise(0, 1, 2)
         for j in range(PACK):
             if j == PACK - 1:
                 negate_step(*units[1])
@@ -371,90 +373,73 @@ def tile_echo_nlms_gradient_s11_kernel(
 
         def echo_round(r):
             g, h = units[r]
+            for j in reversed(range(POOL_ROWS)):
+                mic_scale("gpsimd", *units[r + 1], j)
             for j in range(PACK):
                 echo_mm(g, h, j)
                 err(g, h, j)
-                if r + 1 < len(units) and j < POOL_ROWS:
-                    mic_scale("gpsimd", *units[r + 1], j)
 
-        def rest_of_mic(r, engine="vector"):
+        def rest_of_mic(r):
             for j in range(POOL_ROWS, PACK):
-                mic_scale(engine, *units[r + 1], j)
+                mic_scale("scalar", *units[r + 1], j)
 
         echo_round(0)
-        far_quantise(1, 0, 2)
-        far_quantise(1, 2, 4)
+        widen_pass("scalar", 1, 1)
+        far_quantise(1, 0, 4)
         turn_group(2)
         rest_of_mic(0)
         negate_step(*units[2])
-        comp_quantise(0)
+        path_interleave(0, 1)
 
         echo_round(1)
-        far_sort("scalar", 3, 0)
-        far_sort("scalar", 3, 2)
-        far_quantise(2, 0, 2)
-        far_quantise(2, 2, 4)
+        err_interleave("scalar", *units[0])
+        far_quantise(2, 0, 4)
         turn_group(3)
         rest_of_mic(1)
-        for t in range(PACK):
-            if t == PACK - 2:
-                negate_step(*units[3])
-            path_widen("vector", 0, 1, t)
+        negate_step(*units[3])
+        path_interleave(1, 1)
 
         echo_round(2)
-        widen_pass("scalar", 1, 1)
-        far_quantise(3, 0, 2)
-        far_quantise(3, 2, 4)
+        err_interleave("scalar", *units[1])
+        far_quantise(3, 0, 4)
         comp_group(1)
-        path_interleave("vector", 0, 1)
+        rest_of_mic(2)
         negate_step(*units[4])
-        path_interleave("vector", 1, 1)
-        rest_of_mic(2, "scalar")
-        err_interleave("scalar", *units[0])
+        path_quantise(1, 0, 2)
 
         echo_round(3)
-        comp_copies(1)
+        err_interleave("scalar", *units[2])
         comp_group(2)
-        path_quantise(0, 1)
-        path_quantise(1, 1)
         rest_of_mic(3)
-        err_quantise(*units[0])
+        err_quantise(0, 0, 2)
         negate_step(*units[5])
-        comp_quantise(1)
-        err_interleave("scalar", *units[1])
+        comp_quantise(0, 2)
 
         echo_round(4)
-        comp_copies(2)
         comp_group(3)
-        err_interleave("vector", *units[2])
         rest_of_mic(4)
-        err_quantise(*units[1])
+        err_interleave("vector", *units[3])
         negate_step(*units[6])
-        comp_quantise(2)
-        err_interleave("scalar", *units[3])
+        err_quantise(0, 2, 4)
 
         nc.scalar.copy(out=gains[:], in_=gain_bf[:])
         echo_round(5)
-        comp_copies(3)
+        err_interleave("scalar", *units[4])
         for m in range(PACK):
             grad_mm(0, m, range(NG // 2))
-        err_interleave("scalar", *units[4])
-        err_quantise(*units[2])
         rest_of_mic(5)
-        err_quantise(*units[3])
+        err_interleave("scalar", *units[5])
         negate_step(*units[7])
-        comp_quantise(3)
+        comp_quantise(2, 4)
 
         echo_round(6)
-        err_interleave("scalar", *units[5])
-        err_interleave("scalar", *units[6], TAIL, WIDTH[1])
+        rest_of_mic(6)
+        err_interleave("scalar", *units[6], SPLIT, PASS)
         for m in range(PACK):
             grad_mm(0, m, range(NG // 2, NG))
             grad_out("scalar", 0, m)
-        rest_of_mic(6)
-        err_quantise(*units[4])
-        err_interleave("vector", *units[6], 0, TAIL)
-        err_quantise(*units[5])
+        err_quantise(1, 0, 2)
+        err_interleave("vector", *units[6], 0, SPLIT)
 
         for c in range(2):
             for j in range(PACK):
@@ -462,13 +447,13 @@ def tile_echo_nlms_gradient_s11_kernel(
                 err(*units[7], j, c * TAIL, (c + 1) * TAIL)
             if c == 0:
                 err_interleave("scalar", *units[7], 0, TAIL)
-                err_quantise(*units[6])
-        err_quantise(*units[7], 0, TAIL)
-        err_interleave("vector", *units[7], TAIL, WIDTH[1])
+                err_quantise(1, 2, 3)
+        err_quantise_columns(*units[7], 0, TAIL)
+        err_interleave("vector", *units[7], TAIL, PASS)
         for g in range(NG - 1):
             for m in range(PACK):
                 tail_mm(0, m, g)
-        err_quantise(*units[7], TAIL, WIDTH[1])
+        err_quantise_columns(*units[7], TAIL, PASS)
         for c in range(2):
             for m in range(PACK):
                 for g in range(NG - 1 if c == 0 else 0, NG):

@@ -56,12 +56,6 @@ def tile_echo_nlms_gradient_s11_kernel(
         out_v = out.rearrange("(q m) c -> m q c", m=PACK)
 
         far_t, mic_t, pbytes = {}, {}, {}
-        zeros = keep.tile([P, PASS], BF16, name="zeros")
-
-        def warm_tensor(count):
-            bank = echo.tile([P, PASS], F32, name="echo_bank")
-            for i in range(count):
-                nc.tensor.matmul(bank[:], lhsT=zeros[:, :P], rhs=zeros[:], start=(i == 0), stop=(i == count - 1))
 
         def load_far(g, lo, hi):
             rows = keep.tile([P, hi - lo, K], BF16, name=f"far{g}_{lo}")
@@ -299,19 +293,18 @@ def tile_echo_nlms_gradient_s11_kernel(
             nc.sync.dma_start(out=out_v[m][:, COLS[h]], in_=res)
 
         nc.vector.memset(bscale[:].rearrange("p g n -> p (g n)").bitcast(I32), 0)
-        nc.vector.memset(zeros[:], 0.0)
         make_identity(nc, ident[:])
         nc.scalar.dma_start(out=pscale[:], in_=path_scale.rearrange("(g p t) o -> p g (t o)", p=P, t=PACK))
-        warm_column = keep.tile([P, 1], F32, name="warm_column")
-        nc.scalar.activation(out=warm_column[:], in_=zeros[:, :1], func=COPY, scale=1.0)
-        load_path(0, [0, 1])
         load_far(0, 0, 1)
+        load_far(0, 1, 2)
         for q in range(4):
             load_basis_scales(q)
-        load_far(0, 1, 2)
-        load_far(0, 2, 4)
+        load_far(0, 2, 3)
+        load_path(0, [0])
+        load_far(0, 3, 4)
         load_basis_words()
         load_path(1, [0])
+        load_path(0, [1])
         load_far(1, 0, 2)
         load_far(1, 2, 4)
         nc.sync.dma_start(out=step_bf[:], in_=step.rearrange("(g p j) -> p g j", p=P, j=PACK))
@@ -342,21 +335,19 @@ def tile_echo_nlms_gradient_s11_kernel(
             for t in range(PACK):
                 path_widen(engine, k, h, t)
 
-        warm_tensor(4)
         for j in range(PACK):
             far_turn(0, j)
             far_copy(0, j)
-            if j == 1:
-                warm_tensor(2)
-        widen_pass("vector", 0, 0)
-        path_interleave(0, 0)
-        far_quantise(0, 0, 2)
-        path_quantise(0, 0, 1)
-        path_widen("vector", 1, 0, 0)
+        for j in range(PACK):
+            far_quantise(0, j, j + 1)
+            if j < PACK - 1:
+                for plane in (2 * j, 2 * j + 1):
+                    path_widen("vector", plane // PACK, 0, plane % PACK)
         widen_pass("scalar", 0, 1)
-        far_quantise(0, 2, 4)
-        for t in range(1, PACK):
+        path_interleave(0, 0)
+        for t in range(2, PACK):
             path_widen("vector", 1, 0, t)
+        path_quantise(0, 0, 1)
         for j in range(PACK):
             for chunk in range(PACK):
                 comp_mm(0, chunk, j, echo, "echo_bank")
@@ -384,50 +375,52 @@ def tile_echo_nlms_gradient_s11_kernel(
                 mic_scale("scalar", *units[r + 1], j)
 
         echo_round(0)
+        rest_of_mic(0)
         widen_pass("scalar", 1, 1)
         far_quantise(1, 0, 4)
         turn_group(2)
-        rest_of_mic(0)
         negate_step(*units[2])
         path_interleave(0, 1)
 
         echo_round(1)
+        rest_of_mic(1)
         err_interleave("scalar", *units[0])
         far_quantise(2, 0, 4)
         turn_group(3)
-        rest_of_mic(1)
         negate_step(*units[3])
         path_interleave(1, 1)
 
         echo_round(2)
-        err_interleave("scalar", *units[1])
+        rest_of_mic(2)
+        err_interleave("scalar", *units[1], SPLIT, PASS)
         far_quantise(3, 0, 4)
         comp_group(1)
-        rest_of_mic(2)
+        err_interleave("vector", *units[1], 0, SPLIT)
         negate_step(*units[4])
         path_quantise(1, 0, 2)
 
         echo_round(3)
+        rest_of_mic(3)
         err_interleave("scalar", *units[2])
         comp_group(2)
-        rest_of_mic(3)
         err_quantise(0, 0, 2)
         negate_step(*units[5])
         comp_quantise(0, 2)
 
         echo_round(4)
-        comp_group(3)
         rest_of_mic(4)
-        err_interleave("vector", *units[3])
+        err_interleave("scalar", *units[3])
+        comp_group(3)
+        err_interleave("vector", *units[4], 0, SPLIT)
         negate_step(*units[6])
         err_quantise(0, 2, 4)
 
         nc.scalar.copy(out=gains[:], in_=gain_bf[:])
         echo_round(5)
-        err_interleave("scalar", *units[4])
+        rest_of_mic(5)
+        err_interleave("scalar", *units[4], SPLIT, PASS)
         for m in range(PACK):
             grad_mm(0, m, range(NG // 2))
-        rest_of_mic(5)
         err_interleave("scalar", *units[5])
         negate_step(*units[7])
         comp_quantise(2, 4)

@@ -392,10 +392,9 @@ def tile_echo_nlms_gradient_s11_kernel(
 
         echo_round(2)
         rest_of_mic(2)
-        err_interleave("scalar", *units[1], SPLIT, PASS)
+        err_interleave("scalar", *units[1])
         far_quantise(3, 0, 4)
         comp_group(1)
-        err_interleave("vector", *units[1], 0, SPLIT)
         negate_step(*units[4])
         path_quantise(1, 0, 2)
 
@@ -409,21 +408,21 @@ def tile_echo_nlms_gradient_s11_kernel(
 
         echo_round(4)
         rest_of_mic(4)
-        err_interleave("scalar", *units[3])
         comp_group(3)
-        err_interleave("vector", *units[4], 0, SPLIT)
+        err_interleave("vector", *units[3])
         negate_step(*units[6])
         err_quantise(0, 2, 4)
 
         nc.scalar.copy(out=gains[:], in_=gain_bf[:])
         echo_round(5)
         rest_of_mic(5)
-        err_interleave("scalar", *units[4], SPLIT, PASS)
+        err_interleave("scalar", *units[4])
         for m in range(PACK):
             grad_mm(0, m, range(NG // 2))
-        err_interleave("scalar", *units[5])
-        negate_step(*units[7])
+        err_interleave("scalar", *units[5], SPLIT, PASS)
         comp_quantise(2, 4)
+        negate_step(*units[7])
+        err_interleave("vector", *units[5], 0, SPLIT)
 
         echo_round(6)
         rest_of_mic(6)

@@ -22,14 +22,11 @@ PACK = 4
 PASS = P * PACK
 NG = T // PASS
 NK = K // PASS
-WIDTH = [512, 512]
-POOL_ROWS = 3
-TAIL = 256
-SPLIT = 256
-U_BUFS = 2
-E_BUFS = 3
-NH = len(WIDTH)
-COLS = [slice(sum(WIDTH[:h]), sum(WIDTH[: h + 1])) for h in range(NH)]
+NH = C // PASS
+UNITS = [(g, h) for h in range(NH) for g in range(NG)]
+SLABS = 3
+SPLIT = 320
+LOW, HIGH = 0, PACK
 
 
 def tile_echo_nlms_gradient_s11_kernel(
@@ -39,13 +36,13 @@ def tile_echo_nlms_gradient_s11_kernel(
     with ExitStack() as ctx:
         keep = ctx.enter_context(tc.tile_pool(name="keep", bufs=1))
         work = ctx.enter_context(tc.tile_pool(name="work", bufs=2))
-        side = ctx.enter_context(tc.psum_pool(name="side", bufs=4))
-        echo = ctx.enter_context(tc.psum_pool(name="echo", bufs=4))
+        psum = ctx.enter_context(tc.psum_pool(name="psum", bufs=1))
         ctx.enter_context(tc.manual_schedule())
 
         ident = keep.tile([P, P], F32, name="ident")
         pscale = keep.tile([P, NK, PACK], F32, name="pscale")
         step_bf = keep.tile([P, NG, PACK], BF16, name="step_bf")
+        negstep = keep.tile([P, NG, PACK], F32, name="negstep")
         gain_bf = keep.tile([P, PACK], BF16, name="gain_bf")
         gains = keep.tile([P, PACK], F32, name="gains")
         bscale = keep.tile([P, NK, R], U8, name="bscale", align_bytes=64)
@@ -58,24 +55,20 @@ def tile_echo_nlms_gradient_s11_kernel(
         far_t, mic_t, pbytes = {}, {}, {}
 
         def load_far(g, lo, hi):
-            rows = keep.tile([P, hi - lo, K], BF16, name=f"far{g}_{lo}")
+            rows = keep.tile([P, hi - lo, K], BF16, name=f"rows{g}_{lo}", align_bytes=64)
             nc.sync.dma_start(out=rows[:], in_=far_v[g][:, lo:hi, :])
             for j in range(lo, hi):
                 far_t[g, j] = rows[:, j - lo, :]
 
-        def load_mic(g, h):
-            mic_t[g, h] = keep.tile([P, PACK, WIDTH[h]], BF16, name=f"mic{g}_{h}")
-            nc.sync.dma_start(out=mic_t[g, h][:], in_=mic_v[g][:, :, COLS[h]])
+        def load_mic(g):
+            mic_t[g] = keep.tile([P, PACK, C], BF16, name=f"mic{g}")
+            nc.sync.dma_start(out=mic_t[g][:], in_=mic_v[g])
 
-        def load_path(k, halves):
-            cols = slice(COLS[halves[0]].start, COLS[halves[-1]].stop)
-            rows = keep.tile([P, PACK, cols.stop - cols.start], U8, name=f"pbytes{k}_{halves[0]}", align_bytes=64)
-            nc.sync.dma_start(out=rows[:], in_=path_v[k][:, :, cols])
-            for h in halves:
-                pbytes[k, h] = rows[:, :, COLS[h].start - cols.start : COLS[h].stop - cols.start]
-
-        def load_basis_words():
-            nc.sync.dma_start(out=bwords[:], in_=basis_words.rearrange("g p n -> p g n"))
+        def load_path(k, lo, hi):
+            planes = keep.tile([P, hi - lo, C], U8, name=f"pbytes{k}_{lo}", align_bytes=64)
+            nc.sync.dma_start(out=planes[:], in_=path_v[k][:, lo:hi, :])
+            for t in range(lo, hi):
+                pbytes[k, t] = planes[:, t - lo, :]
 
         def load_basis_scales(q):
             nc.sync.dma_start(
@@ -85,16 +78,19 @@ def tile_echo_nlms_gradient_s11_kernel(
 
         x_codes = [keep.tile([P, PACK, NK, P], U32, name=f"x_codes{g}", align_bytes=64) for g in range(NG)]
         x_scales = [keep.tile([P, PACK, NK, P], U8, name=f"x_scales{g}", align_bytes=64) for g in range(NG)]
-        p_codes = [keep.tile([P, NK, PASS], U32, name=f"p_codes{h}", align_bytes=64) for h in range(NH)]
-        p_scales = [keep.tile([P, NK, PASS], U8, name=f"p_scales{h}", align_bytes=64) for h in range(NH)]
+        p_codes = keep.tile([P, NK, C], U32, name="p_codes", align_bytes=64)
+        p_scales = keep.tile([P, NK, C], U8, name="p_scales", align_bytes=64)
         u_codes = keep.tile([P, NG, R], U32, name="u_codes", align_bytes=64)
         u_scales = keep.tile([P, NG, R], U8, name="u_scales", align_bytes=64)
-        e_codes = [keep.tile([P, NG, PASS], U32, name=f"e_codes{h}", align_bytes=64) for h in range(NH)]
-        e_scales = [keep.tile([P, NG, PASS], U8, name=f"e_scales{h}", align_bytes=64) for h in range(NH)]
+        e_codes = keep.tile([P, len(UNITS), PASS], U32, name="e_codes", align_bytes=64)
+        e_scales = keep.tile([P, len(UNITS), PASS], U8, name="e_scales", align_bytes=64)
 
-        def interleave(engine, grouped, rows, lo, hi):
-            dst = grouped[:, lo:hi, :].rearrange("p (c i) t -> p c t i", i=4)
-            src = rows[:, :, lo:hi].rearrange("p t (c i) -> p c t i", i=4)
+        def half(h):
+            return slice(h * PASS, (h + 1) * PASS)
+
+        def interleave(engine, grouped, rows):
+            dst = grouped.rearrange("p (c i) t -> p c t i", i=4)
+            src = rows.rearrange("p t (c i) -> p c t i", i=4)
             if engine == "vector":
                 nc.vector.tensor_copy(out=dst, in_=src)
             else:
@@ -103,94 +99,7 @@ def tile_echo_nlms_gradient_s11_kernel(
         def quantise(codes, scales, values):
             nc.vector.quantize_mx(out=codes.bitcast(FP8X4), scales=scales, in_=values)
 
-        def quantise_slots(codes, scales, grouped, lo, hi, first):
-            quantise(
-                codes[:, lo:hi, :].rearrange("p a c -> p (a c)"),
-                scales[:, lo:hi, :].rearrange("p a c -> p (a c)"),
-                grouped[:, lo - first : hi - first, :, :].rearrange("p a c t -> p (a c t)"),
-            )
-
-        p_rows, p_grouped = {}, {}
-
-        def path_widen(engine, k, h, t):
-            if (k, h) not in p_rows:
-                p_rows[k, h] = work.tile([P, PACK, WIDTH[h]], BF16, name="p_rows", bufs=3)
-            dst, src, scale = p_rows[k, h][:, t, :], pbytes[k, h][:, t, :].bitcast(FP8), pscale[:, k, t : t + 1]
-            if engine == "vector":
-                nc.vector.tensor_scalar(out=dst, in0=src, scalar1=scale, scalar2=None, op0=ALU.mult)
-            else:
-                nc.scalar.activation(out=dst, in_=src, func=COPY, scale=scale)
-
-        def path_interleave(k, h):
-            if h not in p_grouped:
-                p_grouped[h] = work.tile([P, NK, PASS, PACK], BF16, name="p_grouped", align_bytes=64, bufs=1)
-            interleave("vector", p_grouped[h][:, k, :, :], p_rows[k, h], 0, PASS)
-
-        def path_quantise(h, lo, hi):
-            quantise_slots(p_codes[h], p_scales[h], p_grouped[h], lo, hi, 0)
-
-        x_grouped, side_bank = {}, {}
-
-        def far_turn(g, j):
-            words = far_t[g, j].bitcast(F32)
-            bank = side.tile([P, NK, 2, P], F32, name="side_bank")
-            for k in range(NK):
-                for u in range(2):
-                    nc.tensor.transpose(bank[:, k, u, :], words[:, 256 * k + u : 256 * (k + 1) : 2], ident[:])
-            side_bank["far", g, j] = bank
-
-        def far_copy(g, j):
-            if g not in x_grouped:
-                x_grouped[g] = work.tile([P, PACK, NK, P, 2], F32, name="x_grouped", align_bytes=64)
-            nc.scalar.copy(out=x_grouped[g][:, j, :, :, :], in_=side_bank["far", g, j][:].rearrange("p k u n -> p k n u"))
-
-        def far_quantise(g, lo, hi):
-            quantise(
-                x_codes[g][:, lo:hi, :, :].rearrange("p j k n -> p (j k n)"),
-                x_scales[g][:, lo:hi, :, :].rearrange("p j k n -> p (j k n)"),
-                x_grouped[g][:, lo:hi, :, :, :].rearrange("p j k n u -> p (j k n u)").bitcast(BF16),
-            )
-
-        u_grouped = {}
-
-        def comp_mm(g, chunk, j, pool, name):
-            if ("u", g, chunk) not in side_bank:
-                side_bank["u", g, chunk] = pool.tile([P, PACK, P], F32, name=name)
-            for k in range(NK):
-                nc.tensor.matmul_mx(
-                    out=side_bank["u", g, chunk][:, j, :],
-                    lhsT=x_codes[g][:, j, k, :].bitcast(FP8X4),
-                    lhsT_scale=x_scales[g][:, j, k, :],
-                    rhs=bwords[:, k, 2 * chunk * P : 2 * (chunk + 1) * P].bitcast(FP4X4),
-                    rhs_scale=bscale[:, k, chunk * P : (chunk + 1) * P],
-                    start=(k == 0),
-                    stop=(k == NK - 1),
-                )
-
-        def comp_copy(g, chunk):
-            if g // 2 not in u_grouped:
-                u_grouped[g // 2] = work.tile([P, 2, R, PACK], BF16, name="u_grouped", align_bytes=64, bufs=U_BUFS)
-            nc.scalar.copy(
-                out=u_grouped[g // 2][:, g % 2, :, :].rearrange("p (m q) j -> p m q j", m=PACK)[
-                    :, :, 32 * chunk : 32 * (chunk + 1), :
-                ],
-                in_=side_bank["u", g, chunk][:].rearrange("p j (q m) -> p m q j", m=PACK),
-            )
-
-        def comp_quantise(lo, hi):
-            quantise_slots(u_codes, u_scales, u_grouped[lo // 2], lo, hi, lo - lo % 2)
-
-        mic_scaled, e_rows, e_grouped, echo_bank = {}, {}, {}, {}
-
-        negstep = {}
-
-        def negate_step(g, h):
-            negstep[g, h] = keep.tile([P, PACK], F32, name=f"negstep{g}_{h}")
-            nc.vector.tensor_scalar(out=negstep[g, h][:], in0=step_bf[:, g, :], scalar1=-1.0, scalar2=None, op0=ALU.mult)
-
-        def mic_scale(engine, g, h, j):
-            mic_scaled[g, h, j] = work.tile([P, WIDTH[h]], F32, name=f"mic_scaled{j}", bufs=2)
-            dst, src, scale = mic_scaled[g, h, j][:], mic_t[g, h][:, j, :], negstep[g, h][:, j : j + 1]
+        def scale_rows(engine, dst, src, scale):
             if engine == "vector":
                 nc.vector.tensor_scalar(out=dst, in0=src, scalar1=scale, scalar2=None, op0=ALU.mult)
             elif engine == "gpsimd":
@@ -198,256 +107,261 @@ def tile_echo_nlms_gradient_s11_kernel(
             else:
                 nc.scalar.activation(out=dst, in_=src, func=COPY, scale=scale)
 
-        def echo_mm(g, h, j, lo=0, hi=PASS):
-            bank = echo.tile([P, hi - lo], F32, name="echo_bank")
-            for k in range(NK):
-                nc.tensor.matmul_mx(
-                    out=bank[:],
-                    lhsT=x_codes[g][:, j, k, :].bitcast(FP8X4),
-                    lhsT_scale=x_scales[g][:, j, k, :],
-                    rhs=p_codes[h][:, k, lo:hi].bitcast(FP8X4),
-                    rhs_scale=p_scales[h][:, k, lo:hi],
-                    start=(k == 0),
-                    stop=(k == NK - 1),
-                )
-            echo_bank[g, h, j] = bank
+        p_rows, p_grouped = {}, {}
 
-        def err(g, h, j, lo=0, hi=PASS):
-            if (g, h) not in e_rows:
-                e_rows[g, h] = work.tile([P, PACK, WIDTH[h]], BF16, name="e_rows", bufs=E_BUFS)
-            nc.vector.scalar_tensor_tensor(
-                out=e_rows[g, h][:, j, lo:hi],
-                in0=echo_bank[g, h, j][:],
-                scalar=negstep[g, h][:, j : j + 1],
-                in1=mic_scaled[g, h, j][:, lo:hi],
-                op0=ALU.mult,
-                op1=ALU.subtract,
-            )
+        def path_widen(engine, k, planes, cols=slice(0, C)):
+            if k not in p_rows:
+                p_rows[k] = work.tile([P, PACK, C], BF16, name="p_rows")
+            for t in planes:
+                scale_rows(engine, p_rows[k][:, t, cols], pbytes[k, t][:, cols].bitcast(FP8), pscale[:, k, t : t + 1])
 
-        def err_interleave(engine, g, h, lo=0, hi=PASS):
-            if (g // 2, h) not in e_grouped:
-                e_grouped[g // 2, h] = work.tile([P, 2, PASS, PACK], BF16, name="e_grouped", align_bytes=64)
-            interleave(engine, e_grouped[g // 2, h][:, g % 2, :, :], e_rows[g, h], lo, hi)
+        def path_interleave(k, h):
+            if k not in p_grouped:
+                p_grouped[k] = work.tile([P, C, PACK], BF16, name="p_grouped", align_bytes=64)
+            interleave("vector", p_grouped[k][:, half(h), :], p_rows[k][:, :, half(h)])
 
-        def err_quantise(h, lo, hi):
-            quantise_slots(e_codes[h], e_scales[h], e_grouped[lo // 2, h], lo, hi, lo - lo % 2)
+        def path_quantise(k, cols):
+            quantise(p_codes[:, k, cols], p_scales[:, k, cols], p_grouped[k][:, cols, :].rearrange("p c t -> p (c t)"))
 
-        def err_quantise_columns(g, h, lo, hi):
+        x_grouped = {}
+
+        def turn_group(g, first):
+            x_grouped[g] = work.tile([P, PACK, NK, P, 2], F32, name="wide", align_bytes=64)
+            for j in range(PACK):
+                words = far_t[g, j].bitcast(F32)
+                bank = psum.tile([P, NK, 2, P], F32, name=f"bank{first + j}")
+                for k in range(NK):
+                    for u in range(2):
+                        nc.tensor.transpose(bank[:, k, u, :], words[:, 256 * k + u : 256 * (k + 1) : 2], ident[:])
+                nc.scalar.copy(out=x_grouped[g][:, j, :, :, :], in_=bank[:].rearrange("p k u n -> p k n u"))
+
+        def far_quantise(g, rows=slice(0, PACK)):
             quantise(
-                e_codes[h][:, g, lo:hi],
-                e_scales[h][:, g, lo:hi],
-                e_grouped[g // 2, h][:, g % 2, lo:hi, :].rearrange("p c j -> p (c j)"),
+                x_codes[g][:, rows, :, :].rearrange("p j k n -> p (j k n)"),
+                x_scales[g][:, rows, :, :].rearrange("p j k n -> p (j k n)"),
+                x_grouped[g][:, rows, :, :, :].rearrange("p j k n u -> p (j k n u)").bitcast(BF16),
             )
 
-        def grad_mm(h, m, groups):
-            if ("grad", h, m) not in side_bank:
-                side_bank["grad", h, m] = side.tile([P, WIDTH[h]], F32, name="side_bank")
+        u_grouped, comp_bank = {}, {}
+
+        def comp_mm(g, first):
+            u_grouped[g] = keep.tile([P, R, PACK], BF16, name=f"slab{g + 1}", align_bytes=64)
+            for chunk in range(PACK):
+                bank = comp_bank[g, chunk] = psum.tile([P, PACK, P], F32, name=f"bank{first + chunk}")
+                for j in range(PACK):
+                    for k in range(NK):
+                        nc.tensor.matmul_mx(
+                            out=bank[:, j, :],
+                            lhsT=x_codes[g][:, j, k, :].bitcast(FP8X4),
+                            lhsT_scale=x_scales[g][:, j, k, :],
+                            rhs=bwords[:, k, 2 * chunk * P : 2 * (chunk + 1) * P].bitcast(FP4X4),
+                            rhs_scale=bscale[:, k, chunk * P : (chunk + 1) * P],
+                            start=(k == 0),
+                            stop=(k == NK - 1),
+                        )
+
+        def comp_copy(g):
+            for chunk in range(PACK):
+                bank = comp_bank[g, chunk]
+                nc.scalar.copy(
+                    out=u_grouped[g][:].rearrange("p (m q) j -> p m q j", m=PACK)[:, :, 32 * chunk : 32 * (chunk + 1), :],
+                    in_=bank[:].rearrange("p j (q m) -> p m q j", m=PACK),
+                )
+
+        def comp_group(g, first):
+            comp_mm(g, first)
+            comp_copy(g)
+
+        def comp_quantise(g):
+            quantise(u_codes[:, g, :], u_scales[:, g, :], u_grouped[g][:].rearrange("p r j -> p (r j)"))
+
+        mic_scaled, e_rows, e_grouped, echo_bank = {}, {}, {}, {}
+
+        def mic_scale(engine, r, lo, name):
+            g, h = UNITS[r]
+            pair = keep.tile([P, 2, PASS], F32, name=name, align_bytes=64)
+            for j in range(lo, lo + 2):
+                mic_scaled[r, j] = pair[:, j - lo, :]
+                scale_rows(engine, mic_scaled[r, j], mic_t[g][:, j, half(h)], negstep[:, g, j : j + 1])
+
+        def echo_mm(r, first):
+            g, h = UNITS[r]
+            for j in range(PACK):
+                echo_bank[r, j] = psum.tile([P, PASS], F32, name=f"bank{first + j}")
+                for k in range(NK):
+                    nc.tensor.matmul_mx(
+                        out=echo_bank[r, j][:],
+                        lhsT=x_codes[g][:, j, k, :].bitcast(FP8X4),
+                        lhsT_scale=x_scales[g][:, j, k, :],
+                        rhs=p_codes[:, k, half(h)].bitcast(FP8X4),
+                        rhs_scale=p_scales[:, k, half(h)],
+                        start=(k == 0),
+                        stop=(k == NK - 1),
+                    )
+
+        def err(r):
+            g, h = UNITS[r]
+            e_rows[r] = work.tile([P, PACK, PASS], BF16, name="e_rows")
+            for j in range(PACK):
+                nc.vector.scalar_tensor_tensor(
+                    out=e_rows[r][:, j, :],
+                    in0=echo_bank[r, j][:],
+                    scalar=negstep[:, g, j : j + 1],
+                    in1=mic_scaled[r, j],
+                    op0=ALU.mult,
+                    op1=ALU.subtract,
+                )
+
+        def err_interleave(engine, r, lo=0, hi=PASS):
+            if r not in e_grouped:
+                e_grouped[r] = keep.tile([P, PASS, PACK], BF16, name=f"slab{r % SLABS}", align_bytes=64)
+            interleave(engine, e_grouped[r][:, lo:hi, :], e_rows[r][:, :, lo:hi])
+
+        def err_quantise(r):
+            quantise(e_codes[:, r, :], e_scales[:, r, :], e_grouped[r][:].rearrange("p c j -> p (c j)"))
+
+        grad_bank, result = {}, {}
+
+        def grad_mm(h, m, groups, bank):
+            if (h, m) not in grad_bank:
+                grad_bank[h, m] = psum.tile([P, PASS], F32, name=f"bank{bank}")
             for g in groups:
                 nc.tensor.matmul_mx(
-                    out=side_bank["grad", h, m][:],
+                    out=grad_bank[h, m][:],
                     lhsT=u_codes[:, g, m * P : (m + 1) * P].bitcast(FP8X4),
                     lhsT_scale=u_scales[:, g, m * P : (m + 1) * P],
-                    rhs=e_codes[h][:, g, :].bitcast(FP8X4),
-                    rhs_scale=e_scales[h][:, g, :],
+                    rhs=e_codes[:, NG * h + g, :].bitcast(FP8X4),
+                    rhs_scale=e_scales[:, NG * h + g, :],
                     start=(g == 0),
                     stop=(g == NG - 1),
                 )
 
-        def tail_mm(c, m, g):
-            if ("tail", c, m) not in side_bank:
-                pool, name = (side, "side_bank") if c == 0 else (echo, "echo_bank")
-                side_bank["tail", c, m] = pool.tile([P, TAIL], F32, name=name)
-            nc.tensor.matmul_mx(
-                out=side_bank["tail", c, m][:],
-                lhsT=u_codes[:, g, m * P : (m + 1) * P].bitcast(FP8X4),
-                lhsT_scale=u_scales[:, g, m * P : (m + 1) * P],
-                rhs=e_codes[1][:, g, c * TAIL : (c + 1) * TAIL].bitcast(FP8X4),
-                rhs_scale=e_scales[1][:, g, c * TAIL : (c + 1) * TAIL],
-                start=(g == 0),
-                stop=(g == NG - 1),
-            )
-
-        tail_res, half_res = [], []
-
-        def tail_out(engine, c, m):
-            if not tail_res:
-                tail_res.append(work.tile([P, 2, PACK, TAIL], F32, name="x_grouped", align_bytes=64))
-            res = tail_res[0][:, c, m, :]
-            src, scale = side_bank["tail", c, m][:], gains[:, m : m + 1]
-            if engine == "vector":
-                nc.vector.tensor_scalar(out=res, in0=src, scalar1=scale, scalar2=None, op0=ALU.mult)
-            else:
-                nc.scalar.activation(out=res, in_=src, func=COPY, scale=scale)
-            first = WIDTH[0] + c * TAIL
-            nc.sync.dma_start(out=out_v[m][:, first : first + TAIL], in_=res)
-
         def grad_out(engine, h, m):
-            if not half_res:
-                half_res.append(work.tile([P, PACK, PASS], F32, name="x_grouped", align_bytes=64))
-            res = half_res[0][:, m, :]
-            bank, scale = side_bank["grad", h, m], gains[:, m : m + 1]
-            if engine == "vector":
-                nc.vector.tensor_scalar(out=res, in0=bank[:], scalar1=scale, scalar2=None, op0=ALU.mult)
-            else:
-                nc.scalar.activation(out=res, in_=bank[:], func=COPY, scale=scale)
-            nc.sync.dma_start(out=out_v[m][:, COLS[h]], in_=res)
+            if h not in result:
+                result[h] = work.tile([P, PACK, PASS], F32, name="wide", align_bytes=64)
+            scale_rows(engine, result[h][:, m, :], grad_bank[h, m][:], gains[:, m : m + 1])
+            nc.sync.dma_start(out=out_v[m][:, half(h)], in_=result[h][:, m, :])
 
         nc.vector.memset(bscale[:].rearrange("p g n -> p (g n)").bitcast(I32), 0)
         make_identity(nc, ident[:])
         nc.scalar.dma_start(out=pscale[:], in_=path_scale.rearrange("(g p t) o -> p g (t o)", p=P, t=PACK))
-        load_far(0, 0, 1)
-        load_far(0, 1, 2)
+        nc.scalar.dma_start(out=step_bf[:], in_=step.rearrange("(g p j) -> p g j", p=P, j=PACK))
+        load_path(0, 0, 2)
+        load_path(0, 2, 4)
+        for j in range(PACK):
+            load_far(0, j, j + 1)
         for q in range(4):
             load_basis_scales(q)
-        load_far(0, 2, 3)
-        load_path(0, [0])
-        load_far(0, 3, 4)
-        load_basis_words()
-        load_path(1, [0])
-        load_path(0, [1])
-        load_far(1, 0, 2)
-        load_far(1, 2, 4)
-        nc.sync.dma_start(out=step_bf[:], in_=step.rearrange("(g p j) -> p g j", p=P, j=PACK))
-        units = [(g, h) for h in range(NH) for g in range(NG)]
-        load_mic(0, 0)
+        for j in range(PACK):
+            load_far(1, j, j + 1)
+        nc.sync.dma_start(out=bwords[:], in_=basis_words.rearrange("g p n -> p g n"))
+        load_path(1, 0, 4)
         for g in range(2, NG):
-            load_mic(g - 1, 0)
             load_far(g, 0, 2)
-            if g == 2:
-                load_path(1, [1])
             load_far(g, 2, 4)
-        for g, h in units[NG - 1 :]:
-            load_mic(g, h)
+        for g in range(NG):
+            load_mic(g)
         nc.sync.dma_start(out=gain_bf[:], in_=gain.rearrange("(q m) -> q m", m=PACK))
 
-        def turn_group(g):
-            for j in range(PACK):
-                far_turn(g, j)
-                far_copy(g, j)
+        spare = {0: "rows2_0", 1: "rows2_2", 2: "rows3_0", 3: "rows3_2", 4: "pair4", 5: "pair5", 6: "pair6", 7: "pair7"}
 
-        def comp_group(g):
-            for chunk in range(PACK):
-                for j in range(PACK):
-                    comp_mm(g, chunk, j, side, "side_bank")
-                comp_copy(g, chunk)
+        def upper_rows(engine, *rounds):
+            for r in rounds:
+                mic_scale(engine, r, 2, spare[r])
 
-        def widen_pass(engine, k, h):
-            for t in range(PACK):
-                path_widen(engine, k, h, t)
+        def error_round(r):
+            if r + 1 < len(UNITS):
+                mic_scale("gpsimd", r + 1, 0, f"slab{(r + 1) % SLABS}")
+            err(r)
 
-        for j in range(PACK):
-            far_turn(0, j)
-            far_copy(0, j)
-        for j in range(PACK):
-            far_quantise(0, j, j + 1)
-            if j < PACK - 1:
-                for plane in (2 * j, 2 * j + 1):
-                    path_widen("vector", plane // PACK, 0, plane % PACK)
-        widen_pass("scalar", 0, 1)
+        nc.scalar.activation(out=negstep[:], in_=step_bf[:], func=COPY, scale=-1.0)
+        path_widen("vector", 0, range(3))
+        path_widen("vector", 0, [3], half(0))
+        path_widen("vector", 0, [3], half(1))
+        turn_group(0, LOW)
         path_interleave(0, 0)
-        for t in range(2, PACK):
-            path_widen("vector", 1, 0, t)
-        path_quantise(0, 0, 1)
-        for j in range(PACK):
-            for chunk in range(PACK):
-                comp_mm(0, chunk, j, echo, "echo_bank")
-        for chunk in range(PACK):
-            comp_copy(0, chunk)
-        turn_group(1)
-        path_interleave(1, 0)
-        negate_step(0, 0)
-        path_quantise(0, 1, 2)
-        for j in range(PACK):
-            if j == PACK - 1:
-                negate_step(*units[1])
-            mic_scale("vector", 0, 0, j)
-
-        def echo_round(r):
-            g, h = units[r]
-            for j in reversed(range(POOL_ROWS)):
-                mic_scale("gpsimd", *units[r + 1], j)
-            for j in range(PACK):
-                echo_mm(g, h, j)
-                err(g, h, j)
-
-        def rest_of_mic(r):
-            for j in range(POOL_ROWS, PACK):
-                mic_scale("scalar", *units[r + 1], j)
-
-        echo_round(0)
-        rest_of_mic(0)
-        widen_pass("scalar", 1, 1)
-        far_quantise(1, 0, 4)
-        turn_group(2)
-        negate_step(*units[2])
+        far_quantise(0, slice(0, 2))
+        path_quantise(0, half(0))
+        far_quantise(0, slice(2, 4))
         path_interleave(0, 1)
-
-        echo_round(1)
-        rest_of_mic(1)
-        err_interleave("scalar", *units[0])
-        far_quantise(2, 0, 4)
-        turn_group(3)
-        negate_step(*units[3])
+        turn_group(1, HIGH)
+        far_quantise(1)
+        path_quantise(0, half(1))
+        path_widen("scalar", 1, [3], half(1))
+        comp_group(0, LOW)
+        turn_group(2, HIGH)
+        path_widen("vector", 1, range(3))
+        path_widen("vector", 1, [3], half(0))
+        path_interleave(1, 0)
         path_interleave(1, 1)
+        far_quantise(2)
+        path_quantise(1, slice(0, C))
+        comp_group(1, LOW)
+        turn_group(3, HIGH)
+        mic_scale("vector", 0, 0, "slab0")
+        upper_rows("vector", 0, 1, 4)
+        comp_quantise(0)
+        upper_rows("scalar", 5, 2)
 
-        echo_round(2)
-        rest_of_mic(2)
-        err_interleave("scalar", *units[1])
-        far_quantise(3, 0, 4)
-        comp_group(1)
-        negate_step(*units[4])
-        path_quantise(1, 0, 2)
-
-        echo_round(3)
-        rest_of_mic(3)
-        err_interleave("scalar", *units[2])
-        comp_group(2)
-        err_quantise(0, 0, 2)
-        negate_step(*units[5])
-        comp_quantise(0, 2)
-
-        echo_round(4)
-        rest_of_mic(4)
-        comp_group(3)
-        err_interleave("vector", *units[3])
-        negate_step(*units[6])
-        err_quantise(0, 2, 4)
-
+        echo_mm(0, HIGH)
+        error_round(0)
+        far_quantise(3)
+        comp_group(2, LOW)
+        err_interleave("scalar", 0)
+        upper_rows("vector", 7)
+        comp_quantise(1)
+        echo_mm(1, HIGH)
+        error_round(1)
+        echo_mm(2, LOW)
+        err_interleave("scalar", 1)
+        comp_group(3, HIGH)
+        upper_rows("vector", 3)
+        err_quantise(0)
+        error_round(2)
+        echo_mm(3, LOW)
+        err_interleave("scalar", 2)
+        upper_rows("scalar", 6)
+        comp_quantise(2)
+        err_quantise(1)
+        echo_mm(4, HIGH)
+        error_round(3)
+        err_interleave("scalar", 3)
+        comp_quantise(3)
+        err_quantise(2)
+        echo_mm(5, LOW)
+        error_round(4)
         nc.scalar.copy(out=gains[:], in_=gain_bf[:])
-        echo_round(5)
-        rest_of_mic(5)
-        err_interleave("scalar", *units[4])
+        err_interleave("scalar", 4)
+        err_quantise(3)
+        for m in range(3):
+            grad_mm(0, m, range(NG - 1), HIGH + m)
+        for m in range(3):
+            grad_mm(0, m, [NG - 1], HIGH + m)
+        error_round(5)
+        grad_out("scalar", 0, 0)
+        err_interleave("scalar", 5)
+        err_quantise(4)
+        echo_mm(6, LOW)
+        error_round(6)
+        grad_out("scalar", 0, 1)
+        err_interleave("scalar", 6)
+        grad_out("scalar", 0, 2)
+        err_quantise(5)
+        echo_mm(7, LOW)
+        error_round(7)
+        grad_mm(0, 3, range(NG), HIGH + 3)
+        err_interleave("scalar", 7, SPLIT, PASS)
+        grad_out("scalar", 0, 3)
+        err_quantise(6)
+        err_interleave("vector", 7, 0, SPLIT)
+        err_quantise(7)
+        last_banks = [HIGH, HIGH + 1, LOW, LOW + 1]
         for m in range(PACK):
-            grad_mm(0, m, range(NG // 2))
-        err_interleave("scalar", *units[5], SPLIT, PASS)
-        comp_quantise(2, 4)
-        negate_step(*units[7])
-        err_interleave("vector", *units[5], 0, SPLIT)
-
-        echo_round(6)
-        rest_of_mic(6)
-        err_interleave("scalar", *units[6], SPLIT, PASS)
+            grad_mm(1, m, range(NG - 2), last_banks[m])
+        for g in range(NG - 2, NG):
+            for m in range(2):
+                grad_mm(1, m, [g], last_banks[m])
+        for m in range(2, PACK):
+            grad_mm(1, m, range(NG - 2, NG), last_banks[m])
         for m in range(PACK):
-            grad_mm(0, m, range(NG // 2, NG))
-            grad_out("scalar", 0, m)
-        err_quantise(1, 0, 2)
-        err_interleave("vector", *units[6], 0, SPLIT)
-
-        for c in range(2):
-            for j in range(PACK):
-                echo_mm(*units[7], j, c * TAIL, (c + 1) * TAIL)
-                err(*units[7], j, c * TAIL, (c + 1) * TAIL)
-            if c == 0:
-                err_interleave("scalar", *units[7], 0, TAIL)
-                err_quantise(1, 2, 3)
-        err_quantise_columns(*units[7], 0, TAIL)
-        err_interleave("vector", *units[7], TAIL, PASS)
-        for g in range(NG - 1):
-            for m in range(PACK):
-                tail_mm(0, m, g)
-        err_quantise_columns(*units[7], TAIL, PASS)
-        for c in range(2):
-            for m in range(PACK):
-                for g in range(NG - 1 if c == 0 else 0, NG):
-                    tail_mm(c, m, g)
-                tail_out("scalar" if m % 2 == 0 else "vector", c, m)
+            grad_out("vector" if m % 2 == 0 else "scalar", 1, m)

@@ -24,7 +24,17 @@ NG = T // PASS
 NK = K // PASS
 NH = C // PASS
 UNITS = [(g, h) for h in range(NH) for g in range(NG)]
-SLABS = 3
+POOL_COLS = 352
+MIC_BUFFERS = [
+    [f"rows0_{j}" for j in range(PACK)],
+    ["slab1", "rows2_0"],
+    [f"rows1_{j}" for j in range(PACK)],
+    ["rows2_2", "rows3_0"],
+    ["rows3_2", "pair0"],
+    ["pair1", "pair2"],
+    [f"rows0_{j}" for j in range(PACK)],
+    [f"rows1_{j}" for j in range(PACK)],
+]
 SPLIT = 320
 LOW, HIGH = 0, PACK
 
@@ -93,6 +103,9 @@ def tile_echo_nlms_gradient_s11_kernel(
             src = rows.rearrange("p t (c i) -> p c t i", i=4)
             if engine == "vector":
                 nc.vector.tensor_copy(out=dst, in_=src)
+            elif engine == "gpsimd":
+                by_column = rows.rearrange("p t c -> p c t")
+                nc.gpsimd.tensor_scalar(out=grouped, in0=by_column, scalar1=1.0, scalar2=0.0, op0=ALU.mult, op1=ALU.add)
             else:
                 nc.scalar.copy(out=dst, in_=src)
 
@@ -177,11 +190,16 @@ def tile_echo_nlms_gradient_s11_kernel(
 
         mic_scaled, e_rows, e_grouped, echo_bank = {}, {}, {}, {}
 
-        def mic_scale(engine, r, lo, name):
+        def mic_scale(engine, r, lo):
             g, h = UNITS[r]
-            pair = keep.tile([P, 2, PASS], F32, name=name, align_bytes=64)
+            names = MIC_BUFFERS[r]
+            if len(names) == 2:
+                pair = keep.tile([P, 2, PASS], F32, name=names[lo // 2], align_bytes=64)
             for j in range(lo, lo + 2):
-                mic_scaled[r, j] = pair[:, j - lo, :]
+                if len(names) == 2:
+                    mic_scaled[r, j] = pair[:, j - lo, :]
+                else:
+                    mic_scaled[r, j] = keep.tile([P, PASS], F32, name=names[j], align_bytes=64)[:]
                 scale_rows(engine, mic_scaled[r, j], mic_t[g][:, j, half(h)], negstep[:, g, j : j + 1])
 
         def echo_mm(r, first):
@@ -214,7 +232,7 @@ def tile_echo_nlms_gradient_s11_kernel(
 
         def err_interleave(engine, r, lo=0, hi=PASS):
             if r not in e_grouped:
-                e_grouped[r] = keep.tile([P, PASS, PACK], BF16, name=f"slab{r % SLABS}", align_bytes=64)
+                e_grouped[r] = keep.tile([P, PASS, PACK], BF16, name="slab2" if r < len(UNITS) - 1 else "slab1", align_bytes=64)
             interleave(engine, e_grouped[r][:, lo:hi, :], e_rows[r][:, :, lo:hi])
 
         def err_quantise(r):
@@ -222,25 +240,25 @@ def tile_echo_nlms_gradient_s11_kernel(
 
         grad_bank, result = {}, {}
 
-        def grad_mm(h, m, groups, bank):
-            if (h, m) not in grad_bank:
-                grad_bank[h, m] = psum.tile([P, PASS], F32, name=f"bank{bank}")
+        def grad_mm(h, m, groups, bank, lo=0, hi=PASS):
+            if (h, m, lo) not in grad_bank:
+                grad_bank[h, m, lo] = psum.tile([P, hi - lo], F32, name=f"bank{bank}")
             for g in groups:
                 nc.tensor.matmul_mx(
-                    out=grad_bank[h, m][:],
+                    out=grad_bank[h, m, lo][:],
                     lhsT=u_codes[:, g, m * P : (m + 1) * P].bitcast(FP8X4),
                     lhsT_scale=u_scales[:, g, m * P : (m + 1) * P],
-                    rhs=e_codes[:, NG * h + g, :].bitcast(FP8X4),
-                    rhs_scale=e_scales[:, NG * h + g, :],
+                    rhs=e_codes[:, NG * h + g, lo:hi].bitcast(FP8X4),
+                    rhs_scale=e_scales[:, NG * h + g, lo:hi],
                     start=(g == 0),
                     stop=(g == NG - 1),
                 )
 
-        def grad_out(engine, h, m):
+        def grad_out(engine, h, m, lo=0, hi=PASS):
             if h not in result:
                 result[h] = work.tile([P, PACK, PASS], F32, name="wide", align_bytes=64)
-            scale_rows(engine, result[h][:, m, :], grad_bank[h, m][:], gains[:, m : m + 1])
-            nc.sync.dma_start(out=out_v[m][:, half(h)], in_=result[h][:, m, :])
+            scale_rows(engine, result[h][:, m, lo:hi], grad_bank[h, m, lo][:], gains[:, m : m + 1])
+            nc.sync.dma_start(out=out_v[m][:, h * PASS + lo : h * PASS + hi], in_=result[h][:, m, lo:hi])
 
         nc.vector.memset(bscale[:].rearrange("p g n -> p (g n)").bitcast(I32), 0)
         make_identity(nc, ident[:])
@@ -263,16 +281,19 @@ def tile_echo_nlms_gradient_s11_kernel(
             load_mic(g)
         nc.sync.dma_start(out=gain_bf[:], in_=gain.rearrange("(q m) -> q m", m=PACK))
 
-        spare = {0: "rows2_0", 1: "rows2_2", 2: "rows3_0", 3: "rows3_2", 4: "pair4", 5: "pair5", 6: "pair6", 7: "pair7"}
-
-        def upper_rows(engine, *rounds):
-            for r in rounds:
-                mic_scale(engine, r, 2, spare[r])
-
         def error_round(r):
-            if r + 1 < len(UNITS):
-                mic_scale("gpsimd", r + 1, 0, f"slab{(r + 1) % SLABS}")
+            if r == 0:
+                mic_scale("gpsimd", 1, 0)
+            else:
+                err_interleave("gpsimd", r - 1, 0, POOL_COLS)
             err(r)
+
+        def rest_of_interleave(r):
+            err_interleave("scalar", r, POOL_COLS, PASS)
+
+        def mic_unit(engine, r):
+            mic_scale(engine, r, 0)
+            mic_scale(engine, r, 2)
 
         nc.scalar.activation(out=negstep[:], in_=step_bf[:], func=COPY, scale=-1.0)
         path_widen("vector", 0, range(3))
@@ -298,70 +319,73 @@ def tile_echo_nlms_gradient_s11_kernel(
         path_quantise(1, slice(0, C))
         comp_group(1, LOW)
         turn_group(3, HIGH)
-        mic_scale("vector", 0, 0, "slab0")
-        upper_rows("vector", 0, 1, 4)
+        mic_unit("vector", 0)
+        mic_scale("vector", 1, 2)
         comp_quantise(0)
-        upper_rows("scalar", 5, 2)
+        mic_unit("scalar", 4)
+        mic_unit("scalar", 2)
+        mic_scale("scalar", 3, 0)
 
         echo_mm(0, HIGH)
+        echo_mm(1, LOW)
         error_round(0)
         far_quantise(3)
-        comp_group(2, LOW)
-        err_interleave("scalar", 0)
-        upper_rows("vector", 7)
+        comp_mm(2, HIGH)
         comp_quantise(1)
-        echo_mm(1, HIGH)
         error_round(1)
+        rest_of_interleave(0)
+        comp_copy(2)
         echo_mm(2, LOW)
-        err_interleave("scalar", 1)
-        comp_group(3, HIGH)
-        upper_rows("vector", 3)
+        echo_mm(3, HIGH)
         err_quantise(0)
         error_round(2)
-        echo_mm(3, LOW)
-        err_interleave("scalar", 2)
-        upper_rows("scalar", 6)
+        rest_of_interleave(1)
+        mic_scale("scalar", 3, 2)
+        comp_mm(3, LOW)
         comp_quantise(2)
         err_quantise(1)
-        echo_mm(4, HIGH)
         error_round(3)
-        err_interleave("scalar", 3)
-        comp_quantise(3)
-        err_quantise(2)
+        rest_of_interleave(2)
+        comp_copy(3)
+        echo_mm(4, HIGH)
         echo_mm(5, LOW)
+        err_quantise(2)
         error_round(4)
+        rest_of_interleave(3)
+        mic_unit("scalar", 5)
         nc.scalar.copy(out=gains[:], in_=gain_bf[:])
-        err_interleave("scalar", 4)
+        comp_quantise(3)
         err_quantise(3)
-        for m in range(3):
-            grad_mm(0, m, range(NG - 1), HIGH + m)
-        for m in range(3):
-            grad_mm(0, m, [NG - 1], HIGH + m)
+        for m in range(2):
+            grad_mm(0, m, range(NG), HIGH + m)
         error_round(5)
-        grad_out("scalar", 0, 0)
-        err_interleave("scalar", 5)
+        rest_of_interleave(4)
+        mic_unit("scalar", 6)
         err_quantise(4)
         echo_mm(6, LOW)
         error_round(6)
-        grad_out("scalar", 0, 1)
-        err_interleave("scalar", 6)
-        grad_out("scalar", 0, 2)
+        rest_of_interleave(5)
+        mic_unit("scalar", 7)
         err_quantise(5)
         echo_mm(7, LOW)
         error_round(7)
-        grad_mm(0, 3, range(NG), HIGH + 3)
+        rest_of_interleave(6)
+        for m in range(2):
+            grad_out("scalar", 0, m)
+        for m in range(2, PACK):
+            grad_mm(0, m, range(NG), HIGH + m)
         err_interleave("scalar", 7, SPLIT, PASS)
-        grad_out("scalar", 0, 3)
+        for m in range(2, PACK):
+            grad_out("scalar", 0, m)
         err_quantise(6)
         err_interleave("vector", 7, 0, SPLIT)
         err_quantise(7)
-        last_banks = [HIGH, HIGH + 1, LOW, LOW + 1]
-        for m in range(PACK):
-            grad_mm(1, m, range(NG - 2), last_banks[m])
-        for g in range(NG - 2, NG):
-            for m in range(2):
-                grad_mm(1, m, [g], last_banks[m])
-        for m in range(2, PACK):
-            grad_mm(1, m, range(NG - 2, NG), last_banks[m])
-        for m in range(PACK):
+        for m in range(PACK - 1):
+            grad_mm(1, m, range(NG - 2), LOW + m)
+        for m in range(PACK - 1):
+            grad_mm(1, m, range(NG - 2, NG), LOW + m)
             grad_out("vector" if m % 2 == 0 else "scalar", 1, m)
+        grad_mm(1, PACK - 1, range(NG), LOW + 3, 0, PASS // 2)
+        grad_out("scalar", 1, PACK - 1, 0, PASS // 2)
+        grad_mm(1, PACK - 1, range(NG), HIGH, PASS // 2, PASS)
+        grad_out("vector", 1, PACK - 1, PASS // 2, PASS)

@@ -24,7 +24,7 @@ NG = T // PASS
 NK = K // PASS
 NH = C // PASS
 UNITS = [(g, h) for h in range(NH) for g in range(NG)]
-POOL_COLS = 352
+POOL_COLS = [320, 384, 384, 384, 384, 320, 320]
 MIC_BUFFERS = [
     [f"rows0_{j}" for j in range(PACK)],
     ["slab1", "rows2_0"],
@@ -62,17 +62,18 @@ def tile_echo_nlms_gradient_s11_kernel(
         path_v = path_bytes.rearrange("(g p t) c -> g p t c", p=P, t=PACK)
         out_v = out.rearrange("(q m) c -> m q c", m=PACK)
 
-        far_t, mic_t, pbytes = {}, {}, {}
+        far_t, far_pair, mic_t, pbytes = {}, {}, {}, {}
 
         def load_far(g, lo, hi):
             rows = keep.tile([P, hi - lo, K], BF16, name=f"rows{g}_{lo}", align_bytes=64)
             nc.sync.dma_start(out=rows[:], in_=far_v[g][:, lo:hi, :])
+            far_pair[g, lo] = rows[:]
             for j in range(lo, hi):
                 far_t[g, j] = rows[:, j - lo, :]
 
-        def load_mic(g):
-            mic_t[g] = keep.tile([P, PACK, C], BF16, name=f"mic{g}")
-            nc.sync.dma_start(out=mic_t[g][:], in_=mic_v[g])
+        def load_mic(g, h):
+            mic_t[g, h] = keep.tile([P, PACK, PASS], BF16, name=f"mic{g}_{h}")
+            nc.sync.dma_start(out=mic_t[g, h][:], in_=mic_v[g][:, :, half(h)])
 
         def load_path(k, lo, hi):
             planes = keep.tile([P, hi - lo, C], U8, name=f"pbytes{k}_{lo}", align_bytes=64)
@@ -136,7 +137,18 @@ def tile_echo_nlms_gradient_s11_kernel(
         def path_quantise(k, cols):
             quantise(p_codes[:, k, cols], p_scales[:, k, cols], p_grouped[k][:, cols, :].rearrange("p c t -> p (c t)"))
 
-        x_grouped = {}
+        x_grouped, sorted_words = {}, {}
+
+        def far_sort(engine, g, lo):
+            pair = keep.tile([P, 2, NK, 2, P], F32, name=f"sorted{lo}", align_bytes=64)
+            for j in range(lo, lo + 2):
+                sorted_words[g, j] = pair[:, j - lo, :, :, :]
+            dst = pair[:].rearrange("p j k u w -> p (j k) u w")
+            src = far_pair[g, lo].bitcast(F32).rearrange("p j (k w u) -> p (j k) u w", k=NK, u=2)
+            if engine == "vector":
+                nc.vector.tensor_copy(out=dst, in_=src)
+            else:
+                nc.scalar.copy(out=dst, in_=src)
 
         def turn_group(g, first):
             x_grouped[g] = work.tile([P, PACK, NK, P, 2], F32, name="wide", align_bytes=64)
@@ -145,7 +157,11 @@ def tile_echo_nlms_gradient_s11_kernel(
                 bank = psum.tile([P, NK, 2, P], F32, name=f"bank{first + j}")
                 for k in range(NK):
                     for u in range(2):
-                        nc.tensor.transpose(bank[:, k, u, :], words[:, 256 * k + u : 256 * (k + 1) : 2], ident[:])
+                        if (g, j) in sorted_words:
+                            block = sorted_words[g, j][:, k, u, :]
+                        else:
+                            block = words[:, 256 * k + u : 256 * (k + 1) : 2]
+                        nc.tensor.transpose(bank[:, k, u, :], block, ident[:])
                 nc.scalar.copy(out=x_grouped[g][:, j, :, :, :], in_=bank[:].rearrange("p k u n -> p k n u"))
 
         def far_quantise(g, rows=slice(0, PACK)):
@@ -190,17 +206,16 @@ def tile_echo_nlms_gradient_s11_kernel(
 
         mic_scaled, e_rows, e_grouped, echo_bank = {}, {}, {}, {}
 
-        def mic_scale(engine, r, lo):
+        def mic_scale(engine, r, rows):
             g, h = UNITS[r]
             names = MIC_BUFFERS[r]
-            if len(names) == 2:
-                pair = keep.tile([P, 2, PASS], F32, name=names[lo // 2], align_bytes=64)
-            for j in range(lo, lo + 2):
-                if len(names) == 2:
-                    mic_scaled[r, j] = pair[:, j - lo, :]
-                else:
+            for j in rows:
+                if len(names) == PACK:
                     mic_scaled[r, j] = keep.tile([P, PASS], F32, name=names[j], align_bytes=64)[:]
-                scale_rows(engine, mic_scaled[r, j], mic_t[g][:, j, half(h)], negstep[:, g, j : j + 1])
+                elif j % 2 == 0:
+                    pair = keep.tile([P, 2, PASS], F32, name=names[j // 2], align_bytes=64)
+                    mic_scaled[r, j], mic_scaled[r, j + 1] = pair[:, 0, :], pair[:, 1, :]
+                scale_rows(engine, mic_scaled[r, j], mic_t[g, h][:, j, :], negstep[:, g, j : j + 1])
 
         def echo_mm(r, first):
             g, h = UNITS[r]
@@ -273,27 +288,28 @@ def tile_echo_nlms_gradient_s11_kernel(
         for j in range(PACK):
             load_far(1, j, j + 1)
         nc.sync.dma_start(out=bwords[:], in_=basis_words.rearrange("g p n -> p g n"))
+        load_far(2, 0, 2)
+        load_far(2, 2, 4)
         load_path(1, 0, 4)
-        for g in range(2, NG):
-            load_far(g, 0, 2)
-            load_far(g, 2, 4)
-        for g in range(NG):
-            load_mic(g)
+        load_far(3, 0, 2)
+        load_far(3, 2, 4)
+        for g, h in UNITS:
+            load_mic(g, h)
         nc.sync.dma_start(out=gain_bf[:], in_=gain.rearrange("(q m) -> q m", m=PACK))
 
         def error_round(r):
             if r == 0:
-                mic_scale("gpsimd", 1, 0)
+                mic_scale("gpsimd", 1, range(3))
+                mic_scale("scalar", 1, [3])
             else:
-                err_interleave("gpsimd", r - 1, 0, POOL_COLS)
+                err_interleave("gpsimd", r - 1, 0, POOL_COLS[r - 1])
             err(r)
 
         def rest_of_interleave(r):
-            err_interleave("scalar", r, POOL_COLS, PASS)
+            err_interleave("scalar", r, POOL_COLS[r], PASS)
 
         def mic_unit(engine, r):
-            mic_scale(engine, r, 0)
-            mic_scale(engine, r, 2)
+            mic_scale(engine, r, range(PACK))
 
         nc.scalar.activation(out=negstep[:], in_=step_bf[:], func=COPY, scale=-1.0)
         path_widen("vector", 0, range(3))
@@ -307,85 +323,89 @@ def tile_echo_nlms_gradient_s11_kernel(
         path_interleave(0, 1)
         turn_group(1, HIGH)
         far_quantise(1)
-        path_quantise(0, half(1))
-        path_widen("scalar", 1, [3], half(1))
+        far_sort("scalar", 2, 0)
         comp_group(0, LOW)
+        far_sort("vector", 2, 2)
         turn_group(2, HIGH)
-        path_widen("vector", 1, range(3))
-        path_widen("vector", 1, [3], half(0))
+        path_quantise(0, half(1))
+        path_widen("vector", 1, range(PACK), half(0))
+        far_sort("vector", 3, 0)
         path_interleave(1, 0)
-        path_interleave(1, 1)
+        far_sort("vector", 3, 2)
+        path_quantise(1, half(0))
         far_quantise(2)
-        path_quantise(1, slice(0, C))
         comp_group(1, LOW)
         turn_group(3, HIGH)
-        mic_unit("vector", 0)
-        mic_scale("vector", 1, 2)
+        mic_scale("vector", 0, range(2))
         comp_quantise(0)
-        mic_unit("scalar", 4)
-        mic_unit("scalar", 2)
-        mic_scale("scalar", 3, 0)
+        mic_scale("vector", 0, range(2, PACK))
 
-        echo_mm(0, HIGH)
-        echo_mm(1, LOW)
+        echo_mm(0, LOW)
+        echo_mm(1, HIGH)
         error_round(0)
-        far_quantise(3)
-        comp_mm(2, HIGH)
+        path_widen("scalar", 1, range(PACK), half(1))
         comp_quantise(1)
-        error_round(1)
         rest_of_interleave(0)
+        mic_unit("scalar", 2)
+        comp_mm(2, LOW)
+        error_round(1)
         comp_copy(2)
-        echo_mm(2, LOW)
-        echo_mm(3, HIGH)
+        echo_mm(2, HIGH)
         err_quantise(0)
+        far_quantise(3)
+        echo_mm(3, LOW)
         error_round(2)
         rest_of_interleave(1)
-        mic_scale("scalar", 3, 2)
-        comp_mm(3, LOW)
-        comp_quantise(2)
+        mic_unit("scalar", 3)
+        comp_mm(3, HIGH)
+        path_interleave(1, 1)
         err_quantise(1)
+        path_quantise(1, half(1))
         error_round(3)
         rest_of_interleave(2)
+        mic_scale("scalar", 4, range(2))
         comp_copy(3)
-        echo_mm(4, HIGH)
-        echo_mm(5, LOW)
+        mic_scale("scalar", 4, range(2, PACK))
+        echo_mm(4, LOW)
+        echo_mm(5, HIGH)
         err_quantise(2)
+        comp_quantise(2)
         error_round(4)
         rest_of_interleave(3)
         mic_unit("scalar", 5)
         nc.scalar.copy(out=gains[:], in_=gain_bf[:])
-        comp_quantise(3)
         err_quantise(3)
-        for m in range(2):
-            grad_mm(0, m, range(NG), HIGH + m)
+        comp_quantise(3)
+        for groups in (range(NG - 1), [NG - 1]):
+            for m in range(2):
+                grad_mm(0, m, groups, LOW + m)
         error_round(5)
         rest_of_interleave(4)
         mic_unit("scalar", 6)
         err_quantise(4)
-        echo_mm(6, LOW)
+        echo_mm(6, HIGH)
         error_round(6)
         rest_of_interleave(5)
         mic_unit("scalar", 7)
         err_quantise(5)
-        echo_mm(7, LOW)
+        echo_mm(7, HIGH)
         error_round(7)
         rest_of_interleave(6)
-        for m in range(2):
-            grad_out("scalar", 0, m)
+        grad_out("scalar", 0, 0)
         for m in range(2, PACK):
-            grad_mm(0, m, range(NG), HIGH + m)
+            grad_mm(0, m, range(NG), LOW + m)
         err_interleave("scalar", 7, SPLIT, PASS)
-        for m in range(2, PACK):
+        for m in range(1, PACK):
             grad_out("scalar", 0, m)
         err_quantise(6)
         err_interleave("vector", 7, 0, SPLIT)
         err_quantise(7)
         for m in range(PACK - 1):
-            grad_mm(1, m, range(NG - 2), LOW + m)
+            grad_mm(1, m, range(NG - 2), HIGH + m)
         for m in range(PACK - 1):
-            grad_mm(1, m, range(NG - 2, NG), LOW + m)
+            grad_mm(1, m, range(NG - 2, NG), HIGH + m)
             grad_out("vector" if m % 2 == 0 else "scalar", 1, m)
-        grad_mm(1, PACK - 1, range(NG), LOW + 3, 0, PASS // 2)
+        grad_mm(1, PACK - 1, range(NG), HIGH + 3, 0, PASS // 2)
         grad_out("scalar", 1, PACK - 1, 0, PASS // 2)
-        grad_mm(1, PACK - 1, range(NG), HIGH, PASS // 2, PASS)
+        grad_mm(1, PACK - 1, range(NG), LOW, PASS // 2, PASS)
         grad_out("vector", 1, PACK - 1, PASS // 2, PASS)

@@ -289,11 +289,13 @@ def tile_echo_nlms_gradient_s11_kernel(
             load_far(1, j, j + 1)
         nc.sync.dma_start(out=bwords[:], in_=basis_words.rearrange("g p n -> p g n"))
         load_far(2, 0, 2)
+        load_path(1, 0, 2)
         load_far(2, 2, 4)
-        load_path(1, 0, 4)
+        load_path(1, 2, 4)
+        load_mic(*UNITS[0])
         load_far(3, 0, 2)
         load_far(3, 2, 4)
-        for g, h in UNITS:
+        for g, h in UNITS[1:]:
             load_mic(g, h)
         nc.sync.dma_start(out=gain_bf[:], in_=gain.rearrange("(q m) -> q m", m=PACK))
 
@@ -322,28 +324,28 @@ def tile_echo_nlms_gradient_s11_kernel(
         far_quantise(0, slice(2, 4))
         path_interleave(0, 1)
         turn_group(1, HIGH)
-        far_quantise(1)
+        far_quantise(1, slice(0, 2))
+        far_quantise(1, slice(2, 4))
         far_sort("scalar", 2, 0)
         comp_group(0, LOW)
+        path_widen("vector", 1, range(2))
         far_sort("vector", 2, 2)
         turn_group(2, HIGH)
+        path_widen("vector", 1, range(2, PACK), half(0))
         path_quantise(0, half(1))
-        path_widen("vector", 1, range(PACK), half(0))
-        far_sort("vector", 3, 0)
         path_interleave(1, 0)
-        far_sort("vector", 3, 2)
+        mic_scale("vector", 0, range(2))
         path_quantise(1, half(0))
+        mic_scale("vector", 0, range(2, PACK))
         far_quantise(2)
         comp_group(1, LOW)
-        turn_group(3, HIGH)
-        mic_scale("vector", 0, range(2))
         comp_quantise(0)
-        mic_scale("vector", 0, range(2, PACK))
 
-        echo_mm(0, LOW)
-        echo_mm(1, HIGH)
+        echo_mm(0, HIGH)
+        path_widen("scalar", 1, range(2, PACK), half(1))
+        turn_group(3, LOW)
         error_round(0)
-        path_widen("scalar", 1, range(PACK), half(1))
+        echo_mm(1, HIGH)
         comp_quantise(1)
         rest_of_interleave(0)
         mic_unit("scalar", 2)

@@ -50,6 +50,7 @@ def tile_echo_nlms_gradient_s11_kernel(
         ctx.enter_context(tc.manual_schedule())
 
         ident = keep.tile([P, P], F32, name="ident")
+        zeros = keep.tile([P, 2 * P], F32, name="zeros")
         pscale = keep.tile([P, NK, PACK], F32, name="pscale")
         step_bf = keep.tile([P, NG, PACK], BF16, name="step_bf")
         negstep = keep.tile([P, NG, PACK], F32, name="negstep")
@@ -150,7 +151,11 @@ def tile_echo_nlms_gradient_s11_kernel(
             else:
                 nc.scalar.copy(out=dst, in_=src)
 
-        def turn_group(g, first):
+        def warm_up(bank):
+            unread = psum.tile([P, 2 * P], F32, name=f"bank{bank}")
+            nc.tensor.matmul(unread[:], lhsT=ident[:], rhs=zeros[:], start=True, stop=True)
+
+        def turn_group(g, first, warm_after=None, warm_bank=None):
             x_grouped[g] = work.tile([P, PACK, NK, P, 2], F32, name="wide", align_bytes=64)
             for j in range(PACK):
                 words = far_t[g, j].bitcast(F32)
@@ -162,6 +167,8 @@ def tile_echo_nlms_gradient_s11_kernel(
                         else:
                             block = words[:, 256 * k + u : 256 * (k + 1) : 2]
                         nc.tensor.transpose(bank[:, k, u, :], block, ident[:])
+                    if (j, k) == warm_after:
+                        warm_up(warm_bank)
                 nc.scalar.copy(out=x_grouped[g][:, j, :, :, :], in_=bank[:].rearrange("p k u n -> p k n u"))
 
         def far_quantise(g, rows=slice(0, PACK)):
@@ -276,6 +283,7 @@ def tile_echo_nlms_gradient_s11_kernel(
             nc.sync.dma_start(out=out_v[m][:, h * PASS + lo : h * PASS + hi], in_=result[h][:, m, lo:hi])
 
         nc.vector.memset(bscale[:].rearrange("p g n -> p (g n)").bitcast(I32), 0)
+        nc.vector.memset(zeros[:], 0.0)
         make_identity(nc, ident[:])
         nc.scalar.dma_start(out=pscale[:], in_=path_scale.rearrange("(g p t) o -> p g (t o)", p=P, t=PACK))
         nc.scalar.dma_start(out=step_bf[:], in_=step.rearrange("(g p j) -> p g j", p=P, j=PACK))
@@ -317,13 +325,15 @@ def tile_echo_nlms_gradient_s11_kernel(
         path_widen("vector", 0, range(3))
         path_widen("vector", 0, [3], half(0))
         path_widen("vector", 0, [3], half(1))
-        turn_group(0, LOW)
+        for bank in range(HIGH, HIGH + 3):
+            warm_up(bank)
+        turn_group(0, LOW, (2, 0), HIGH + 3)
         path_interleave(0, 0)
         far_quantise(0, slice(0, 2))
         path_quantise(0, half(0))
         far_quantise(0, slice(2, 4))
         path_interleave(0, 1)
-        turn_group(1, HIGH)
+        turn_group(1, HIGH, (1, 0), LOW)
         far_quantise(1, slice(0, 2))
         far_quantise(1, slice(2, 4))
         far_sort("scalar", 2, 0)

@@ -27,8 +27,8 @@ UNITS = [(g, h) for h in range(NH) for g in range(NG)]
 POOL_COLS = [320, 384, 384, 384, 384, 320, 320]
 MIC_BUFFERS = [
     [f"rows0_{j}" for j in range(PACK)],
-    ["slab1", "rows2_0"],
     [f"rows1_{j}" for j in range(PACK)],
+    ["rows2_0", "pair3"],
     ["rows2_2", "rows3_0"],
     ["rows3_2", "pair0"],
     ["pair1", "pair2"],
@@ -36,6 +36,7 @@ MIC_BUFFERS = [
     [f"rows1_{j}" for j in range(PACK)],
 ]
 SPLIT = 320
+POOL_PATH = 352
 LOW, HIGH = 0, PACK
 
 
@@ -63,12 +64,11 @@ def tile_echo_nlms_gradient_s11_kernel(
         path_v = path_bytes.rearrange("(g p t) c -> g p t c", p=P, t=PACK)
         out_v = out.rearrange("(q m) c -> m q c", m=PACK)
 
-        far_t, far_pair, mic_t, pbytes = {}, {}, {}, {}
+        far_t, mic_t, pbytes = {}, {}, {}
 
         def load_far(g, lo, hi):
             rows = keep.tile([P, hi - lo, K], BF16, name=f"rows{g}_{lo}", align_bytes=64)
             nc.sync.dma_start(out=rows[:], in_=far_v[g][:, lo:hi, :])
-            far_pair[g, lo] = rows[:]
             for j in range(lo, hi):
                 far_t[g, j] = rows[:, j - lo, :]
 
@@ -130,26 +130,16 @@ def tile_echo_nlms_gradient_s11_kernel(
             for t in planes:
                 scale_rows(engine, p_rows[k][:, t, cols], pbytes[k, t][:, cols].bitcast(FP8), pscale[:, k, t : t + 1])
 
-        def path_interleave(k, h):
-            if k not in p_grouped:
-                p_grouped[k] = work.tile([P, C, PACK], BF16, name="p_grouped", align_bytes=64)
-            interleave("vector", p_grouped[k][:, half(h), :], p_rows[k][:, :, half(h)])
+        def path_interleave(engine, k, h, lo=0, hi=PASS):
+            if (k, h) not in p_grouped:
+                name = "slab1" if (k, h) == (1, 1) else f"p_grouped{k}_{h}"
+                p_grouped[k, h] = keep.tile([P, PASS, PACK], BF16, name=name, align_bytes=64)
+            interleave(engine, p_grouped[k, h][:, lo:hi, :], p_rows[k][:, :, h * PASS + lo : h * PASS + hi])
 
-        def path_quantise(k, cols):
-            quantise(p_codes[:, k, cols], p_scales[:, k, cols], p_grouped[k][:, cols, :].rearrange("p c t -> p (c t)"))
+        def path_quantise(k, h):
+            quantise(p_codes[:, k, half(h)], p_scales[:, k, half(h)], p_grouped[k, h][:].rearrange("p c t -> p (c t)"))
 
-        x_grouped, sorted_words = {}, {}
-
-        def far_sort(engine, g, lo):
-            pair = keep.tile([P, 2, NK, 2, P], F32, name=f"sorted{lo}", align_bytes=64)
-            for j in range(lo, lo + 2):
-                sorted_words[g, j] = pair[:, j - lo, :, :, :]
-            dst = pair[:].rearrange("p j k u w -> p (j k) u w")
-            src = far_pair[g, lo].bitcast(F32).rearrange("p j (k w u) -> p (j k) u w", k=NK, u=2)
-            if engine == "vector":
-                nc.vector.tensor_copy(out=dst, in_=src)
-            else:
-                nc.scalar.copy(out=dst, in_=src)
+        x_grouped = {}
 
         def warm_up(bank):
             unread = psum.tile([P, 2 * P], F32, name=f"bank{bank}")
@@ -162,11 +152,7 @@ def tile_echo_nlms_gradient_s11_kernel(
                 bank = psum.tile([P, NK, 2, P], F32, name=f"bank{first + j}")
                 for k in range(NK):
                     for u in range(2):
-                        if (g, j) in sorted_words:
-                            block = sorted_words[g, j][:, k, u, :]
-                        else:
-                            block = words[:, 256 * k + u : 256 * (k + 1) : 2]
-                        nc.tensor.transpose(bank[:, k, u, :], block, ident[:])
+                        nc.tensor.transpose(bank[:, k, u, :], words[:, 256 * k + u : 256 * (k + 1) : 2], ident[:])
                     if (j, k) == warm_after:
                         warm_up(warm_bank)
                 nc.scalar.copy(out=x_grouped[g][:, j, :, :, :], in_=bank[:].rearrange("p k u n -> p k n u"))
@@ -296,21 +282,21 @@ def tile_echo_nlms_gradient_s11_kernel(
         for j in range(PACK):
             load_far(1, j, j + 1)
         nc.sync.dma_start(out=bwords[:], in_=basis_words.rearrange("g p n -> p g n"))
-        load_far(2, 0, 2)
         load_path(1, 0, 2)
-        load_far(2, 2, 4)
         load_path(1, 2, 4)
+        load_far(2, 0, 2)
+        load_far(2, 2, 4)
         load_mic(*UNITS[0])
+        load_mic(*UNITS[1])
         load_far(3, 0, 2)
         load_far(3, 2, 4)
-        for g, h in UNITS[1:]:
+        for g, h in UNITS[2:]:
             load_mic(g, h)
         nc.sync.dma_start(out=gain_bf[:], in_=gain.rearrange("(q m) -> q m", m=PACK))
 
         def error_round(r):
             if r == 0:
-                mic_scale("gpsimd", 1, range(3))
-                mic_scale("scalar", 1, [3])
+                path_interleave("gpsimd", 1, 1, 0, POOL_PATH)
             else:
                 err_interleave("gpsimd", r - 1, 0, POOL_COLS[r - 1])
             err(r)
@@ -323,42 +309,44 @@ def tile_echo_nlms_gradient_s11_kernel(
 
         nc.scalar.activation(out=negstep[:], in_=step_bf[:], func=COPY, scale=-1.0)
         path_widen("vector", 0, range(3))
-        path_widen("vector", 0, [3], half(0))
-        path_widen("vector", 0, [3], half(1))
+        path_widen("scalar", 0, [3])
         for bank in range(HIGH, HIGH + 3):
             warm_up(bank)
         turn_group(0, LOW, (2, 0), HIGH + 3)
-        path_interleave(0, 0)
+        path_interleave("vector", 0, 0)
+        path_interleave("vector", 0, 1)
         far_quantise(0, slice(0, 2))
-        path_quantise(0, half(0))
+        path_quantise(0, 0)
         far_quantise(0, slice(2, 4))
-        path_interleave(0, 1)
+        path_quantise(0, 1)
         turn_group(1, HIGH, (1, 0), LOW)
         far_quantise(1, slice(0, 2))
+        path_widen("vector", 1, [0], half(0))
         far_quantise(1, slice(2, 4))
-        far_sort("scalar", 2, 0)
+        path_widen("scalar", 1, [0], half(1))
         comp_group(0, LOW)
-        path_widen("vector", 1, range(2))
-        far_sort("vector", 2, 2)
+        path_widen("vector", 1, range(1, PACK), half(0))
+        path_widen("vector", 1, range(1, PACK), half(1))
         turn_group(2, HIGH)
-        path_widen("vector", 1, range(2, PACK), half(0))
-        path_quantise(0, half(1))
-        path_interleave(1, 0)
-        mic_scale("vector", 0, range(2))
-        path_quantise(1, half(0))
-        mic_scale("vector", 0, range(2, PACK))
-        far_quantise(2)
+        path_interleave("vector", 1, 0)
+        far_quantise(2, slice(0, 2))
+        path_quantise(1, 0)
+        mic_scale("vector", 0, range(PACK))
+        far_quantise(2, slice(2, 4))
         comp_group(1, LOW)
         comp_quantise(0)
 
         echo_mm(0, HIGH)
-        path_widen("scalar", 1, range(2, PACK), half(1))
+        mic_unit("scalar", 1)
         turn_group(3, LOW)
         error_round(0)
         echo_mm(1, HIGH)
+        path_interleave("vector", 1, 1, POOL_PATH, PASS)
+        mic_unit("vector", 2)
+        path_quantise(1, 1)
         comp_quantise(1)
         rest_of_interleave(0)
-        mic_unit("scalar", 2)
+        mic_unit("scalar", 3)
         comp_mm(2, LOW)
         error_round(1)
         comp_copy(2)
@@ -368,16 +356,12 @@ def tile_echo_nlms_gradient_s11_kernel(
         echo_mm(3, LOW)
         error_round(2)
         rest_of_interleave(1)
-        mic_unit("scalar", 3)
+        mic_unit("scalar", 4)
         comp_mm(3, HIGH)
-        path_interleave(1, 1)
         err_quantise(1)
-        path_quantise(1, half(1))
         error_round(3)
         rest_of_interleave(2)
-        mic_scale("scalar", 4, range(2))
         comp_copy(3)
-        mic_scale("scalar", 4, range(2, PACK))
         echo_mm(4, LOW)
         echo_mm(5, HIGH)
         err_quantise(2)

@@ -24,7 +24,7 @@ NG = T // PASS
 NK = K // PASS
 NH = C // PASS
 UNITS = [(g, h) for h in range(NH) for g in range(NG)]
-POOL_COLS = [320, 384, 384, 384, 384, 320, 320]
+POOL_COLS = [320, 384, 352, 384, 384, 320, 320]
 MIC_BUFFERS = [
     [f"rows0_{j}" for j in range(PACK)],
     [f"rows1_{j}" for j in range(PACK)],
@@ -64,11 +64,12 @@ def tile_echo_nlms_gradient_s11_kernel(
         path_v = path_bytes.rearrange("(g p t) c -> g p t c", p=P, t=PACK)
         out_v = out.rearrange("(q m) c -> m q c", m=PACK)
 
-        far_t, mic_t, pbytes = {}, {}, {}
+        far_t, far_pair, mic_t, pbytes = {}, {}, {}, {}
 
         def load_far(g, lo, hi):
             rows = keep.tile([P, hi - lo, K], BF16, name=f"rows{g}_{lo}", align_bytes=64)
             nc.sync.dma_start(out=rows[:], in_=far_v[g][:, lo:hi, :])
+            far_pair[g, lo] = rows[:]
             for j in range(lo, hi):
                 far_t[g, j] = rows[:, j - lo, :]
 
@@ -139,7 +140,13 @@ def tile_echo_nlms_gradient_s11_kernel(
         def path_quantise(k, h):
             quantise(p_codes[:, k, half(h)], p_scales[:, k, half(h)], p_grouped[k, h][:].rearrange("p c t -> p (c t)"))
 
-        x_grouped = {}
+        x_grouped, sorted_words = {}, {}
+
+        def far_sort(g, lo):
+            pair = keep.tile([P, 2, NK, 2, P], F32, name="sorted", align_bytes=64)
+            sorted_words[g, lo], sorted_words[g, lo + 1] = pair[:, 0, :, :, :], pair[:, 1, :, :, :]
+            words = far_pair[g, lo].bitcast(F32).rearrange("p j (k w u) -> p (j k) u w", k=NK, u=2)
+            nc.scalar.copy(out=pair[:].rearrange("p j k u w -> p (j k) u w"), in_=words)
 
         def warm_up(bank):
             unread = psum.tile([P, 2 * P], F32, name=f"bank{bank}")
@@ -152,7 +159,11 @@ def tile_echo_nlms_gradient_s11_kernel(
                 bank = psum.tile([P, NK, 2, P], F32, name=f"bank{first + j}")
                 for k in range(NK):
                     for u in range(2):
-                        nc.tensor.transpose(bank[:, k, u, :], words[:, 256 * k + u : 256 * (k + 1) : 2], ident[:])
+                        if (g, j) in sorted_words:
+                            block = sorted_words[g, j][:, k, u, :]
+                        else:
+                            block = words[:, 256 * k + u : 256 * (k + 1) : 2]
+                        nc.tensor.transpose(bank[:, k, u, :], block, ident[:])
                     if (j, k) == warm_after:
                         warm_up(warm_bank)
                 nc.scalar.copy(out=x_grouped[g][:, j, :, :, :], in_=bank[:].rearrange("p k u n -> p k n u"))
@@ -243,8 +254,8 @@ def tile_echo_nlms_gradient_s11_kernel(
                 e_grouped[r] = keep.tile([P, PASS, PACK], BF16, name="slab2" if r < len(UNITS) - 1 else "slab1", align_bytes=64)
             interleave(engine, e_grouped[r][:, lo:hi, :], e_rows[r][:, :, lo:hi])
 
-        def err_quantise(r):
-            quantise(e_codes[:, r, :], e_scales[:, r, :], e_grouped[r][:].rearrange("p c j -> p (c j)"))
+        def err_quantise(r, cols=slice(0, PASS)):
+            quantise(e_codes[:, r, cols], e_scales[:, r, cols], e_grouped[r][:, cols, :].rearrange("p c j -> p (c j)"))
 
         grad_bank, result = {}, {}
 
@@ -287,8 +298,8 @@ def tile_echo_nlms_gradient_s11_kernel(
         load_far(2, 0, 2)
         load_far(2, 2, 4)
         load_mic(*UNITS[0])
-        load_mic(*UNITS[1])
         load_far(3, 0, 2)
+        load_mic(*UNITS[1])
         load_far(3, 2, 4)
         for g, h in UNITS[2:]:
             load_mic(g, h)
@@ -337,8 +348,10 @@ def tile_echo_nlms_gradient_s11_kernel(
         comp_quantise(0)
 
         echo_mm(0, HIGH)
-        mic_unit("scalar", 1)
+        far_sort(3, 0)
+        mic_scale("scalar", 1, range(2))
         turn_group(3, LOW)
+        mic_scale("scalar", 1, range(2, PACK))
         error_round(0)
         echo_mm(1, HIGH)
         path_interleave("vector", 1, 1, POOL_PATH, PASS)
@@ -378,6 +391,7 @@ def tile_echo_nlms_gradient_s11_kernel(
         error_round(5)
         rest_of_interleave(4)
         mic_unit("scalar", 6)
+        grad_out("scalar", 0, 0)
         err_quantise(4)
         echo_mm(6, HIGH)
         error_round(6)
@@ -387,14 +401,15 @@ def tile_echo_nlms_gradient_s11_kernel(
         echo_mm(7, HIGH)
         error_round(7)
         rest_of_interleave(6)
-        grad_out("scalar", 0, 0)
+        grad_out("scalar", 0, 1)
         for m in range(2, PACK):
             grad_mm(0, m, range(NG), LOW + m)
         err_interleave("scalar", 7, SPLIT, PASS)
-        for m in range(1, PACK):
+        for m in range(2, PACK):
             grad_out("scalar", 0, m)
-        err_quantise(6)
+        err_quantise(6, slice(0, PASS // 2))
         err_interleave("vector", 7, 0, SPLIT)
+        err_quantise(6, slice(PASS // 2, PASS))
         err_quantise(7)
         for m in range(PACK - 1):
             grad_mm(1, m, range(NG - 2), HIGH + m)

@@ -37,6 +37,7 @@ MIC_BUFFERS = [
 ]
 SPLIT = 320
 POOL_PATH = 352
+MOVING_CODES, MOVING_SCALES, FIXED_CODES, FIXED_SCALES = 0, 128, 64, 192
 LOW, HIGH = 0, PACK
 
 
@@ -50,6 +51,11 @@ def tile_echo_nlms_gradient_s11_kernel(
         psum = ctx.enter_context(tc.psum_pool(name="psum", bufs=1))
         ctx.enter_context(tc.manual_schedule())
 
+        def operand(name, shape, dtype, size, shift):
+            skip, count = shift // size, shape[0] * shape[1]
+            flat = keep.tile([P, skip + count], dtype, name=name, align_bytes=256)
+            return flat[:, skip:].rearrange("p (a b) -> p a b", a=shape[0])
+
         ident = keep.tile([P, P], F32, name="ident")
         zeros = keep.tile([P, 2 * P], F32, name="zeros")
         pscale = keep.tile([P, NK, PACK], F32, name="pscale")
@@ -57,8 +63,8 @@ def tile_echo_nlms_gradient_s11_kernel(
         negstep = keep.tile([P, NG, PACK], F32, name="negstep")
         gain_bf = keep.tile([P, PACK], BF16, name="gain_bf")
         gains = keep.tile([P, PACK], F32, name="gains")
-        bscale = keep.tile([P, NK, R], U8, name="bscale", align_bytes=64)
-        bwords = keep.tile([P, NK, 2 * R], U8, name="bwords", align_bytes=64)
+        bscale = operand("bscale", [NK, R], U8, 1, MOVING_SCALES)
+        bwords = operand("bwords", [NK, 2 * R], U8, 1, MOVING_CODES)
         far_v = far.rearrange("(g p j) k -> g p j k", p=P, j=PACK)
         mic_v = mic.rearrange("(g p j) c -> g p j c", p=P, j=PACK)
         path_v = path_bytes.rearrange("(g p t) c -> g p t c", p=P, t=PACK)
@@ -89,14 +95,14 @@ def tile_echo_nlms_gradient_s11_kernel(
                 in_=basis_scales[:, 4 * q : 4 * q + 4, :].bitcast(I32).rearrange("g q n -> q g n"),
             )
 
-        x_codes = [keep.tile([P, PACK, NK, P], U32, name=f"x_codes{g}", align_bytes=64) for g in range(NG)]
-        x_scales = [keep.tile([P, PACK, NK, P], U8, name=f"x_scales{g}", align_bytes=64) for g in range(NG)]
-        p_codes = keep.tile([P, NK, C], U32, name="p_codes", align_bytes=64)
-        p_scales = keep.tile([P, NK, C], U8, name="p_scales", align_bytes=64)
-        u_codes = keep.tile([P, NG, R], U32, name="u_codes", align_bytes=64)
-        u_scales = keep.tile([P, NG, R], U8, name="u_scales", align_bytes=64)
-        e_codes = keep.tile([P, len(UNITS), PASS], U32, name="e_codes", align_bytes=64)
-        e_scales = keep.tile([P, len(UNITS), PASS], U8, name="e_scales", align_bytes=64)
+        x_codes = [operand(f"x_codes{g}", [PACK, NK * P], U32, 4, FIXED_CODES).rearrange("p j (k n) -> p j k n", k=NK) for g in range(NG)]
+        x_scales = [operand(f"x_scales{g}", [PACK, NK * P], U8, 1, FIXED_SCALES).rearrange("p j (k n) -> p j k n", k=NK) for g in range(NG)]
+        p_codes = operand("p_codes", [NK, C], U32, 4, MOVING_CODES)
+        p_scales = operand("p_scales", [NK, C], U8, 1, MOVING_SCALES)
+        u_codes = operand("u_codes", [NG, R], U32, 4, FIXED_CODES)
+        u_scales = operand("u_scales", [NG, R], U8, 1, FIXED_SCALES)
+        e_codes = operand("e_codes", [len(UNITS), PASS], U32, 4, MOVING_CODES)
+        e_scales = operand("e_scales", [len(UNITS), PASS], U8, 1, MOVING_SCALES)
 
         def half(h):
             return slice(h * PASS, (h + 1) * PASS)
@@ -279,7 +285,7 @@ def tile_echo_nlms_gradient_s11_kernel(
             scale_rows(engine, result[h][:, m, lo:hi], grad_bank[h, m, lo][:], gains[:, m : m + 1])
             nc.sync.dma_start(out=out_v[m][:, h * PASS + lo : h * PASS + hi], in_=result[h][:, m, lo:hi])
 
-        nc.vector.memset(bscale[:].rearrange("p g n -> p (g n)").bitcast(I32), 0)
+        nc.vector.memset(bscale.rearrange("p g n -> p (g n)").bitcast(I32), 0)
         nc.vector.memset(zeros[:], 0.0)
         make_identity(nc, ident[:])
         nc.scalar.dma_start(out=pscale[:], in_=path_scale.rearrange("(g p t) o -> p g (t o)", p=P, t=PACK))
@@ -292,7 +298,7 @@ def tile_echo_nlms_gradient_s11_kernel(
             load_basis_scales(q)
         for j in range(PACK):
             load_far(1, j, j + 1)
-        nc.sync.dma_start(out=bwords[:], in_=basis_words.rearrange("g p n -> p g n"))
+        nc.sync.dma_start(out=bwords, in_=basis_words.rearrange("g p n -> p g n"))
         load_path(1, 0, 2)
         load_path(1, 2, 4)
         load_far(2, 0, 2)

@@ -38,6 +38,7 @@ MIC_BUFFERS = [
 SPLIT = 320
 POOL_PATH = 352
 MOVING_CODES, MOVING_SCALES, FIXED_CODES, FIXED_SCALES = 0, 128, 64, 192
+ROW_PAD = 32
 LOW, HIGH = 0, PACK
 
 
@@ -133,7 +134,7 @@ def tile_echo_nlms_gradient_s11_kernel(
 
         def path_widen(engine, k, planes, cols=slice(0, C)):
             if k not in p_rows:
-                p_rows[k] = work.tile([P, PACK, C], BF16, name="p_rows")
+                p_rows[k] = work.tile([P, PACK, C + ROW_PAD], BF16, name="p_rows", align_bytes=256)
             for t in planes:
                 scale_rows(engine, p_rows[k][:, t, cols], pbytes[k, t][:, cols].bitcast(FP8), pscale[:, k, t : t + 1])
 
@@ -244,10 +245,10 @@ def tile_echo_nlms_gradient_s11_kernel(
 
         def err(r):
             g, h = UNITS[r]
-            e_rows[r] = work.tile([P, PACK, PASS], BF16, name="e_rows")
+            e_rows[r] = work.tile([P, PACK, PASS + ROW_PAD], BF16, name="e_rows", align_bytes=256)
             for j in range(PACK):
                 nc.vector.scalar_tensor_tensor(
-                    out=e_rows[r][:, j, :],
+                    out=e_rows[r][:, j, :PASS],
                     in0=echo_bank[r, j][:],
                     scalar=negstep[:, g, j : j + 1],
                     in1=mic_scaled[r, j],

@@ -38,6 +38,7 @@ MIC_BUFFERS = [
 SPLIT = 320
 POOL_PATH = 352
 MOVING_CODES, MOVING_SCALES, FIXED_CODES, FIXED_SCALES = 0, 128, 64, 192
+IDENTITY = 64
 ROW_PAD = 32
 LOW, HIGH = 0, PACK
 
@@ -57,7 +58,7 @@ def tile_echo_nlms_gradient_s11_kernel(
             flat = keep.tile([P, skip + count], dtype, name=name, align_bytes=256)
             return flat[:, skip:].rearrange("p (a b) -> p a b", a=shape[0])
 
-        ident = keep.tile([P, P], F32, name="ident")
+        ident = operand("ident", [1, P], F32, 4, IDENTITY)[:, 0, :]
         zeros = keep.tile([P, 2 * P], F32, name="zeros")
         pscale = keep.tile([P, NK, PACK], F32, name="pscale")
         step_bf = keep.tile([P, NG, PACK], BF16, name="step_bf")
@@ -74,7 +75,7 @@ def tile_echo_nlms_gradient_s11_kernel(
         far_t, far_pair, mic_t, pbytes = {}, {}, {}, {}
 
         def load_far(g, lo, hi):
-            rows = keep.tile([P, hi - lo, K], BF16, name=f"rows{g}_{lo}", align_bytes=64)
+            rows = keep.tile([P, hi - lo, K], BF16, name=f"rows{g}_{lo}", align_bytes=256)
             nc.sync.dma_start(out=rows[:], in_=far_v[g][:, lo:hi, :])
             far_pair[g, lo] = rows[:]
             for j in range(lo, hi):
@@ -150,14 +151,14 @@ def tile_echo_nlms_gradient_s11_kernel(
         x_grouped, sorted_words = {}, {}
 
         def far_sort(g, lo):
-            pair = keep.tile([P, 2, NK, 2, P], F32, name="sorted", align_bytes=64)
+            pair = keep.tile([P, 2, NK, 2, P], F32, name="sorted", align_bytes=256)
             sorted_words[g, lo], sorted_words[g, lo + 1] = pair[:, 0, :, :, :], pair[:, 1, :, :, :]
             words = far_pair[g, lo].bitcast(F32).rearrange("p j (k w u) -> p (j k) u w", k=NK, u=2)
             nc.scalar.copy(out=pair[:].rearrange("p j k u w -> p (j k) u w"), in_=words)
 
         def warm_up(bank):
             unread = psum.tile([P, 2 * P], F32, name=f"bank{bank}")
-            nc.tensor.matmul(unread[:], lhsT=ident[:], rhs=zeros[:], start=True, stop=True)
+            nc.tensor.matmul(unread[:], lhsT=ident, rhs=zeros[:], start=True, stop=True)
 
         def turn_group(g, first, warm_after=None, warm_bank=None):
             x_grouped[g] = work.tile([P, PACK, NK, P, 2], F32, name="wide", align_bytes=64)
@@ -170,7 +171,7 @@ def tile_echo_nlms_gradient_s11_kernel(
                             block = sorted_words[g, j][:, k, u, :]
                         else:
                             block = words[:, 256 * k + u : 256 * (k + 1) : 2]
-                        nc.tensor.transpose(bank[:, k, u, :], block, ident[:])
+                        nc.tensor.transpose(bank[:, k, u, :], block, ident)
                     if (j, k) == warm_after:
                         warm_up(warm_bank)
                 nc.scalar.copy(out=x_grouped[g][:, j, :, :, :], in_=bank[:].rearrange("p k u n -> p k n u"))
@@ -222,9 +223,9 @@ def tile_echo_nlms_gradient_s11_kernel(
             names = MIC_BUFFERS[r]
             for j in rows:
                 if len(names) == PACK:
-                    mic_scaled[r, j] = keep.tile([P, PASS], F32, name=names[j], align_bytes=64)[:]
+                    mic_scaled[r, j] = keep.tile([P, PASS], F32, name=names[j], align_bytes=256)[:]
                 elif j % 2 == 0:
-                    pair = keep.tile([P, 2, PASS], F32, name=names[j // 2], align_bytes=64)
+                    pair = keep.tile([P, 2, PASS], F32, name=names[j // 2], align_bytes=256)
                     mic_scaled[r, j], mic_scaled[r, j + 1] = pair[:, 0, :], pair[:, 1, :]
                 scale_rows(engine, mic_scaled[r, j], mic_t[g, h][:, j, :], negstep[:, g, j : j + 1])
 
@@ -288,7 +289,7 @@ def tile_echo_nlms_gradient_s11_kernel(
 
         nc.vector.memset(bscale.rearrange("p g n -> p (g n)").bitcast(I32), 0)
         nc.vector.memset(zeros[:], 0.0)
-        make_identity(nc, ident[:])
+        make_identity(nc, ident)
         nc.scalar.dma_start(out=pscale[:], in_=path_scale.rearrange("(g p t) o -> p g (t o)", p=P, t=PACK))
         nc.scalar.dma_start(out=step_bf[:], in_=step.rearrange("(g p j) -> p g j", p=P, j=PACK))
         load_path(0, 0, 2)

@@ -24,23 +24,15 @@ NG = T // PASS
 NK = K // PASS
 NH = C // PASS
 UNITS = [(g, h) for h in range(NH) for g in range(NG)]
-POOL_COLS = [320, 384, 352, 384, 384, 320, 320]
-MIC_BUFFERS = [
-    [f"rows0_{j}" for j in range(PACK)],
-    [f"rows1_{j}" for j in range(PACK)],
-    ["rows2_0", "pair3"],
-    ["rows2_2", "rows3_0"],
-    ["rows3_2", "pair0"],
-    ["pair1", "pair2"],
-    [f"rows0_{j}" for j in range(PACK)],
-    [f"rows1_{j}" for j in range(PACK)],
-]
+POOL_COLS = [384, 384, 384, 384, 384, 384, 288]
+E_BUFFERS = ["p_rows1", "x_pair1_0"] * 3 + ["x_pair1_0", "p_grouped0_0"]
 SPLIT = 320
-POOL_PATH = 352
+POOL_PATH = 384
 MOVING_CODES, MOVING_SCALES, FIXED_CODES, FIXED_SCALES = 0, 128, 64, 192
 IDENTITY = 64
 ROW_PAD = 32
 LOW, HIGH = 0, PACK
+FRONT, BACK = range(2), range(2, PACK)
 
 
 def tile_echo_nlms_gradient_s11_kernel(
@@ -49,7 +41,7 @@ def tile_echo_nlms_gradient_s11_kernel(
     nc = tc.nc
     with ExitStack() as ctx:
         keep = ctx.enter_context(tc.tile_pool(name="keep", bufs=1))
-        work = ctx.enter_context(tc.tile_pool(name="work", bufs=2))
+        work = ctx.enter_context(tc.tile_pool(name="work", bufs=3))
         psum = ctx.enter_context(tc.psum_pool(name="psum", bufs=1))
         ctx.enter_context(tc.manual_schedule())
 
@@ -82,7 +74,7 @@ def tile_echo_nlms_gradient_s11_kernel(
                 far_t[g, j] = rows[:, j - lo, :]
 
         def load_mic(g, h):
-            mic_t[g, h] = keep.tile([P, PACK, PASS], BF16, name=f"mic{g}_{h}")
+            mic_t[g, h] = keep.tile([P, PACK, PASS], BF16, name=f"mic{g}_{h}", align_bytes=256)
             nc.sync.dma_start(out=mic_t[g, h][:], in_=mic_v[g][:, :, half(h)])
 
         def load_path(k, lo, hi):
@@ -97,8 +89,13 @@ def tile_echo_nlms_gradient_s11_kernel(
                 in_=basis_scales[:, 4 * q : 4 * q + 4, :].bitcast(I32).rearrange("g q n -> q g n"),
             )
 
-        x_codes = [operand(f"x_codes{g}", [PACK, NK * P], U32, 4, FIXED_CODES).rearrange("p j (k n) -> p j k n", k=NK) for g in range(NG)]
-        x_scales = [operand(f"x_scales{g}", [PACK, NK * P], U8, 1, FIXED_SCALES).rearrange("p j (k n) -> p j k n", k=NK) for g in range(NG)]
+        x_codes, x_scales = [], []
+        for g in range(NG):
+            codes = operand(f"x_codes{g}", [PACK, NK * P], U32, 4, FIXED_CODES)
+            x_codes.append(codes.rearrange("p j (k n) -> p j k n", k=NK))
+        for g in range(NG):
+            scales = operand(f"x_scales{g}", [PACK, NK * P], U8, 1, FIXED_SCALES)
+            x_scales.append(scales.rearrange("p j (k n) -> p j k n", k=NK))
         p_codes = operand("p_codes", [NK, C], U32, 4, MOVING_CODES)
         p_scales = operand("p_scales", [NK, C], U8, 1, MOVING_SCALES)
         u_codes = operand("u_codes", [NG, R], U32, 4, FIXED_CODES)
@@ -126,8 +123,6 @@ def tile_echo_nlms_gradient_s11_kernel(
         def scale_rows(engine, dst, src, scale):
             if engine == "vector":
                 nc.vector.tensor_scalar(out=dst, in0=src, scalar1=scale, scalar2=None, op0=ALU.mult)
-            elif engine == "gpsimd":
-                nc.gpsimd.tensor_scalar(out=dst, in0=src, scalar1=scale, scalar2=0.0, op0=ALU.mult, op1=ALU.add)
             else:
                 nc.scalar.activation(out=dst, in_=src, func=COPY, scale=scale)
 
@@ -135,36 +130,36 @@ def tile_echo_nlms_gradient_s11_kernel(
 
         def path_widen(engine, k, planes, cols=slice(0, C)):
             if k not in p_rows:
-                p_rows[k] = work.tile([P, PACK, C + ROW_PAD], BF16, name="p_rows", align_bytes=256)
+                p_rows[k] = keep.tile([P, PACK, C + ROW_PAD], BF16, name=f"p_rows{k}", align_bytes=256)
             for t in planes:
                 scale_rows(engine, p_rows[k][:, t, cols], pbytes[k, t][:, cols].bitcast(FP8), pscale[:, k, t : t + 1])
 
         def path_interleave(engine, k, h, lo=0, hi=PASS):
             if (k, h) not in p_grouped:
-                name = "slab1" if (k, h) == (1, 1) else f"p_grouped{k}_{h}"
-                p_grouped[k, h] = keep.tile([P, PASS, PACK], BF16, name=name, align_bytes=64)
+                name = "x_pair0_0" if (k, h) == (1, 1) else f"p_grouped{k}_{h}"
+                p_grouped[k, h] = keep.tile([P, PASS, PACK], BF16, name=name, align_bytes=256)
             interleave(engine, p_grouped[k, h][:, lo:hi, :], p_rows[k][:, :, h * PASS + lo : h * PASS + hi])
 
         def path_quantise(k, h):
             quantise(p_codes[:, k, half(h)], p_scales[:, k, half(h)], p_grouped[k, h][:].rearrange("p c t -> p (c t)"))
 
-        x_grouped, sorted_words = {}, {}
+        x_grouped, sorted_words, turned = {}, {}, {}
 
-        def far_sort(g, lo):
-            pair = keep.tile([P, 2, NK, 2, P], F32, name="sorted", align_bytes=256)
+        def far_sort(engine, g, lo):
+            pair = keep.tile([P, 2, NK, 2, P], F32, name=f"sorted{lo}", align_bytes=256)
             sorted_words[g, lo], sorted_words[g, lo + 1] = pair[:, 0, :, :, :], pair[:, 1, :, :, :]
             words = far_pair[g, lo].bitcast(F32).rearrange("p j (k w u) -> p (j k) u w", k=NK, u=2)
-            nc.scalar.copy(out=pair[:].rearrange("p j k u w -> p (j k) u w"), in_=words)
+            copy = nc.vector.tensor_copy if engine == "vector" else nc.scalar.copy
+            copy(out=pair[:].rearrange("p j k u w -> p (j k) u w"), in_=words)
 
         def warm_up(bank):
             unread = psum.tile([P, 2 * P], F32, name=f"bank{bank}")
             nc.tensor.matmul(unread[:], lhsT=ident, rhs=zeros[:], start=True, stop=True)
 
-        def turn_group(g, first, warm_after=None, warm_bank=None):
-            x_grouped[g] = work.tile([P, PACK, NK, P, 2], F32, name="wide", align_bytes=64)
-            for j in range(PACK):
+        def turn_group(g, first, rows=range(PACK), warm_after=None, warm_bank=None):
+            for j in rows:
                 words = far_t[g, j].bitcast(F32)
-                bank = psum.tile([P, NK, 2, P], F32, name=f"bank{first + j}")
+                bank = turned[g, j] = psum.tile([P, NK, 2, P], F32, name=f"bank{first + j}")
                 for k in range(NK):
                     for u in range(2):
                         if (g, j) in sorted_words:
@@ -174,22 +169,29 @@ def tile_echo_nlms_gradient_s11_kernel(
                         nc.tensor.transpose(bank[:, k, u, :], block, ident)
                     if (j, k) == warm_after:
                         warm_up(warm_bank)
-                nc.scalar.copy(out=x_grouped[g][:, j, :, :, :], in_=bank[:].rearrange("p k u n -> p k n u"))
 
-        def far_quantise(g, rows=slice(0, PACK)):
+        def turn_copy(g, rows=range(PACK)):
+            for j in rows:
+                if j % 2 == 0:
+                    x_grouped[g, j // 2] = keep.tile([P, 2, NK, P, 2], F32, name=f"x_pair{g % 2}_{j // 2}", align_bytes=256)
+                nc.scalar.copy(out=x_grouped[g, j // 2][:, j % 2, :, :, :], in_=turned[g, j][:].rearrange("p k u n -> p k n u"))
+
+        def far_quantise(g, pair):
+            rows = slice(2 * pair, 2 * pair + 2)
             quantise(
                 x_codes[g][:, rows, :, :].rearrange("p j k n -> p (j k n)"),
                 x_scales[g][:, rows, :, :].rearrange("p j k n -> p (j k n)"),
-                x_grouped[g][:, rows, :, :, :].rearrange("p j k n u -> p (j k n u)").bitcast(BF16),
+                x_grouped[g, pair][:].rearrange("p j k n u -> p (j k n u)").bitcast(BF16),
             )
 
         u_grouped, comp_bank = {}, {}
 
-        def comp_mm(g, first):
-            u_grouped[g] = keep.tile([P, R, PACK], BF16, name=f"slab{g + 1}", align_bytes=64)
+        def comp_mm(g, first, rows=range(PACK)):
             for chunk in range(PACK):
-                bank = comp_bank[g, chunk] = psum.tile([P, PACK, P], F32, name=f"bank{first + chunk}")
-                for j in range(PACK):
+                if (g, chunk) not in comp_bank:
+                    comp_bank[g, chunk] = psum.tile([P, PACK, P], F32, name=f"bank{first + chunk}")
+                bank = comp_bank[g, chunk]
+                for j in rows:
                     for k in range(NK):
                         nc.tensor.matmul_mx(
                             out=bank[:, j, :],
@@ -201,31 +203,28 @@ def tile_echo_nlms_gradient_s11_kernel(
                             stop=(k == NK - 1),
                         )
 
-        def comp_copy(g):
-            for chunk in range(PACK):
+        def comp_copy(g, chunks=range(PACK)):
+            if g not in u_grouped:
+                u_grouped[g] = keep.tile([P, R, PACK], BF16, name=f"u_grouped{g}", align_bytes=256)
+            for chunk in chunks:
                 bank = comp_bank[g, chunk]
                 nc.scalar.copy(
                     out=u_grouped[g][:].rearrange("p (m q) j -> p m q j", m=PACK)[:, :, 32 * chunk : 32 * (chunk + 1), :],
                     in_=bank[:].rearrange("p j (q m) -> p m q j", m=PACK),
                 )
 
-        def comp_group(g, first):
-            comp_mm(g, first)
-            comp_copy(g)
-
         def comp_quantise(g):
             quantise(u_codes[:, g, :], u_scales[:, g, :], u_grouped[g][:].rearrange("p r j -> p (r j)"))
 
         mic_scaled, e_rows, e_grouped, echo_bank = {}, {}, {}, {}
 
-        def mic_scale(engine, r, rows):
+        def mic_scale(engine, r, rows=range(PACK)):
             g, h = UNITS[r]
-            names = MIC_BUFFERS[r]
             for j in rows:
-                if len(names) == PACK:
-                    mic_scaled[r, j] = keep.tile([P, PASS], F32, name=names[j], align_bytes=256)[:]
+                if g < 2:
+                    mic_scaled[r, j] = keep.tile([P, PASS], F32, name=f"rows{g}_{j}", align_bytes=256)[:]
                 elif j % 2 == 0:
-                    pair = keep.tile([P, 2, PASS], F32, name=names[j // 2], align_bytes=256)
+                    pair = keep.tile([P, 2, PASS], F32, name=f"rows{g}_{j}", align_bytes=256)
                     mic_scaled[r, j], mic_scaled[r, j + 1] = pair[:, 0, :], pair[:, 1, :]
                 scale_rows(engine, mic_scaled[r, j], mic_t[g, h][:, j, :], negstep[:, g, j : j + 1])
 
@@ -259,7 +258,8 @@ def tile_echo_nlms_gradient_s11_kernel(
 
         def err_interleave(engine, r, lo=0, hi=PASS):
             if r not in e_grouped:
-                e_grouped[r] = keep.tile([P, PASS, PACK], BF16, name="slab2" if r < len(UNITS) - 1 else "slab1", align_bytes=64)
+                name = E_BUFFERS[r]
+                e_grouped[r] = keep.tile([P, PASS, PACK], BF16, name=name, align_bytes=256)
             interleave(engine, e_grouped[r][:, lo:hi, :], e_rows[r][:, :, lo:hi])
 
         def err_quantise(r, cols=slice(0, PASS)):
@@ -282,10 +282,11 @@ def tile_echo_nlms_gradient_s11_kernel(
                 )
 
         def grad_out(engine, h, m, lo=0, hi=PASS):
-            if h not in result:
-                result[h] = work.tile([P, PACK, PASS], F32, name="wide", align_bytes=64)
-            scale_rows(engine, result[h][:, m, lo:hi], grad_bank[h, m, lo][:], gains[:, m : m + 1])
-            nc.sync.dma_start(out=out_v[m][:, h * PASS + lo : h * PASS + hi], in_=result[h][:, m, lo:hi])
+            if (h, m // 2) not in result:
+                result[h, m // 2] = keep.tile([P, 2, PASS], F32, name=f"mic{2 * h + m // 2}_0", align_bytes=256)
+            rows = result[h, m // 2][:, m % 2, lo:hi]
+            scale_rows(engine, rows, grad_bank[h, m, lo][:], gains[:, m : m + 1])
+            nc.sync.dma_start(out=out_v[m][:, h * PASS + lo : h * PASS + hi], in_=rows)
 
         nc.vector.memset(bscale.rearrange("p g n -> p (g n)").bitcast(I32), 0)
         nc.vector.memset(zeros[:], 0.0)
@@ -323,108 +324,113 @@ def tile_echo_nlms_gradient_s11_kernel(
         def rest_of_interleave(r):
             err_interleave("scalar", r, POOL_COLS[r], PASS)
 
-        def mic_unit(engine, r):
-            mic_scale(engine, r, range(PACK))
-
         nc.scalar.activation(out=negstep[:], in_=step_bf[:], func=COPY, scale=-1.0)
         path_widen("vector", 0, range(3))
         path_widen("scalar", 0, [3])
         for bank in range(HIGH, HIGH + 3):
             warm_up(bank)
-        turn_group(0, LOW, (2, 0), HIGH + 3)
+        turn_group(0, LOW, range(PACK), (2, 0), HIGH + 3)
+        turn_copy(0)
         path_interleave("vector", 0, 0)
         path_interleave("vector", 0, 1)
-        far_quantise(0, slice(0, 2))
+        far_quantise(0, 0)
         path_quantise(0, 0)
-        far_quantise(0, slice(2, 4))
+        far_quantise(0, 1)
         path_quantise(0, 1)
-        turn_group(1, HIGH, (1, 0), LOW)
-        far_quantise(1, slice(0, 2))
+        turn_group(1, HIGH, range(PACK), (1, 0), LOW)
+        turn_copy(1)
+        far_quantise(1, 0)
         path_widen("vector", 1, [0], half(0))
-        far_quantise(1, slice(2, 4))
+        far_quantise(1, 1)
         path_widen("scalar", 1, [0], half(1))
-        comp_group(0, LOW)
+        comp_mm(0, LOW)
+        comp_copy(0)
         path_widen("vector", 1, range(1, PACK), half(0))
         path_widen("vector", 1, range(1, PACK), half(1))
         turn_group(2, HIGH)
+        turn_copy(2)
         path_interleave("vector", 1, 0)
-        far_quantise(2, slice(0, 2))
+        mic_scale("vector", 0)
         path_quantise(1, 0)
-        mic_scale("vector", 0, range(PACK))
-        far_quantise(2, slice(2, 4))
-        comp_group(1, LOW)
-        comp_quantise(0)
+        far_quantise(2, 0)
+        far_quantise(2, 1)
+        comp_mm(1, LOW)
+        comp_copy(1)
 
         echo_mm(0, HIGH)
-        far_sort(3, 0)
-        mic_scale("scalar", 1, range(2))
+        far_sort("scalar", 3, 0)
+        mic_scale("scalar", 1, FRONT)
         turn_group(3, LOW)
-        mic_scale("scalar", 1, range(2, PACK))
+        turn_copy(3)
         error_round(0)
         echo_mm(1, HIGH)
+        echo_mm(2, LOW)
+        mic_scale("vector", 1, BACK)
         path_interleave("vector", 1, 1, POOL_PATH, PASS)
-        mic_unit("vector", 2)
-        path_quantise(1, 1)
-        comp_quantise(1)
-        rest_of_interleave(0)
-        mic_unit("scalar", 3)
-        comp_mm(2, LOW)
+        comp_quantise(0)
+        mic_scale("scalar", 2)
         error_round(1)
-        comp_copy(2)
-        echo_mm(2, HIGH)
-        err_quantise(0)
-        far_quantise(3)
-        echo_mm(3, LOW)
+        comp_mm(2, HIGH)
+        rest_of_interleave(0)
+        mic_scale("scalar", 3)
+        far_quantise(3, 0)
+        far_quantise(3, 1)
         error_round(2)
+        comp_copy(2)
+        echo_mm(3, LOW)
+        err_quantise(0)
+        path_quantise(1, 1)
+        echo_mm(4, HIGH)
         rest_of_interleave(1)
-        mic_unit("scalar", 4)
-        comp_mm(3, HIGH)
-        err_quantise(1)
+        mic_scale("scalar", 4)
         error_round(3)
+        comp_mm(3, LOW)
         rest_of_interleave(2)
-        comp_copy(3)
-        echo_mm(4, LOW)
+        err_quantise(1)
+        comp_quantise(1)
+        error_round(4)
         echo_mm(5, HIGH)
+        rest_of_interleave(3)
+        mic_scale("scalar", 5, FRONT)
+        comp_copy(3, FRONT)
+        mic_scale("scalar", 5, BACK)
+        comp_copy(3, BACK)
+        echo_mm(6, LOW)
         err_quantise(2)
         comp_quantise(2)
-        error_round(4)
-        rest_of_interleave(3)
-        mic_unit("scalar", 5)
+        error_round(5)
+        mic_scale("scalar", 6)
         nc.scalar.copy(out=gains[:], in_=gain_bf[:])
         err_quantise(3)
         comp_quantise(3)
         for groups in (range(NG - 1), [NG - 1]):
             for m in range(2):
-                grad_mm(0, m, groups, LOW + m)
-        error_round(5)
+                grad_mm(0, m, groups, HIGH + m)
         rest_of_interleave(4)
-        mic_unit("scalar", 6)
-        grad_out("scalar", 0, 0)
-        err_quantise(4)
-        echo_mm(6, HIGH)
         error_round(6)
         rest_of_interleave(5)
-        mic_unit("scalar", 7)
+        mic_scale("scalar", 7)
+        err_quantise(4)
         err_quantise(5)
-        echo_mm(7, HIGH)
+        echo_mm(7, LOW)
+        grad_out("scalar", 0, 0)
         error_round(7)
         rest_of_interleave(6)
-        grad_out("scalar", 0, 1)
         for m in range(2, PACK):
-            grad_mm(0, m, range(NG), LOW + m)
+            grad_mm(0, m, range(NG), HIGH + m)
         err_interleave("scalar", 7, SPLIT, PASS)
-        for m in range(2, PACK):
+        for m in range(1, PACK):
             grad_out("scalar", 0, m)
         err_quantise(6, slice(0, PASS // 2))
         err_interleave("vector", 7, 0, SPLIT)
         err_quantise(6, slice(PASS // 2, PASS))
         err_quantise(7)
         for m in range(PACK - 1):
-            grad_mm(1, m, range(NG - 2), HIGH + m)
+            grad_mm(1, m, range(NG - 2), LOW + m)
         for m in range(PACK - 1):
-            grad_mm(1, m, range(NG - 2, NG), HIGH + m)
+            grad_mm(1, m, range(NG - 2, NG), LOW + m)
             grad_out("vector" if m % 2 == 0 else "scalar", 1, m)
-        grad_mm(1, PACK - 1, range(NG), HIGH + 3, 0, PASS // 2)
+        grad_mm(1, PACK - 1, range(NG), LOW + 3, 0, PASS // 2)
         grad_out("scalar", 1, PACK - 1, 0, PASS // 2)
-        grad_mm(1, PACK - 1, range(NG), LOW, PASS // 2, PASS)
+        grad_mm(1, PACK - 1, range(NG), HIGH, PASS // 2, PASS)
         grad_out("vector", 1, PACK - 1, PASS // 2, PASS)

@@ -24,8 +24,8 @@ NG = T // PASS
 NK = K // PASS
 NH = C // PASS
 UNITS = [(g, h) for h in range(NH) for g in range(NG)]
-POOL_COLS = [384, 384, 384, 384, 384, 384, 288]
-E_BUFFERS = ["p_rows1", "x_pair1_0"] * 3 + ["x_pair1_0", "p_grouped0_0"]
+POOL_COLS = [400, 400, 400, 400, 400, 400, 288]
+E_BUFFERS = ["e_even", "x_pair1_0"] * 3 + ["x_pair1_0", "p_grouped0_0"]
 SPLIT = 320
 POOL_PATH = 384
 MOVING_CODES, MOVING_SCALES, FIXED_CODES, FIXED_SCALES = 0, 128, 64, 192
@@ -134,14 +134,13 @@ def tile_echo_nlms_gradient_s11_kernel(
             for t in planes:
                 scale_rows(engine, p_rows[k][:, t, cols], pbytes[k, t][:, cols].bitcast(FP8), pscale[:, k, t : t + 1])
 
-        def path_interleave(engine, k, h, lo=0, hi=PASS):
-            if (k, h) not in p_grouped:
-                name = "x_pair0_0" if (k, h) == (1, 1) else f"p_grouped{k}_{h}"
-                p_grouped[k, h] = keep.tile([P, PASS, PACK], BF16, name=name, align_bytes=256)
-            interleave(engine, p_grouped[k, h][:, lo:hi, :], p_rows[k][:, :, h * PASS + lo : h * PASS + hi])
+        def path_interleave(engine, k, h, name, lo=0, hi=PASS):
+            p_grouped[k, h, lo] = keep.tile([P, hi - lo, PACK], BF16, name=name, align_bytes=256)
+            interleave(engine, p_grouped[k, h, lo][:], p_rows[k][:, :, h * PASS + lo : h * PASS + hi])
 
-        def path_quantise(k, h):
-            quantise(p_codes[:, k, half(h)], p_scales[:, k, half(h)], p_grouped[k, h][:].rearrange("p c t -> p (c t)"))
+        def path_quantise(k, h, lo=0, hi=PASS):
+            cols = slice(h * PASS + lo, h * PASS + hi)
+            quantise(p_codes[:, k, cols], p_scales[:, k, cols], p_grouped[k, h, lo][:].rearrange("p c t -> p (c t)"))
 
         x_grouped, sorted_words, turned = {}, {}, {}
 
@@ -308,15 +307,15 @@ def tile_echo_nlms_gradient_s11_kernel(
         load_far(2, 2, 4)
         load_mic(*UNITS[0])
         load_far(3, 0, 2)
-        load_mic(*UNITS[1])
         load_far(3, 2, 4)
+        load_mic(*UNITS[1])
         for g, h in UNITS[2:]:
             load_mic(g, h)
         nc.sync.dma_start(out=gain_bf[:], in_=gain.rearrange("(q m) -> q m", m=PACK))
 
         def error_round(r):
             if r == 0:
-                path_interleave("gpsimd", 1, 1, 0, POOL_PATH)
+                path_interleave("gpsimd", 1, 1, "mic0_0", 0, POOL_PATH)
             else:
                 err_interleave("gpsimd", r - 1, 0, POOL_COLS[r - 1])
             err(r)
@@ -331,34 +330,36 @@ def tile_echo_nlms_gradient_s11_kernel(
             warm_up(bank)
         turn_group(0, LOW, range(PACK), (2, 0), HIGH + 3)
         turn_copy(0)
-        path_interleave("vector", 0, 0)
-        path_interleave("vector", 0, 1)
+        path_interleave("vector", 0, 0, "p_grouped0_0")
+        path_interleave("vector", 0, 1, "p_grouped0_1")
         far_quantise(0, 0)
         path_quantise(0, 0)
         far_quantise(0, 1)
         path_quantise(0, 1)
-        turn_group(1, HIGH, range(PACK), (1, 0), LOW)
+        turn_group(1, HIGH, range(PACK), (1, 1), LOW)
         turn_copy(1)
         far_quantise(1, 0)
         path_widen("vector", 1, [0], half(0))
-        far_quantise(1, 1)
+        path_widen("vector", 1, [1])
+        path_widen("vector", 1, BACK)
         path_widen("scalar", 1, [0], half(1))
         comp_mm(0, LOW)
         comp_copy(0)
-        path_widen("vector", 1, range(1, PACK), half(0))
-        path_widen("vector", 1, range(1, PACK), half(1))
+        far_quantise(1, 1)
         turn_group(2, HIGH)
         turn_copy(2)
-        path_interleave("vector", 1, 0)
-        mic_scale("vector", 0)
+        path_interleave("vector", 1, 0, "p_grouped0_0")
+        path_interleave("vector", 1, 1, "e_even", POOL_PATH, PASS)
         path_quantise(1, 0)
         far_quantise(2, 0)
         far_quantise(2, 1)
+        mic_scale("vector", 0)
+        far_sort("vector", 3, 0)
         comp_mm(1, LOW)
         comp_copy(1)
 
         echo_mm(0, HIGH)
-        far_sort("scalar", 3, 0)
+        far_sort("scalar", 3, 2)
         mic_scale("scalar", 1, FRONT)
         turn_group(3, LOW)
         turn_copy(3)
@@ -366,7 +367,7 @@ def tile_echo_nlms_gradient_s11_kernel(
         echo_mm(1, HIGH)
         echo_mm(2, LOW)
         mic_scale("vector", 1, BACK)
-        path_interleave("vector", 1, 1, POOL_PATH, PASS)
+        path_quantise(1, 1, POOL_PATH, PASS)
         comp_quantise(0)
         mic_scale("scalar", 2)
         error_round(1)
@@ -379,7 +380,7 @@ def tile_echo_nlms_gradient_s11_kernel(
         comp_copy(2)
         echo_mm(3, LOW)
         err_quantise(0)
-        path_quantise(1, 1)
+        path_quantise(1, 1, 0, POOL_PATH)
         echo_mm(4, HIGH)
         rest_of_interleave(1)
         mic_scale("scalar", 4)
@@ -416,10 +417,11 @@ def tile_echo_nlms_gradient_s11_kernel(
         grad_out("scalar", 0, 0)
         error_round(7)
         rest_of_interleave(6)
+        grad_out("scalar", 0, 1)
         for m in range(2, PACK):
             grad_mm(0, m, range(NG), HIGH + m)
         err_interleave("scalar", 7, SPLIT, PASS)
-        for m in range(1, PACK):
+        for m in range(2, PACK):
             grad_out("scalar", 0, m)
         err_quantise(6, slice(0, PASS // 2))
         err_interleave("vector", 7, 0, SPLIT)

from contextlib import ExitStack

import concourse.mybir as mybir
from concourse.masks import make_identity

T, K, R, C = 2048, 1024, 512, 1024
FLOPS = 2 * T * K * C + 2 * T * K * R + 2 * T * R * C

F32 = mybir.dt.float32
BF16 = mybir.dt.bfloat16
I32 = mybir.dt.int32
U32 = mybir.dt.uint32
U8 = mybir.dt.uint8
FP8 = mybir.dt.float8_e4m3fn
FP8X4 = mybir.dt.float8_e4m3fn_x4
FP4X4 = mybir.dt.float4_e2m1fn_x4
ALU = mybir.AluOpType
COPY = mybir.ActivationFunctionType.Copy

P = 128
PACK = 4
PASS = P * PACK
NG = T // PASS
NK = K // PASS
NH = C // PASS
UNITS = [(g, h) for h in range(NH) for g in range(NG)]
POOL_COLS = [400, 400, 400, 400, 400, 400, 288]
E_BUFFERS = ["e_even", "x_pair1_0"] * 3 + ["x_pair1_0", "p_grouped0_0"]
SPLIT = 320
POOL_PATH = 384
MOVING_CODES, MOVING_SCALES, FIXED_CODES, FIXED_SCALES = 0, 128, 64, 192
IDENTITY = 64
ROW_PAD = 32
LOW, HIGH = 0, PACK
FRONT, BACK = range(2), range(2, PACK)


def tile_echo_nlms_gradient_s11_kernel(
    tc, far, mic, path_bytes, path_scale, basis_words, basis_scales, step, gain, out
):
    nc = tc.nc
    with ExitStack() as ctx:
        keep = ctx.enter_context(tc.tile_pool(name="keep", bufs=1))
        work = ctx.enter_context(tc.tile_pool(name="work", bufs=3))
        psum = ctx.enter_context(tc.psum_pool(name="psum", bufs=1))
        ctx.enter_context(tc.manual_schedule())

        def operand(name, shape, dtype, size, shift):
            skip, count = shift // size, shape[0] * shape[1]
            flat = keep.tile([P, skip + count], dtype, name=name, align_bytes=256)
            return flat[:, skip:].rearrange("p (a b) -> p a b", a=shape[0])

        ident = operand("ident", [1, P], F32, 4, IDENTITY)[:, 0, :]
        zeros = keep.tile([P, 2 * P], F32, name="zeros")
        pscale = keep.tile([P, NK, PACK], F32, name="pscale")
        step_bf = keep.tile([P, NG, PACK], BF16, name="step_bf")
        negstep = keep.tile([P, NG, PACK], F32, name="negstep")
        gain_bf = keep.tile([P, PACK], BF16, name="gain_bf")
        gains = keep.tile([P, PACK], F32, name="gains")
        bscale = operand("bscale", [NK, R], U8, 1, MOVING_SCALES)
        bwords = operand("bwords", [NK, 2 * R], U8, 1, MOVING_CODES)
        far_v = far.rearrange("(g p j) k -> g p j k", p=P, j=PACK)
        mic_v = mic.rearrange("(g p j) c -> g p j c", p=P, j=PACK)
        path_v = path_bytes.rearrange("(g p t) c -> g p t c", p=P, t=PACK)
        out_v = out.rearrange("(q m) c -> m q c", m=PACK)

        far_t, far_pair, mic_t, pbytes = {}, {}, {}, {}

        def load_far(g, lo, hi):
            rows = keep.tile([P, hi - lo, K], BF16, name=f"rows{g}_{lo}", align_bytes=256)
            nc.sync.dma_start(out=rows[:], in_=far_v[g][:, lo:hi, :])
            far_pair[g, lo] = rows[:]
            for j in range(lo, hi):
                far_t[g, j] = rows[:, j - lo, :]

        def load_mic(g, h):
            mic_t[g, h] = keep.tile([P, PACK, PASS], BF16, name=f"mic{g}_{h}", align_bytes=256)
            nc.sync.dma_start(out=mic_t[g, h][:], in_=mic_v[g][:, :, half(h)])

        def load_path(k, lo, hi):
            planes = keep.tile([P, hi - lo, C], U8, name=f"pbytes{k}_{lo}", align_bytes=64)
            nc.sync.dma_start(out=planes[:], in_=path_v[k][:, lo:hi, :])
            for t in range(lo, hi):
                pbytes[k, t] = planes[:, t - lo, :]

        def load_basis_scales(q):
            nc.sync.dma_start(
                out=bscale[32 * q : 32 * q + 4, :, :].bitcast(I32),
                in_=basis_scales[:, 4 * q : 4 * q + 4, :].bitcast(I32).rearrange("g q n -> q g n"),
            )

        x_codes, x_scales = [], []
        for g in range(NG):
            codes = operand(f"x_codes{g}", [PACK, NK * P], U32, 4, FIXED_CODES)
            x_codes.append(codes.rearrange("p j (k n) -> p j k n", k=NK))
        for g in range(NG):
            scales = operand(f"x_scales{g}", [PACK, NK * P], U8, 1, FIXED_SCALES)
            x_scales.append(scales.rearrange("p j (k n) -> p j k n", k=NK))
        p_codes = operand("p_codes", [NK, C], U32, 4, MOVING_CODES)
        p_scales = operand("p_scales", [NK, C], U8, 1, MOVING_SCALES)
        u_codes = operand("u_codes", [NG, R], U32, 4, FIXED_CODES)
        u_scales = operand("u_scales", [NG, R], U8, 1, FIXED_SCALES)
        e_codes = operand("e_codes", [len(UNITS), PASS], U32, 4, MOVING_CODES)
        e_scales = operand("e_scales", [len(UNITS), PASS], U8, 1, MOVING_SCALES)

        def half(h):
            return slice(h * PASS, (h + 1) * PASS)

        def interleave(engine, grouped, rows):
            dst = grouped.rearrange("p (c i) t -> p c t i", i=4)
            src = rows.rearrange("p t (c i) -> p c t i", i=4)
            if engine == "vector":
                nc.vector.tensor_copy(out=dst, in_=src)
            elif engine == "gpsimd":
                by_column = rows.rearrange("p t c -> p c t")
                nc.gpsimd.tensor_scalar(out=grouped, in0=by_column, scalar1=1.0, scalar2=0.0, op0=ALU.mult, op1=ALU.add)
            else:
                nc.scalar.copy(out=dst, in_=src)

        def quantise(codes, scales, values):
            nc.vector.quantize_mx(out=codes.bitcast(FP8X4), scales=scales, in_=values)

        def scale_rows(engine, dst, src, scale):
            if engine == "vector":
                nc.vector.tensor_scalar(out=dst, in0=src, scalar1=scale, scalar2=None, op0=ALU.mult)
            else:
                nc.scalar.activation(out=dst, in_=src, func=COPY, scale=scale)

        p_rows, p_grouped = {}, {}

        def path_widen(engine, k, planes, cols=slice(0, C)):
            if k not in p_rows:
                p_rows[k] = keep.tile([P, PACK, C + ROW_PAD], BF16, name=f"p_rows{k}", align_bytes=256)
            for t in planes:
                scale_rows(engine, p_rows[k][:, t, cols], pbytes[k, t][:, cols].bitcast(FP8), pscale[:, k, t : t + 1])

        def path_interleave(engine, k, h, name, lo=0, hi=PASS):
            p_grouped[k, h, lo] = keep.tile([P, hi - lo, PACK], BF16, name=name, align_bytes=256)
            interleave(engine, p_grouped[k, h, lo][:], p_rows[k][:, :, h * PASS + lo : h * PASS + hi])

        def path_quantise(k, h, lo=0, hi=PASS):
            cols = slice(h * PASS + lo, h * PASS + hi)
            quantise(p_codes[:, k, cols], p_scales[:, k, cols], p_grouped[k, h, lo][:].rearrange("p c t -> p (c t)"))

        x_grouped, sorted_words, turned = {}, {}, {}

        def far_sort(engine, g, lo):
            pair = keep.tile([P, 2, NK, 2, P], F32, name=f"sorted{lo}", align_bytes=256)
            sorted_words[g, lo], sorted_words[g, lo + 1] = pair[:, 0, :, :, :], pair[:, 1, :, :, :]
            words = far_pair[g, lo].bitcast(F32).rearrange("p j (k w u) -> p (j k) u w", k=NK, u=2)
            copy = nc.vector.tensor_copy if engine == "vector" else nc.scalar.copy
            copy(out=pair[:].rearrange("p j k u w -> p (j k) u w"), in_=words)

        def warm_up(bank):
            unread = psum.tile([P, 2 * P], F32, name=f"bank{bank}")
            nc.tensor.matmul(unread[:], lhsT=ident, rhs=zeros[:], start=True, stop=True)

        def turn_group(g, first, rows=range(PACK), warm_after=None, warm_bank=None):
            for j in rows:
                words = far_t[g, j].bitcast(F32)
                bank = turned[g, j] = psum.tile([P, NK, 2, P], F32, name=f"bank{first + j}")
                for k in range(NK):
                    for u in range(2):
                        if (g, j) in sorted_words:
                            block = sorted_words[g, j][:, k, u, :]
                        else:
                            block = words[:, 256 * k + u : 256 * (k + 1) : 2]
                        nc.tensor.transpose(bank[:, k, u, :], block, ident)
                    if (j, k) == warm_after:
                        warm_up(warm_bank)

        def turn_copy(g, rows=range(PACK)):
            for j in rows:
                if j % 2 == 0:
                    x_grouped[g, j // 2] = keep.tile([P, 2, NK, P, 2], F32, name=f"x_pair{g % 2}_{j // 2}", align_bytes=256)
                nc.scalar.copy(out=x_grouped[g, j // 2][:, j % 2, :, :, :], in_=turned[g, j][:].rearrange("p k u n -> p k n u"))

        def far_quantise(g, pair):
            rows = slice(2 * pair, 2 * pair + 2)
            quantise(
                x_codes[g][:, rows, :, :].rearrange("p j k n -> p (j k n)"),
                x_scales[g][:, rows, :, :].rearrange("p j k n -> p (j k n)"),
                x_grouped[g, pair][:].rearrange("p j k n u -> p (j k n u)").bitcast(BF16),
            )

        u_grouped, comp_bank = {}, {}

        def comp_mm(g, first, rows=range(PACK)):
            for chunk in range(PACK):
                if (g, chunk) not in comp_bank:
                    comp_bank[g, chunk] = psum.tile([P, PACK, P], F32, name=f"bank{first + chunk}")
                bank = comp_bank[g, chunk]
                for j in rows:
                    for k in range(NK):
                        nc.tensor.matmul_mx(
                            out=bank[:, j, :],
                            lhsT=x_codes[g][:, j, k, :].bitcast(FP8X4),
                            lhsT_scale=x_scales[g][:, j, k, :],
                            rhs=bwords[:, k, 2 * chunk * P : 2 * (chunk + 1) * P].bitcast(FP4X4),
                            rhs_scale=bscale[:, k, chunk * P : (chunk + 1) * P],
                            start=(k == 0),
                            stop=(k == NK - 1),
                        )

        def comp_copy(g, chunks=range(PACK)):
            if g not in u_grouped:
                u_grouped[g] = keep.tile([P, R, PACK], BF16, name=f"u_grouped{g}", align_bytes=256)
            for chunk in chunks:
                bank = comp_bank[g, chunk]
                nc.scalar.copy(
                    out=u_grouped[g][:].rearrange("p (m q) j -> p m q j", m=PACK)[:, :, 32 * chunk : 32 * (chunk + 1), :],
                    in_=bank[:].rearrange("p j (q m) -> p m q j", m=PACK),
                )

        def comp_quantise(g):
            quantise(u_codes[:, g, :], u_scales[:, g, :], u_grouped[g][:].rearrange("p r j -> p (r j)"))

        mic_scaled, e_rows, e_grouped, echo_bank = {}, {}, {}, {}

        def mic_scale(engine, r, rows=range(PACK)):
            g, h = UNITS[r]
            for j in rows:
                if g < 2:
                    mic_scaled[r, j] = keep.tile([P, PASS], F32, name=f"rows{g}_{j}", align_bytes=256)[:]
                elif j % 2 == 0:
                    pair = keep.tile([P, 2, PASS], F32, name=f"rows{g}_{j}", align_bytes=256)
                    mic_scaled[r, j], mic_scaled[r, j + 1] = pair[:, 0, :], pair[:, 1, :]
                scale_rows(engine, mic_scaled[r, j], mic_t[g, h][:, j, :], negstep[:, g, j : j + 1])

        def echo_mm(r, first):
            g, h = UNITS[r]
            for j in range(PACK):
                echo_bank[r, j] = psum.tile([P, PASS], F32, name=f"bank{first + j}")
                for k in range(NK):
                    nc.tensor.matmul_mx(
                        out=echo_bank[r, j][:],
                        lhsT=x_codes[g][:, j, k, :].bitcast(FP8X4),
                        lhsT_scale=x_scales[g][:, j, k, :],
                        rhs=p_codes[:, k, half(h)].bitcast(FP8X4),
                        rhs_scale=p_scales[:, k, half(h)],
                        start=(k == 0),
                        stop=(k == NK - 1),
                    )

        def err(r):
            g, h = UNITS[r]
            e_rows[r] = work.tile([P, PACK, PASS + ROW_PAD], BF16, name="e_rows", align_bytes=256)
            for j in range(PACK):
                nc.vector.scalar_tensor_tensor(
                    out=e_rows[r][:, j, :PASS],
                    in0=echo_bank[r, j][:],
                    scalar=negstep[:, g, j : j + 1],
                    in1=mic_scaled[r, j],
                    op0=ALU.mult,
                    op1=ALU.subtract,
                )

        def err_interleave(engine, r, lo=0, hi=PASS):
            if r not in e_grouped:
                name = E_BUFFERS[r]
                e_grouped[r] = keep.tile([P, PASS, PACK], BF16, name=name, align_bytes=256)
            interleave(engine, e_grouped[r][:, lo:hi, :], e_rows[r][:, :, lo:hi])

        def err_quantise(r, cols=slice(0, PASS)):
            quantise(e_codes[:, r, cols], e_scales[:, r, cols], e_grouped[r][:, cols, :].rearrange("p c j -> p (c j)"))

        grad_bank, result = {}, {}

        def grad_mm(h, m, groups, bank, lo=0, hi=PASS):
            if (h, m, lo) not in grad_bank:
                grad_bank[h, m, lo] = psum.tile([P, hi - lo], F32, name=f"bank{bank}")
            for g in groups:
                nc.tensor.matmul_mx(
                    out=grad_bank[h, m, lo][:],
                    lhsT=u_codes[:, g, m * P : (m + 1) * P].bitcast(FP8X4),
                    lhsT_scale=u_scales[:, g, m * P : (m + 1) * P],
                    rhs=e_codes[:, NG * h + g, lo:hi].bitcast(FP8X4),
                    rhs_scale=e_scales[:, NG * h + g, lo:hi],
                    start=(g == 0),
                    stop=(g == NG - 1),
                )

        def grad_out(engine, h, m, lo=0, hi=PASS):
            if (h, m // 2) not in result:
                result[h, m // 2] = keep.tile([P, 2, PASS], F32, name=f"mic{2 * h + m // 2}_0", align_bytes=256)
            rows = result[h, m // 2][:, m % 2, lo:hi]
            scale_rows(engine, rows, grad_bank[h, m, lo][:], gains[:, m : m + 1])
            nc.sync.dma_start(out=out_v[m][:, h * PASS + lo : h * PASS + hi], in_=rows)

        nc.vector.memset(bscale.rearrange("p g n -> p (g n)").bitcast(I32), 0)
        nc.vector.memset(zeros[:], 0.0)
        make_identity(nc, ident)
        nc.scalar.dma_start(out=pscale[:], in_=path_scale.rearrange("(g p t) o -> p g (t o)", p=P, t=PACK))
        nc.scalar.dma_start(out=step_bf[:], in_=step.rearrange("(g p j) -> p g j", p=P, j=PACK))
        load_path(0, 0, 2)
        load_path(0, 2, 4)
        for j in range(PACK):
            load_far(0, j, j + 1)
        for q in range(4):
            load_basis_scales(q)
        for j in range(PACK):
            load_far(1, j, j + 1)
        nc.sync.dma_start(out=bwords, in_=basis_words.rearrange("g p n -> p g n"))
        load_path(1, 0, 2)
        load_path(1, 2, 4)
        load_far(2, 0, 2)
        load_far(2, 2, 4)
        load_mic(*UNITS[0])
        load_far(3, 0, 2)
        load_far(3, 2, 4)
        load_mic(*UNITS[1])
        for g, h in UNITS[2:]:
            load_mic(g, h)
        nc.sync.dma_start(out=gain_bf[:], in_=gain.rearrange("(q m) -> q m", m=PACK))

        def error_round(r):
            if r == 0:
                path_interleave("gpsimd", 1, 1, "mic0_0", 0, POOL_PATH)
            else:
                err_interleave("gpsimd", r - 1, 0, POOL_COLS[r - 1])
            err(r)

        def rest_of_interleave(r):
            err_interleave("scalar", r, POOL_COLS[r], PASS)

        nc.scalar.activation(out=negstep[:], in_=step_bf[:], func=COPY, scale=-1.0)
        path_widen("vector", 0, range(3))
        path_widen("scalar", 0, [3])
        for bank in range(HIGH, HIGH + 3):
            warm_up(bank)
        turn_group(0, LOW, range(PACK), (2, 0), HIGH + 3)
        turn_copy(0)
        path_interleave("vector", 0, 0, "p_grouped0_0")
        path_interleave("vector", 0, 1, "p_grouped0_1")
        far_quantise(0, 0)
        path_quantise(0, 0)
        far_quantise(0, 1)
        path_quantise(0, 1)
        turn_group(1, HIGH, range(PACK), (1, 1), LOW)
        turn_copy(1)
        far_quantise(1, 0)
        path_widen("vector", 1, [0], half(0))
        path_widen("vector", 1, [1])
        path_widen("vector", 1, BACK)
        path_widen("scalar", 1, [0], half(1))
        comp_mm(0, LOW)
        comp_copy(0)
        far_quantise(1, 1)
        turn_group(2, HIGH)
        turn_copy(2)
        path_interleave("vector", 1, 0, "p_grouped0_0")
        path_interleave("vector", 1, 1, "e_even", POOL_PATH, PASS)
        path_quantise(1, 0)
        far_quantise(2, 0)
        far_quantise(2, 1)
        mic_scale("vector", 0)
        far_sort("vector", 3, 0)
        comp_mm(1, LOW)
        comp_copy(1)

        echo_mm(0, HIGH)
        far_sort("scalar", 3, 2)
        mic_scale("scalar", 1, FRONT)
        turn_group(3, LOW)
        turn_copy(3)
        error_round(0)
        echo_mm(1, HIGH)
        echo_mm(2, LOW)
        mic_scale("vector", 1, BACK)
        path_quantise(1, 1, POOL_PATH, PASS)
        comp_quantise(0)
        mic_scale("scalar", 2)
        error_round(1)
        comp_mm(2, HIGH)
        rest_of_interleave(0)
        mic_scale("scalar", 3)
        far_quantise(3, 0)
        far_quantise(3, 1)
        error_round(2)
        comp_copy(2)
        echo_mm(3, LOW)
        err_quantise(0)
        path_quantise(1, 1, 0, POOL_PATH)
        echo_mm(4, HIGH)
        rest_of_interleave(1)
        mic_scale("scalar", 4)
        error_round(3)
        comp_mm(3, LOW)
        rest_of_interleave(2)
        err_quantise(1)
        comp_quantise(1)
        error_round(4)
        echo_mm(5, HIGH)
        rest_of_interleave(3)
        mic_scale("scalar", 5, FRONT)
        comp_copy(3, FRONT)
        mic_scale("scalar", 5, BACK)
        comp_copy(3, BACK)
        echo_mm(6, LOW)
        err_quantise(2)
        comp_quantise(2)
        error_round(5)
        mic_scale("scalar", 6)
        nc.scalar.copy(out=gains[:], in_=gain_bf[:])
        err_quantise(3)
        comp_quantise(3)
        for groups in (range(NG - 1), [NG - 1]):
            for m in range(2):
                grad_mm(0, m, groups, HIGH + m)
        rest_of_interleave(4)
        error_round(6)
        rest_of_interleave(5)
        mic_scale("scalar", 7)
        err_quantise(4)
        err_quantise(5)
        echo_mm(7, LOW)
        grad_out("scalar", 0, 0)
        error_round(7)
        rest_of_interleave(6)
        grad_out("scalar", 0, 1)
        for m in range(2, PACK):
            grad_mm(0, m, range(NG), HIGH + m)
        err_interleave("scalar", 7, SPLIT, PASS)
        for m in range(2, PACK):
            grad_out("scalar", 0, m)
        err_quantise(6, slice(0, PASS // 2))
        err_interleave("vector", 7, 0, SPLIT)
        err_quantise(6, slice(PASS // 2, PASS))
        err_quantise(7)
        for m in range(PACK - 1):
            grad_mm(1, m, range(NG - 2), LOW + m)
        for m in range(PACK - 1):
            grad_mm(1, m, range(NG - 2, NG), LOW + m)
            grad_out("vector" if m % 2 == 0 else "scalar", 1, m)
        grad_mm(1, PACK - 1, range(NG), LOW + 3, 0, PASS // 2)
        grad_out("scalar", 1, PACK - 1, 0, PASS // 2)
        grad_mm(1, PACK - 1, range(NG), HIGH, PASS // 2, PASS)
        grad_out("vector", 1, PACK - 1, PASS // 2, PASS)
